import numpy as np
import ml_dtypes


def mxq(x, axis, fmt="e4m3"):
    dtype, down = {"e4m3": (ml_dtypes.float8_e4m3fn, 7), "e5m2": (ml_dtypes.float8_e5m2, 14)}[fmt]
    v = np.moveaxis(np.asarray(x, np.float32).astype(ml_dtypes.bfloat16).astype(np.float64), axis, -1)
    blocks = v.reshape(v.shape[:-1] + (-1, 32))
    amax = np.abs(blocks).max(-1, keepdims=True)
    byte = np.maximum(np.where(amax > 0, np.frexp(amax)[1] - 1 + 127, 0) - down, 1)
    scale = np.exp2(byte - 127.0)
    codes = (blocks / scale).astype(np.float32).astype(dtype).astype(np.float64)
    return np.moveaxis((codes * scale).reshape(v.shape), -1, axis)


WIDE = False


def mx_kscale(k):
    if not WIDE:
        return np.ones(k)
    levels = np.array([10, -10, 5, -5, 0])
    if k % 512:
        return np.exp2(np.random.permutation(np.resize(levels, k // 32))).repeat(32)
    a = np.empty((k // 512, 16))
    for p in range(k // 512):
        a[p, :8] = np.random.permutation(np.resize(levels, 8))
        for g in range(8):
            far = levels[np.abs(levels - a[p, g]) >= 10]
            a[p, g + 8] = far[np.random.randint(len(far))]
    return np.exp2(a.ravel()).repeat(32)


def f64(x):
    return np.asarray(x).astype(np.float64)


def striped(idx):
    return np.tile(idx.reshape(-1, 16).T, (8, 1)).astype(np.uint16)


def unstriped(offs):
    return offs[:16].T.reshape(-1).astype(np.int64)


E2M1 = np.array([0.0, 0.5, 1.0, 1.5, 2.0, 3.0, 4.0, 6.0, -0.0, -0.5, -1.0, -1.5, -2.0, -3.0, -4.0, -6.0])


def pack_weight(w, fmt):
    k, n = w.shape
    w = f64(np.asarray(w, np.float32).astype(ml_dtypes.bfloat16)).reshape(k // 32, 32, n)
    amax = np.abs(w).max(1)
    if fmt == "e4m3":
        byte = np.frexp(amax)[1] - 1 + 127 - 7
    else:
        mant, ex = np.frexp(amax / 6.0)
        byte = np.where(mant > 0.5, ex, ex - 1) + 127
    byte = np.clip(np.where(amax > 0, byte, 1), 1, 254)
    scaled = (w * np.exp2(127.0 - byte)[:, None, :]).reshape(k, n).astype(np.float32)
    by_word = np.ascontiguousarray(scaled.reshape(k // 512, 128, 4, n).transpose(0, 1, 3, 2))
    if fmt == "e4m3":
        words = by_word.astype(ml_dtypes.float8_e4m3fn).view(np.uint8)
    else:
        c = by_word.astype(ml_dtypes.float4_e2m1fn).view(np.uint8) & 0xF
        words = (c[..., 0::2] | (c[..., 1::2] << 4)).reshape(k // 512, 128, 2 * n)
    return np.ascontiguousarray(words), np.ascontiguousarray(byte.astype(np.uint8).reshape(k // 512, 16, n))


def unpack_weight(words, scales, fmt):
    g, _, n = scales.shape
    words = np.ascontiguousarray(words).reshape(g, 128, n, -1)
    if fmt == "e4m3":
        vals = words.view(ml_dtypes.float8_e4m3fn).astype(np.float64)
    else:
        nib = np.empty((g, 128, n, 4), np.uint8)
        nib[..., 0::2] = words & 0xF
        nib[..., 1::2] = words >> 4
        vals = E2M1[nib]
    vals = vals * np.repeat(np.exp2(scales.astype(np.float64) - 127.0), 8, axis=1)[..., None]
    return vals.transpose(0, 1, 3, 2).reshape(g * 512, n)


def gelu(v):
    return 0.5 * v * (1.0 + np.tanh(np.sqrt(2.0 / np.pi) * (v + 0.044715 * v**3)))


def striped8(idx):
    return np.concatenate([v.reshape(-1, 16).T for v in idx]).astype(np.uint16)


def unstriped8(offs):
    return np.stack([offs[16 * g:16 * g + 16].T.reshape(-1) for g in range(8)]).astype(np.int64)


def put_heads(h, wgs, idx8, t2):
    r = np.arange(h.shape[0])
    page = np.zeros((h.shape[0], t2))
    page[r[:, None], idx8[r % 512 // 64]] = wgs[r // 4 % 128] * h
    return page


K, T, S, H, N, T2 = 1536, 2048, 512, 1024, 512, 1024

def setup_inputs():
    n = np.random.standard_normal
    s = mx_kscale(K)[:, None]
    u = mx_kscale(H)[:, None]
    tab_words, tab_scales = pack_weight(n((K, T)) * s, "e4m3")
    w4_words, w4_scales = pack_weight(n((K, H)) / np.sqrt(K) / s, "e2m1")
    wgs = np.repeat(np.random.uniform(0.5, 2.0, (8, S)), 16, axis=0)
    return {
        "tab_words": tab_words, "tab_scales": tab_scales,
        "offs": striped(np.random.permutation(T)[:S]),
        "w4_words": w4_words, "w4_scales": w4_scales,
        "w1": (n((K, H)) / np.sqrt(K) / s * u.T).astype(np.float32),
        "dec": (np.exp(0.3 * n(H)) * u[:, 0]).astype(np.float32),
        "wgs": wgs.astype(np.float32),
        "offs2": striped8(np.stack([np.random.permutation(T2)[:S] for _ in range(8)])),
        "queue": (n((H, T2)) * u).astype(np.float32),
        "wf": (n((H, N)) / np.sqrt(H) / u).astype(np.float32),
        "bf": (0.5 * n(N)).astype(np.float32),
    }

def reference(tab_words, tab_scales, offs, w4_words, w4_scales, w1, dec, wgs, offs2, queue, wf, bf):
    v = unpack_weight(tab_words, tab_scales, "e4m3")[:, unstriped(offs)]
    w4 = unpack_weight(w4_words, w4_scales, "e2m1")
    enc = np.tanh(w4.T @ v)
    orig = mxq(f64(w1), 0, "e4m3").T @ v
    h = orig - f64(dec)[:, None] * enc
    page = put_heads(h, f64(wgs), unstriped8(offs2), T2)
    z = page + f64(queue)
    y = mxq(f64(wf), 0, "e4m3").T @ mxq(z, 0, "e4m3")
    return y + f64(bf)[:, None]

@@ -1,0 +1,288 @@
+from contextlib import ExitStack
+
+import concourse.mybir as mybir
+from concourse.masks import make_identity
+
+K, T, S, H, N, T2 = 1536, 2048, 512, 1024, 512, 1024
+FLOPS = 2 * (2 * K * H * S + H * N * T2)
+
+F32 = mybir.dt.float32
+BF16 = mybir.dt.bfloat16
+I32 = mybir.dt.int32
+U32 = mybir.dt.uint32
+U16 = mybir.dt.uint16
+U8 = mybir.dt.uint8
+FP8X4 = mybir.dt.float8_e4m3fn_x4
+FP4X4 = mybir.dt.float4_e2m1fn_x4
+ACT = mybir.ActivationFunctionType
+ALU = mybir.AluOpType
+
+P = 128
+PACK = 4
+KP = P * PACK
+PASSES = K // KP
+BLOCKS = H // KP
+BANK = 512
+
+
+def tile_list_fraud_residual_queue_kernel(
+    tc, tab_words, tab_scales, offs, w4_words, w4_scales, w1, dec, wgs, offs2, queue, wf, bf, out
+):
+    nc = tc.nc
+    with ExitStack() as ctx:
+        held = ctx.enter_context(tc.tile_pool(name="held", bufs=1))
+        big = ctx.enter_context(tc.tile_pool(name="big", bufs=13))
+        ring = ctx.enter_context(tc.tile_pool(name="ring", bufs=2))
+        turned = ctx.enter_context(tc.tile_pool(name="turned", bufs=12))
+        woven = ctx.enter_context(tc.tile_pool(name="woven", bufs=4))
+        psum = ctx.enter_context(tc.psum_pool(name="psum", bufs=1))
+
+        def keep(shape, dtype, name):
+            return held.tile(shape, dtype, name=name, align_bytes=64)
+
+        def bank(number):
+            return psum.tile([P, BANK], F32, name="bank%d" % number)
+
+        def load_big(shape, dtype, source):
+            t = big.tile(shape, dtype, name="big", align_bytes=64)
+            nc.sync.dma_start(out=t[:], in_=source)
+            return t
+
+        def load_table(a):
+            return load_big([P, T], I32, tab_words[a].rearrange("p t i -> p (t i)").bitcast(I32))
+
+        def load_weight(w, a, b):
+            rows = w[a * KP : (a + 1) * KP, b * KP : (b + 1) * KP]
+            return load_big([P, PACK, KP], F32, rows.rearrange("(p j) c -> p j c", j=PACK))
+
+        def load_queue(b, u):
+            rows = queue[b * KP : (b + 1) * KP, :].rearrange("(p i) m -> p i m", i=PACK)
+            return load_big([P, 2, T2], F32, rows[:, 2 * u : 2 * u + 2, :])
+
+        tab_planes = keep([P, PASSES * T], U8, "tab_planes")
+        nc.gpsimd.memset(tab_planes[:].bitcast(I32), 0)
+        w4_planes_raw = keep([P, PASSES * H], U8, "w4_planes_raw")
+        nc.vector.memset(w4_planes_raw[:].bitcast(I32), 0)
+        v_planes = [keep([P, S], U8, "v_plane%d" % a) for a in range(PASSES)]
+        pages = [keep([P, T2], F32, "page%d" % i) for i in range(PACK)]
+        for i, page in enumerate(pages):
+            (nc.vector if i < 2 else nc.gpsimd).memset(page[:], 0.0)
+
+        picks = held.tile([P, S // 16], U16, name="picks")
+        nc.sync.dma_start(picks[:], offs)
+        places = held.tile([P, S // 16], U16, name="places")
+        nc.sync.dma_start(places[:], offs2)
+        identity = keep([P, P], F32, "identity")
+        make_identity(nc, identity[:])
+        dec_sb = keep([P, BLOCKS, PACK], F32, "dec_sb")
+        nc.scalar.dma_start(out=dec_sb[:], in_=dec.rearrange("(b p i) -> p b i", b=BLOCKS, i=PACK))
+        bias_sb = keep([P, PACK], F32, "bias_sb")
+        nc.scalar.dma_start(out=bias_sb[:], in_=bf.rearrange("(p c) -> p c", c=PACK))
+
+        table = [load_table(0)]
+        w1_raw = {(0, 0): load_weight(w1, 0, 0)}
+        for q in range(4):
+            nc.sync.dma_start(
+                out=tab_planes[32 * q : 32 * q + 4, :].bitcast(I32).rearrange("r (a t) -> r a t", a=PASSES),
+                in_=tab_scales[:, 4 * q : 4 * q + 4, :].bitcast(I32).rearrange("a r t -> r a t"),
+            )
+        w4_raw = keep([P, PASSES, 2 * H], U8, "w4_raw")
+        nc.sync.dma_start(out=w4_raw[:].bitcast(I32), in_=w4_words.rearrange("a p n -> p a n").bitcast(I32))
+        table.append(load_table(1))
+        for q in range(4):
+            nc.sync.dma_start(
+                out=w4_planes_raw[32 * q : 32 * q + 4, :].bitcast(I32).rearrange("r (a c) -> r a c", a=PASSES),
+                in_=w4_scales[:, 4 * q : 4 * q + 4, :].bitcast(I32).rearrange("a r c -> r a c"),
+            )
+        for a in range(PASSES):
+            nc.vector.tensor_copy(v_planes[a][:], tab_planes[:, a * T : (a + 1) * T].indirect(picks[:]))
+        w1_raw[1, 0] = load_weight(w1, 1, 0)
+        table.append(load_table(2))
+        w1_raw[2, 0] = load_weight(w1, 2, 0)
+        wgs_sb = keep([P, S], F32, "wgs_sb")
+        nc.sync.dma_start(out=wgs_sb[:], in_=wgs)
+        for a in range(PASSES):
+            w1_raw[a, 1] = load_weight(w1, a, 1)
+        queue_sb = {(0, u): load_queue(0, u) for u in range(2)}
+        wf_raw = [load_weight(wf, b, 0) for b in range(BLOCKS)]
+        for u in range(2):
+            queue_sb[1, u] = load_queue(1, u)
+
+        v_words = [keep([P, S], U32, "v_words%d" % a) for a in range(PASSES)]
+
+        def gather(a):
+            nc.vector.tensor_copy(v_words[a][:], table[a][:].bitcast(U32).indirect(picks[:]))
+
+        def quantised(name):
+            return keep([P, KP], U32, name + "_codes"), keep([P, KP], U8, name + "_plane")
+
+        def cast(copy, raw, t0, t1, tile):
+            src = raw[:].rearrange("p j (m t) -> p m t j", t=PACK)[:, :, t0:t1, :]
+            copy(tile[:].rearrange("p (t m j) -> p m t j", m=P, j=PACK), src)
+            return tile
+
+        def quantise(operand, c0, tile):
+            c1 = c0 + tile.shape[1] // PACK
+            nc.vector.quantize_mx(out=operand[0][:, c0:c1].bitcast(FP8X4), scales=operand[1][:, c0:c1], in_=tile[:])
+
+        def staged(slot, width=PACK * KP, dtype=BF16):
+            return held.tile([P, width], dtype, name="staged%d" % slot, align_bytes=64)
+
+        w1_q = {(a, b): quantised("w1_%d_%d" % (a, b)) for b in range(BLOCKS) for a in range(PASSES)}
+        wf_q = [quantised("wf_%d" % b) for b in range(BLOCKS)]
+        z_q = {(b, half): quantised("z_%d_%d" % (b, half)) for b in range(BLOCKS) for half in range(2)}
+
+        gather(0)
+        w4_codes = [keep([P, PASSES * 2 * KP], U8, "w4_codes%d" % b) for b in range(BLOCKS)]
+        w4_planes = [keep([P, PASSES * KP], U8, "w4_planes%d" % b) for b in range(BLOCKS)]
+
+        def order_w4(b):
+            nc.vector.tensor_copy(
+                w4_planes[b][:].rearrange("p (a t m) -> p t a m", t=PACK, m=P),
+                w4_planes_raw[:].rearrange("p (a b m t) -> p b t a m", b=BLOCKS, t=PACK, m=P)[:, b],
+            )
+            nc.vector.tensor_copy(
+                w4_codes[b][:].bitcast(U16).rearrange("p (a t m) -> p t a m", t=PACK, m=P),
+                w4_raw[:].bitcast(U16).rearrange("p a (b m t) -> p b t a m", b=BLOCKS, t=PACK)[:, b],
+            )
+
+        quantise(w1_q[0, 0], 0, cast(nc.scalar.copy, w1_raw[0, 0], 0, PACK, staged(0)))
+        order_w4(0)
+        gather(1)
+        quantise(w1_q[1, 0], 0, cast(nc.scalar.copy, w1_raw[1, 0], 0, PACK, staged(1)))
+        gather(2)
+
+        def encode(k, number, minus_enc=None):
+            b, i = divmod(k, PACK)
+            acc = bank(number)
+            for a in range(PASSES):
+                c0 = a * KP + i * P
+                nc.tensor.matmul_mx(
+                    out=acc[:],
+                    lhsT=w4_codes[b][:, 2 * c0 : 2 * (c0 + P)].bitcast(FP4X4),
+                    lhsT_scale=w4_planes[b][:, c0 : c0 + P],
+                    rhs=v_words[a][:].bitcast(FP8X4),
+                    rhs_scale=v_planes[a][:],
+                    start=(a == 0),
+                    stop=(a == PASSES - 1),
+                )
+            if minus_enc is None:
+                minus_enc = ring.tile([P, S], F32, name="minus_enc")
+            nc.scalar.activation(minus_enc[:], acc[:], ACT.Tanh, scale=-1.0)
+            return minus_enc
+
+        def place(k, number, minus_enc, h):
+            b, i = divmod(k, PACK)
+            acc = bank(number)
+            for a in range(PASSES):
+                codes, plane = w1_q[a, b]
+                nc.tensor.matmul_mx(
+                    out=acc[:],
+                    lhsT=codes[:, i * P : (i + 1) * P].bitcast(FP8X4),
+                    lhsT_scale=plane[:, i * P : (i + 1) * P],
+                    rhs=v_words[a][:].bitcast(FP8X4),
+                    rhs_scale=v_planes[a][:],
+                    start=(a == 0),
+                    stop=(a == PASSES - 1),
+                )
+            nc.vector.scalar_tensor_tensor(h[:], minus_enc[:], dec_sb[:, b, i : i + 1], acc[:], ALU.mult, ALU.add)
+            nc.vector.tensor_tensor(pages[i][:].indirect(places[:]), h[:], wgs_sb[:], ALU.mult)
+
+        def fresh_h():
+            return ring.tile([P, S], F32, name="h")
+
+        def add_turned(b, u, numbers, copies):
+            accs = [bank(n) for n in numbers]
+            for step in range(3):
+                for q, acc in enumerate(accs):
+                    for mb in range(2):
+                        cols = slice((2 * q + mb) * P, (2 * q + mb + 1) * P)
+                        for e in ((0, 1), (0,), (1,))[step]:
+                            source = queue_sb[b, u][:, e, cols] if step == 0 else pages[2 * u + e][:, cols]
+                            nc.tensor.matmul(
+                                acc[:, (2 * mb + e) * P : (2 * mb + e + 1) * P],
+                                lhsT=source,
+                                rhs=identity[:],
+                                is_transpose=True,
+                                start=(step == 0 and mb == 0 and e == 0),
+                                stop=(step == 2 and mb == 1),
+                            )
+            pairs = []
+            for q, acc in enumerate(accs):
+                pair = turned.tile([P, BANK], BF16, name="pair", align_bytes=64)
+                copies[q](
+                    pair[:].rearrange("m (g p e) -> m g p e", g=2, e=2),
+                    acc[:].rearrange("m (g e p) -> m g p e", g=2, e=2),
+                )
+                pairs.append(pair)
+            return pairs
+
+        def turn_back(b, q, pairs, number, copy):
+            acc = bank(number)
+            for u in range(2):
+                words = pairs[u][q][:].bitcast(F32)
+                for mb in range(2):
+                    nc.tensor.transpose(
+                        acc[:, (2 * u + mb) * P : (2 * u + mb + 1) * P], words[:, mb * P : (mb + 1) * P], identity[:]
+                    )
+            z = woven.tile([P, 2 * BANK], BF16, name="z", align_bytes=64)
+            copy(z[:].bitcast(F32).rearrange("p (m u) -> p m u", u=2), acc[:].rearrange("p (u m) -> p m u", u=2))
+            quantise(z_q[b, q // 2], (q % 2) * 256, z)
+
+        on_scalar = [nc.scalar.copy] * 4
+        in_turn = [nc.scalar.copy, nc.vector.tensor_copy] * 2
+
+        enc = {0: encode(0, 0, staged(2, S, F32)), 1: encode(1, 2)}
+        quantise(w1_q[2, 0], 0, cast(nc.vector.tensor_copy, w1_raw[2, 0], 0, 2, staged(0, 2 * KP)))
+        quantise(w1_q[2, 0], 256, cast(nc.scalar.copy, w1_raw[2, 0], 2, 4, staged(1, 2 * KP)))
+        h0 = fresh_h()
+        place(0, 1, enc[0], h0)
+        order_w4(1)
+        quantise(w1_q[0, 1], 0, cast(nc.scalar.copy, w1_raw[0, 1], 0, PACK, staged(2)))
+        enc[2] = encode(2, 3)
+        place(1, 5, enc[1], fresh_h())
+        quantise(w1_q[1, 1], 0, cast(nc.scalar.copy, w1_raw[1, 1], 0, PACK, staged(0)))
+        quantise(w1_q[2, 1], 0, cast(nc.scalar.copy, w1_raw[2, 1], 0, PACK, staged(1)))
+        enc[3] = encode(3, 4)
+        place(2, 6, enc[2], fresh_h())
+        pairs0 = [add_turned(0, 0, (1, 2, 3, 4), on_scalar)]
+        enc[4] = encode(4, 0)
+        place(3, 7, enc[3], staged(1, S, F32))
+        enc[5] = encode(5, 0)
+        place(4, 1, enc[4], fresh_h())
+        pairs0.append(add_turned(0, 1, (5, 2, 3, 4), on_scalar))
+        for b in range(BLOCKS):
+            quantise(wf_q[b], 0, cast(nc.scalar.copy, wf_raw[b], 0, PACK, staged(b)))
+        enc[6] = encode(6, 0)
+        place(5, 1, enc[5], fresh_h())
+        for q in range(4):
+            turn_back(0, q, pairs0, 6 + q % 2, nc.scalar.copy)
+        enc[7] = encode(7, 0)
+        place(6, 1, enc[6], fresh_h())
+        pairs1 = [add_turned(1, 0, (5, 2, 3, 4), on_scalar)]
+        place(7, 1, enc[7], fresh_h())
+        pairs1.append(add_turned(1, 1, (5, 2, 3, 4), in_turn))
+
+        out_rows = out.rearrange("(p c) m -> p c m", c=PACK)
+        score_banks = ((0, 1, 5, 2), (3, 4, 0, 1))
+        for half in range(2):
+            for q in (2 * half, 2 * half + 1):
+                turn_back(1, q, pairs1, 6 + q % 2, in_turn[q])
+            scores = big.tile([P, PACK, BANK], F32, name="big", align_bytes=64)
+            for c in range(PACK):
+                acc = bank(score_banks[half][c])
+                for b in range(BLOCKS):
+                    nc.tensor.matmul_mx(
+                        out=acc[:],
+                        lhsT=wf_q[b][0][:, c * P : (c + 1) * P].bitcast(FP8X4),
+                        lhsT_scale=wf_q[b][1][:, c * P : (c + 1) * P],
+                        rhs=z_q[b, half][0][:].bitcast(FP8X4),
+                        rhs_scale=z_q[b, half][1][:],
+                        start=(b == 0),
+                        stop=(b == BLOCKS - 1),
+                    )
+                if c % 2 == 0:
+                    nc.scalar.activation(scores[:, c, :], acc[:], ACT.Identity, bias=bias_sb[:, c : c + 1])
+                else:
+                    nc.vector.tensor_scalar(scores[:, c, :], acc[:], bias_sb[:, c : c + 1], None, ALU.add)
+                nc.sync.dma_start(out=out_rows[:, c, half * BANK : (half + 1) * BANK], in_=scores[:, c, :])

@@ -1,7 +1,6 @@
 from contextlib import ExitStack
 
 import concourse.mybir as mybir
-from concourse.masks import make_identity
 
 K, T, S, H, N, T2 = 1536, 2048, 512, 1024, 512, 1024
 FLOPS = 2 * (2 * K * H * S + H * N * T2)
@@ -23,6 +22,8 @@ KP = P * PACK
 PASSES = K // KP
 BLOCKS = H // KP
 BANK = 512
+SHIFT_ROWS = 112
+QUARTER = T2 // 4
 
 
 def tile_list_fraud_residual_queue_kernel(
@@ -33,7 +34,6 @@ def tile_list_fraud_residual_queue_kernel(
         held = ctx.enter_context(tc.tile_pool(name="held", bufs=1))
         big = ctx.enter_context(tc.tile_pool(name="big", bufs=13))
         ring = ctx.enter_context(tc.tile_pool(name="ring", bufs=2))
-        turned = ctx.enter_context(tc.tile_pool(name="turned", bufs=12))
         woven = ctx.enter_context(tc.tile_pool(name="woven", bufs=4))
         psum = ctx.enter_context(tc.psum_pool(name="psum", bufs=1))
 
@@ -59,54 +59,58 @@ def tile_list_fraud_residual_queue_kernel(
             rows = queue[b * KP : (b + 1) * KP, :].rearrange("(p i) m -> p i m", i=PACK)
             return load_big([P, 2, T2], F32, rows[:, 2 * u : 2 * u + 2, :])
 
-        tab_planes = keep([P, PASSES * T], U8, "tab_planes")
+        tab_planes = keep([P, T], U8, "tab_planes")
         nc.gpsimd.memset(tab_planes[:].bitcast(I32), 0)
         w4_planes_raw = keep([P, PASSES * H], U8, "w4_planes_raw")
         nc.vector.memset(w4_planes_raw[:].bitcast(I32), 0)
         v_planes = [keep([P, S], U8, "v_plane%d" % a) for a in range(PASSES)]
-        pages = [keep([P, T2], F32, "page%d" % i) for i in range(PACK)]
-        for i, page in enumerate(pages):
-            (nc.vector if i < 2 else nc.gpsimd).memset(page[:], 0.0)
+        for a in range(1, PASSES):
+            nc.vector.memset(v_planes[a][:].bitcast(I32), 0)
+        pages = [keep([P, T2], F32, "page%d" % i) for i in range(3)]
+        for page in pages:
+            nc.gpsimd.memset(page[:], 0.0)
 
         picks = held.tile([P, S // 16], U16, name="picks")
         nc.sync.dma_start(picks[:], offs)
-        places = held.tile([P, S // 16], U16, name="places")
-        nc.sync.dma_start(places[:], offs2)
-        identity = keep([P, P], F32, "identity")
-        make_identity(nc, identity[:])
-        dec_sb = keep([P, BLOCKS, PACK], F32, "dec_sb")
-        nc.scalar.dma_start(out=dec_sb[:], in_=dec.rearrange("(b p i) -> p b i", b=BLOCKS, i=PACK))
-        bias_sb = keep([P, PACK], F32, "bias_sb")
-        nc.scalar.dma_start(out=bias_sb[:], in_=bf.rearrange("(p c) -> p c", c=PACK))
 
         table = [load_table(0)]
         w1_raw = {(0, 0): load_weight(w1, 0, 0)}
         for q in range(4):
             nc.sync.dma_start(
-                out=tab_planes[32 * q : 32 * q + 4, :].bitcast(I32).rearrange("r (a t) -> r a t", a=PASSES),
-                in_=tab_scales[:, 4 * q : 4 * q + 4, :].bitcast(I32).rearrange("a r t -> r a t"),
+                out=tab_planes[32 * q : 32 * q + 4 * PASSES, :].bitcast(I32),
+                in_=tab_scales[:, 4 * q : 4 * q + 4, :].bitcast(I32),
             )
         w4_raw = keep([P, PASSES, 2 * H], U8, "w4_raw")
         nc.sync.dma_start(out=w4_raw[:].bitcast(I32), in_=w4_words.rearrange("a p n -> p a n").bitcast(I32))
-        table.append(load_table(1))
+        w1_raw[1, 0] = load_weight(w1, 1, 0)
         for q in range(4):
             nc.sync.dma_start(
                 out=w4_planes_raw[32 * q : 32 * q + 4, :].bitcast(I32).rearrange("r (a c) -> r a c", a=PASSES),
                 in_=w4_scales[:, 4 * q : 4 * q + 4, :].bitcast(I32).rearrange("a r c -> r a c"),
             )
-        for a in range(PASSES):
-            nc.vector.tensor_copy(v_planes[a][:], tab_planes[:, a * T : (a + 1) * T].indirect(picks[:]))
-        w1_raw[1, 0] = load_weight(w1, 1, 0)
+        table.append(load_table(1))
+        nc.vector.tensor_copy(v_planes[0][:], tab_planes[:].indirect(picks[:]))
+        for a in range(1, PASSES):
+            nc.sync.dma_start(
+                out=v_planes[a][0:SHIFT_ROWS, :].bitcast(I32),
+                in_=v_planes[0][4 * a : 4 * a + SHIFT_ROWS, :].bitcast(I32),
+            )
         table.append(load_table(2))
-        w1_raw[2, 0] = load_weight(w1, 2, 0)
         wgs_sb = keep([P, S], F32, "wgs_sb")
         nc.sync.dma_start(out=wgs_sb[:], in_=wgs)
+        w1_raw[2, 0] = load_weight(w1, 2, 0)
+        places = held.tile([P, S // 16], U16, name="places")
+        nc.sync.dma_start(places[:], offs2)
+        dec_sb = keep([P, BLOCKS, PACK], F32, "dec_sb")
+        nc.sync.dma_start(out=dec_sb[:], in_=dec.rearrange("(b p i) -> p b i", b=BLOCKS, i=PACK))
         for a in range(PASSES):
             w1_raw[a, 1] = load_weight(w1, a, 1)
         queue_sb = {(0, u): load_queue(0, u) for u in range(2)}
         wf_raw = [load_weight(wf, b, 0) for b in range(BLOCKS)]
         for u in range(2):
             queue_sb[1, u] = load_queue(1, u)
+        bias_sb = keep([P, PACK], F32, "bias_sb")
+        nc.sync.dma_start(out=bias_sb[:], in_=bf.rearrange("(p c) -> p c", c=PACK))
 
         v_words = [keep([P, S], U32, "v_words%d" % a) for a in range(PASSES)]
 
@@ -117,8 +121,8 @@ def tile_list_fraud_residual_queue_kernel(
             return keep([P, KP], U32, name + "_codes"), keep([P, KP], U8, name + "_plane")
 
         def cast(copy, raw, t0, t1, tile):
-            src = raw[:].rearrange("p j (m t) -> p m t j", t=PACK)[:, :, t0:t1, :]
-            copy(tile[:].rearrange("p (t m j) -> p m t j", m=P, j=PACK), src)
+            src = raw[:].rearrange("p j (m t) -> p m j t", t=PACK)[:, :, :, t0:t1]
+            copy(tile[:].rearrange("p (t m j) -> p m j t", m=P, j=PACK), src)
             return tile
 
         def quantise(operand, c0, tile):
@@ -148,8 +152,8 @@ def tile_list_fraud_residual_queue_kernel(
 
         quantise(w1_q[0, 0], 0, cast(nc.scalar.copy, w1_raw[0, 0], 0, PACK, staged(0)))
         order_w4(0)
-        gather(1)
         quantise(w1_q[1, 0], 0, cast(nc.scalar.copy, w1_raw[1, 0], 0, PACK, staged(1)))
+        gather(1)
         gather(2)
 
         def encode(k, number, minus_enc=None):
@@ -167,7 +171,7 @@ def tile_list_fraud_residual_queue_kernel(
                     stop=(a == PASSES - 1),
                 )
             if minus_enc is None:
-                minus_enc = ring.tile([P, S], F32, name="minus_enc")
+                minus_enc = ring.tile([P, S], F32, name="minus_enc", bufs=3)
             nc.scalar.activation(minus_enc[:], acc[:], ACT.Tanh, scale=-1.0)
             return minus_enc
 
@@ -186,88 +190,70 @@ def tile_list_fraud_residual_queue_kernel(
                     stop=(a == PASSES - 1),
                 )
             nc.vector.scalar_tensor_tensor(h[:], minus_enc[:], dec_sb[:, b, i : i + 1], acc[:], ALU.mult, ALU.add)
-            nc.vector.tensor_tensor(pages[i][:].indirect(places[:]), h[:], wgs_sb[:], ALU.mult)
+            weighted = ring.tile([P, S], F32, name="weighted", bufs=2)
+            nc.gpsimd.tensor_tensor(weighted[:], h[:], wgs_sb[:], ALU.mult)
+            return weighted
+
+        def scatter(k, weighted):
+            nc.vector.tensor_copy(pages[k % 3][:].indirect(places[:]), weighted[:])
 
         def fresh_h():
-            return ring.tile([P, S], F32, name="h")
+            return ring.tile([P, S], F32, name="h", bufs=2)
 
-        def add_turned(b, u, numbers, copies):
-            accs = [bank(n) for n in numbers]
-            for step in range(3):
-                for q, acc in enumerate(accs):
-                    for mb in range(2):
-                        cols = slice((2 * q + mb) * P, (2 * q + mb + 1) * P)
-                        for e in ((0, 1), (0,), (1,))[step]:
-                            source = queue_sb[b, u][:, e, cols] if step == 0 else pages[2 * u + e][:, cols]
-                            nc.tensor.matmul(
-                                acc[:, (2 * mb + e) * P : (2 * mb + e + 1) * P],
-                                lhsT=source,
-                                rhs=identity[:],
-                                is_transpose=True,
-                                start=(step == 0 and mb == 0 and e == 0),
-                                stop=(step == 2 and mb == 1),
-                            )
-            pairs = []
-            for q, acc in enumerate(accs):
-                pair = turned.tile([P, BANK], BF16, name="pair", align_bytes=64)
-                copies[q](
-                    pair[:].rearrange("m (g p e) -> m g p e", g=2, e=2),
-                    acc[:].rearrange("m (g e p) -> m g p e", g=2, e=2),
+        def add_queue(k, rows):
+            b, i = divmod(k, PACK)
+            width = T2 // len(rows)
+            for part, tile in enumerate(rows):
+                cols = slice(part * width, (part + 1) * width)
+                (nc.vector if k == 7 else nc.gpsimd).tensor_tensor(
+                    tile[:, i, :], pages[k % 3][:, cols], queue_sb[b, i // 2][:, i % 2, cols], ALU.add
                 )
-                pairs.append(pair)
-            return pairs
 
-        def turn_back(b, q, pairs, number, copy):
-            acc = bank(number)
-            for u in range(2):
-                words = pairs[u][q][:].bitcast(F32)
-                for mb in range(2):
-                    nc.tensor.transpose(
-                        acc[:, (2 * u + mb) * P : (2 * u + mb + 1) * P], words[:, mb * P : (mb + 1) * P], identity[:]
-                    )
-            z = woven.tile([P, 2 * BANK], BF16, name="z", align_bytes=64)
-            copy(z[:].bitcast(F32).rearrange("p (m u) -> p m u", u=2), acc[:].rearrange("p (u m) -> p m u", u=2))
-            quantise(z_q[b, q // 2], (q % 2) * 256, z)
+        def weave(b, q, rows, copy):
+            width = T2 // len(rows)
+            c0 = q * QUARTER % width
+            z = woven.tile([P, PACK * QUARTER], BF16, name="z", align_bytes=64)
+            copy(
+                z[:].rearrange("p (c e i) -> p c i e", e=4, i=PACK),
+                rows[q * QUARTER // width][:, :, c0 : c0 + QUARTER].rearrange("p i (c e) -> p c i e", e=4),
+            )
+            quantise(z_q[b, q // 2], (q % 2) * QUARTER, z)
 
-        on_scalar = [nc.scalar.copy] * 4
-        in_turn = [nc.scalar.copy, nc.vector.tensor_copy] * 2
+        z_rows = [
+            [keep([P, PACK, T2 // (b + 1)], BF16, "z_rows%d_%d" % (b, part)) for part in range(b + 1)]
+            for b in range(BLOCKS)
+        ]
 
         enc = {0: encode(0, 0, staged(2, S, F32)), 1: encode(1, 2)}
-        quantise(w1_q[2, 0], 0, cast(nc.vector.tensor_copy, w1_raw[2, 0], 0, 2, staged(0, 2 * KP)))
-        quantise(w1_q[2, 0], 256, cast(nc.scalar.copy, w1_raw[2, 0], 2, 4, staged(1, 2 * KP)))
-        h0 = fresh_h()
-        place(0, 1, enc[0], h0)
+        quantise(w1_q[2, 0], 0, cast(nc.vector.tensor_copy, w1_raw[2, 0], 0, 1, staged(0, KP)))
+        quantise(w1_q[2, 0], P, cast(nc.scalar.copy, w1_raw[2, 0], 1, 2, staged(1, KP)))
+        quantise(w1_q[2, 0], 2 * P, cast(nc.scalar.copy, w1_raw[2, 0], 2, 4, staged(3, 2 * KP)))
+        weighted = {0: place(0, 1, enc[0], fresh_h()), 1: place(1, 3, enc[1], fresh_h())}
         order_w4(1)
-        quantise(w1_q[0, 1], 0, cast(nc.scalar.copy, w1_raw[0, 1], 0, PACK, staged(2)))
-        enc[2] = encode(2, 3)
-        place(1, 5, enc[1], fresh_h())
-        quantise(w1_q[1, 1], 0, cast(nc.scalar.copy, w1_raw[1, 1], 0, PACK, staged(0)))
-        quantise(w1_q[2, 1], 0, cast(nc.scalar.copy, w1_raw[2, 1], 0, PACK, staged(1)))
-        enc[3] = encode(3, 4)
-        place(2, 6, enc[2], fresh_h())
-        pairs0 = [add_turned(0, 0, (1, 2, 3, 4), on_scalar)]
-        enc[4] = encode(4, 0)
-        place(3, 7, enc[3], staged(1, S, F32))
-        enc[5] = encode(5, 0)
-        place(4, 1, enc[4], fresh_h())
-        pairs0.append(add_turned(0, 1, (5, 2, 3, 4), on_scalar))
-        for b in range(BLOCKS):
-            quantise(wf_q[b], 0, cast(nc.scalar.copy, wf_raw[b], 0, PACK, staged(b)))
-        enc[6] = encode(6, 0)
-        place(5, 1, enc[5], fresh_h())
-        for q in range(4):
-            turn_back(0, q, pairs0, 6 + q % 2, nc.scalar.copy)
-        enc[7] = encode(7, 0)
-        place(6, 1, enc[6], fresh_h())
-        pairs1 = [add_turned(1, 0, (5, 2, 3, 4), on_scalar)]
-        place(7, 1, enc[7], fresh_h())
-        pairs1.append(add_turned(1, 1, (5, 2, 3, 4), in_turn))
+        scatter(0, weighted[0])
+        enc[2] = encode(2, 1)
+        for k in range(1, 8):
+            if k <= PASSES:
+                quantise(w1_q[k - 1, 1], 0, cast(nc.scalar.copy, w1_raw[k - 1, 1], 0, PACK, staged((2, 0, 1)[k - 1])))
+            if k < 6:
+                enc[k + 2] = encode(k + 2, [0,2,1,0,0,0,0,0][k + 2], None)
+            if k < 7:
+                weighted[k + 1] = place(k + 1, [1,3,3,1,3,1,3,1][k + 1], enc[k + 1], fresh_h())
+            scatter(k, weighted[k])
+            add_queue(k - 1, z_rows[(k - 1) // PACK])
+            if k == 4:
+                for b in range(BLOCKS):
+                    quantise(wf_q[b], 0, cast(nc.scalar.copy, wf_raw[b], 0, PACK, staged(2 - b)))
+                for q in range(4):
+                    weave(0, q, z_rows[0], nc.scalar.copy)
+        add_queue(7, z_rows[1])
 
         out_rows = out.rearrange("(p c) m -> p c m", c=PACK)
-        score_banks = ((0, 1, 5, 2), (3, 4, 0, 1))
+        score_banks = ((0, 2, 4, 5), (6, 7, 1, 3))
         for half in range(2):
-            for q in (2 * half, 2 * half + 1):
-                turn_back(1, q, pairs1, 6 + q % 2, in_turn[q])
+            weave(1, 2 * half, z_rows[1], nc.scalar.copy)
+            weave(1, 2 * half + 1, z_rows[1], nc.vector.tensor_copy)
+        for half in range(2):
             scores = big.tile([P, PACK, BANK], F32, name="big", align_bytes=64)
             for c in range(PACK):
                 acc = bank(score_banks[half][c])

@@ -1,6 +1,7 @@
 from contextlib import ExitStack
 
 import concourse.mybir as mybir
+from concourse.masks import make_identity
 
 K, T, S, H, N, T2 = 1536, 2048, 512, 1024, 512, 1024
 FLOPS = 2 * (2 * K * H * S + H * N * T2)
@@ -32,8 +33,9 @@ def tile_list_fraud_residual_queue_kernel(
     nc = tc.nc
     with ExitStack() as ctx:
         held = ctx.enter_context(tc.tile_pool(name="held", bufs=1))
-        big = ctx.enter_context(tc.tile_pool(name="big", bufs=13))
+        big = ctx.enter_context(tc.tile_pool(name="big", bufs=11))
         ring = ctx.enter_context(tc.tile_pool(name="ring", bufs=2))
+        turned = ctx.enter_context(tc.tile_pool(name="turned", bufs=8))
         woven = ctx.enter_context(tc.tile_pool(name="woven", bufs=4))
         psum = ctx.enter_context(tc.psum_pool(name="psum", bufs=1))
 
@@ -66,10 +68,12 @@ def tile_list_fraud_residual_queue_kernel(
         v_planes = [keep([P, S], U8, "v_plane%d" % a) for a in range(PASSES)]
         for a in range(1, PASSES):
             nc.vector.memset(v_planes[a][:].bitcast(I32), 0)
-        pages = [keep([P, T2], F32, "page%d" % i) for i in range(3)]
+        pages = [keep([P, T2], F32, "page%d" % i) for i in range(6)]
         for page in pages:
             nc.gpsimd.memset(page[:], 0.0)
 
+        identity = keep([P, P], F32, "identity")
+        make_identity(nc, identity[:])
         picks = held.tile([P, S // 16], U16, name="picks")
         nc.sync.dma_start(picks[:], offs)
 
@@ -121,8 +125,11 @@ def tile_list_fraud_residual_queue_kernel(
             return keep([P, KP], U32, name + "_codes"), keep([P, KP], U8, name + "_plane")
 
         def cast(copy, raw, t0, t1, tile):
-            src = raw[:].rearrange("p j (m t) -> p m j t", t=PACK)[:, :, :, t0:t1]
-            copy(tile[:].rearrange("p (t m j) -> p m j t", m=P, j=PACK), src)
+            src = raw[:].rearrange("p j (m t) -> p m j t", t=PACK)
+            dst = tile[:].rearrange("p (t m j) -> p m j t", m=P, j=PACK)
+            for t in range(t0, t1, 2):
+                n = min(2, t1 - t)
+                copy(dst[:, :, :, t - t0 : t - t0 + n], src[:, :, :, t : t + n])
             return tile
 
         def quantise(operand, c0, tile):
@@ -171,7 +178,7 @@ def tile_list_fraud_residual_queue_kernel(
                     stop=(a == PASSES - 1),
                 )
             if minus_enc is None:
-                minus_enc = ring.tile([P, S], F32, name="minus_enc", bufs=3)
+                minus_enc = ring.tile([P, S], F32, name="minus_enc", bufs=7)
             nc.scalar.activation(minus_enc[:], acc[:], ACT.Tanh, scale=-1.0)
             return minus_enc
 
@@ -190,23 +197,59 @@ def tile_list_fraud_residual_queue_kernel(
                     stop=(a == PASSES - 1),
                 )
             nc.vector.scalar_tensor_tensor(h[:], minus_enc[:], dec_sb[:, b, i : i + 1], acc[:], ALU.mult, ALU.add)
-            weighted = ring.tile([P, S], F32, name="weighted", bufs=2)
-            nc.gpsimd.tensor_tensor(weighted[:], h[:], wgs_sb[:], ALU.mult)
-            return weighted
+            return h
 
-        def scatter(k, weighted):
-            nc.vector.tensor_copy(pages[k % 3][:].indirect(places[:]), weighted[:])
+        def scatter(k, h):
+            nc.vector.tensor_tensor(pages[k if k < PACK else PACK + k % 2][:].indirect(places[:]), h[:], wgs_sb[:], ALU.mult)
 
         def fresh_h():
             return ring.tile([P, S], F32, name="h", bufs=2)
+
+        def add_turned(b, u, numbers, copies):
+            accs = [bank(n) for n in numbers]
+            for step in range(3):
+                for q, acc in enumerate(accs):
+                    for mb in range(2):
+                        cols = slice((2 * q + mb) * P, (2 * q + mb + 1) * P)
+                        for e in ((0, 1), (0,), (1,))[step]:
+                            source = queue_sb[b, u][:, e, cols] if step == 0 else pages[2 * u + e][:, cols]
+                            nc.tensor.matmul(
+                                acc[:, (2 * mb + e) * P : (2 * mb + e + 1) * P],
+                                lhsT=source,
+                                rhs=identity[:],
+                                is_transpose=True,
+                                start=(step == 0 and mb == 0 and e == 0),
+                                stop=(step == 2 and mb == 1),
+                            )
+            pairs = []
+            for q, acc in enumerate(accs):
+                pair = turned.tile([P, BANK], BF16, name="pair", align_bytes=64)
+                copies[q](
+                    pair[:].rearrange("m (g p e) -> m g p e", g=2, e=2),
+                    acc[:].rearrange("m (g e p) -> m g p e", g=2, e=2),
+                )
+                pairs.append(pair)
+            return pairs
+
+        def turn_back(b, q, pairs, number, copy):
+            acc = bank(number)
+            for u in range(2):
+                words = pairs[u][q][:].bitcast(F32)
+                for mb in range(2):
+                    nc.tensor.transpose(
+                        acc[:, (2 * u + mb) * P : (2 * u + mb + 1) * P], words[:, mb * P : (mb + 1) * P], identity[:]
+                    )
+            z = woven.tile([P, 2 * BANK], BF16, name="z", align_bytes=64)
+            copy(z[:].bitcast(F32).rearrange("p (m u) -> p m u", u=2), acc[:].rearrange("p (u m) -> p m u", u=2))
+            quantise(z_q[b, q // 2], (q % 2) * 256, z)
 
         def add_queue(k, rows):
             b, i = divmod(k, PACK)
             width = T2 // len(rows)
             for part, tile in enumerate(rows):
                 cols = slice(part * width, (part + 1) * width)
-                (nc.vector if k == 7 else nc.gpsimd).tensor_tensor(
-                    tile[:, i, :], pages[k % 3][:, cols], queue_sb[b, i // 2][:, i % 2, cols], ALU.add
+                nc.vector.tensor_tensor(
+                    tile[:, i, :], pages[k if k < PACK else PACK + k % 2][:, cols], queue_sb[b, i // 2][:, i % 2, cols], ALU.add
                 )
 
         def weave(b, q, rows, copy):
@@ -219,37 +262,38 @@ def tile_list_fraud_residual_queue_kernel(
             )
             quantise(z_q[b, q // 2], (q % 2) * QUARTER, z)
 
-        z_rows = [
-            [keep([P, PACK, T2 // (b + 1)], BF16, "z_rows%d_%d" % (b, part)) for part in range(b + 1)]
-            for b in range(BLOCKS)
-        ]
+        z_rows = [None, [keep([P, PACK, T2 // 2], BF16, "z_rows%d" % part) for part in range(2)]]
 
         enc = {0: encode(0, 0, staged(2, S, F32)), 1: encode(1, 2)}
         quantise(w1_q[2, 0], 0, cast(nc.vector.tensor_copy, w1_raw[2, 0], 0, 1, staged(0, KP)))
         quantise(w1_q[2, 0], P, cast(nc.scalar.copy, w1_raw[2, 0], 1, 2, staged(1, KP)))
         quantise(w1_q[2, 0], 2 * P, cast(nc.scalar.copy, w1_raw[2, 0], 2, 4, staged(3, 2 * KP)))
-        weighted = {0: place(0, 1, enc[0], fresh_h()), 1: place(1, 3, enc[1], fresh_h())}
+        h = {0: place(0, 1, enc[0], fresh_h())}
+        scatter(0, h[0])
         order_w4(1)
-        scatter(0, weighted[0])
-        enc[2] = encode(2, 1)
-        for k in range(1, 8):
-            if k <= PASSES:
-                quantise(w1_q[k - 1, 1], 0, cast(nc.scalar.copy, w1_raw[k - 1, 1], 0, PACK, staged((2, 0, 1)[k - 1])))
-            if k < 6:
-                enc[k + 2] = encode(k + 2, [0,2,1,0,0,0,0,0][k + 2], None)
-            if k < 7:
-                weighted[k + 1] = place(k + 1, [1,3,3,1,3,1,3,1][k + 1], enc[k + 1], fresh_h())
-            scatter(k, weighted[k])
-            add_queue(k - 1, z_rows[(k - 1) // PACK])
-            if k == 4:
-                for b in range(BLOCKS):
-                    quantise(wf_q[b], 0, cast(nc.scalar.copy, wf_raw[b], 0, PACK, staged(2 - b)))
-                for q in range(4):
-                    weave(0, q, z_rows[0], nc.scalar.copy)
+        h[1] = place(1, 3, enc[1], fresh_h())
+        scatter(1, h[1])
+        for k in range(2, 4):
+            enc[k] = encode(k, [0,2,1,1,4,5,6,7][k])
+        for a in range(PASSES):
+            quantise(w1_q[a, 1], 0, cast(nc.scalar.copy, w1_raw[a, 1], 0, PACK, staged((2, 0, 1)[a])))
+        for k in range(4, 8):
+            enc[k] = encode(k, [0,2,1,1,4,5,6,7][k])
+        pairs = []
+        for k in range(2, 8):
+            h[k] = place(k, [1,3,3,3,0,2,1,3][k], enc[k], staged(0, S, F32) if k == 2 else staged(1, S, F32) if k == 3 else fresh_h())
+            if k > 4:
+                add_queue(k - 1, z_rows[1])
+            scatter(k, h[k])
+        pairs = [add_turned(0, u, (4, 5, 6, 7), [nc.scalar.copy] * 4) for u in range(2)]
+        for q in range(4):
+            turn_back(0, q, pairs, 4 + q, nc.scalar.copy)
+        for b in range(BLOCKS):
+            quantise(wf_q[b], 0, cast(nc.scalar.copy, wf_raw[b], 0, PACK, staged(2 + b)))
         add_queue(7, z_rows[1])
 
         out_rows = out.rearrange("(p c) m -> p c m", c=PACK)
-        score_banks = ((0, 2, 4, 5), (6, 7, 1, 3))
+        score_banks = ((4, 5, 6, 7), (0, 2, 1, 3))
         for half in range(2):
             weave(1, 2 * half, z_rows[1], nc.scalar.copy)
             weave(1, 2 * half + 1, z_rows[1], nc.vector.tensor_copy)

@@ -22,9 +22,15 @@ PACK = 4
 KP = P * PACK
 PASSES = K // KP
 BLOCKS = H // KP
+TILES = BLOCKS * PACK
 BANK = 512
-SHIFT_ROWS = 112
 QUARTER = T2 // 4
+PLANE_ROWS = 100
+PACKED_FROM = 32 - 4 * PASSES
+ENCODE_BANK = (2, 0, 0, 0, 0, 0, 0, 0)
+LINEAR_BANK = (0, 1, 2, 1, 2, 1, 2, 1)
+SLOT = 8192
+OVER_AT = {"wf0": 2 * T, "queue00": 2 * T + 2 * SLOT, "wf1": 2 * T + SLOT}
 
 
 def tile_list_fraud_residual_queue_kernel(
@@ -33,10 +39,8 @@ def tile_list_fraud_residual_queue_kernel(
     nc = tc.nc
     with ExitStack() as ctx:
         held = ctx.enter_context(tc.tile_pool(name="held", bufs=1))
-        big = ctx.enter_context(tc.tile_pool(name="big", bufs=11))
+        over = ctx.enter_context(tc.tile_pool(name="over", bufs=1))
         ring = ctx.enter_context(tc.tile_pool(name="ring", bufs=2))
-        turned = ctx.enter_context(tc.tile_pool(name="turned", bufs=8))
-        woven = ctx.enter_context(tc.tile_pool(name="woven", bufs=4))
         psum = ctx.enter_context(tc.psum_pool(name="psum", bufs=1))
 
         def keep(shape, dtype, name):
@@ -45,81 +49,104 @@ def tile_list_fraud_residual_queue_kernel(
         def bank(number):
             return psum.tile([P, BANK], F32, name="bank%d" % number)
 
-        def load_big(shape, dtype, source):
-            t = big.tile(shape, dtype, name="big", align_bytes=64)
+        def slot(number, shape, dtype):
+            return keep(shape, dtype, "slot%d" % number)
+
+        def load_big(number, shape, dtype, source):
+            if number in OVER_AT:
+                t = over.tile(shape, dtype, name=number, offset=OVER_AT[number], align_bytes=64)
+            else:
+                t = slot(number, shape, dtype)
             nc.sync.dma_start(out=t[:], in_=source)
             return t
 
-        def load_table(a):
-            return load_big([P, T], I32, tab_words[a].rearrange("p t i -> p (t i)").bitcast(I32))
+        def load_table(number, a):
+            return load_big(number, [P, T], I32, tab_words[a].rearrange("p t i -> p (t i)").bitcast(I32))
 
-        def load_weight(w, a, b):
+        def load_weight(number, w, a, b):
             rows = w[a * KP : (a + 1) * KP, b * KP : (b + 1) * KP]
-            return load_big([P, PACK, KP], F32, rows.rearrange("(p j) c -> p j c", j=PACK))
+            return load_big(number, [P, PACK, KP], F32, rows.rearrange("(p j) c -> p j c", j=PACK))
 
-        def load_queue(b, u):
+        def load_w4(b):
+            t = keep([P, PASSES, 2 * KP], U8, "w4_raw%d" % b)
+            words = w4_words[:, :, b * 2 * KP : (b + 1) * 2 * KP].rearrange("a p n -> p a n")
+            nc.sync.dma_start(out=t[:].bitcast(I32), in_=words.bitcast(I32))
+            return t
+
+        def load_queue(number, b, u):
             rows = queue[b * KP : (b + 1) * KP, :].rearrange("(p i) m -> p i m", i=PACK)
-            return load_big([P, 2, T2], F32, rows[:, 2 * u : 2 * u + 2, :])
+            return load_big(number, [P, 2, T2], F32, rows[:, 2 * u : 2 * u + 2, :])
 
-        tab_planes = keep([P, T], U8, "tab_planes")
-        nc.gpsimd.memset(tab_planes[:].bitcast(I32), 0)
         w4_planes_raw = keep([P, PASSES * H], U8, "w4_planes_raw")
-        nc.vector.memset(w4_planes_raw[:].bitcast(I32), 0)
+        nc.gpsimd.memset(w4_planes_raw[:].bitcast(I32), 0)
+        tab_planes = over.tile([P, T], U8, name="tab_planes", offset=T // 2, align_bytes=64)
+        for q in range(4):
+            nc.vector.memset(tab_planes[32 * q : 32 * q + PACKED_FROM, :].bitcast(I32), 0)
         v_planes = [keep([P, S], U8, "v_plane%d" % a) for a in range(PASSES)]
-        for a in range(1, PASSES):
-            nc.vector.memset(v_planes[a][:].bitcast(I32), 0)
-        pages = [keep([P, T2], F32, "page%d" % i) for i in range(6)]
+        for plane in v_planes:
+            nc.vector.memset(plane[:].bitcast(I32), 0)
+        pages = [keep([P, T2], F32, "page%d" % i) for i in range(PACK)]
         for page in pages:
             nc.gpsimd.memset(page[:], 0.0)
-
         identity = keep([P, P], F32, "identity")
         make_identity(nc, identity[:])
+
+        table = [load_table(0, 0)]
         picks = held.tile([P, S // 16], U16, name="picks")
         nc.sync.dma_start(picks[:], offs)
-
-        table = [load_table(0)]
-        w1_raw = {(0, 0): load_weight(w1, 0, 0)}
+        w4_raw = [load_w4(0)]
         for q in range(4):
             nc.sync.dma_start(
-                out=tab_planes[32 * q : 32 * q + 4 * PASSES, :].bitcast(I32),
+                out=tab_planes[32 * q + PACKED_FROM : 32 * (q + 1), :].bitcast(I32),
                 in_=tab_scales[:, 4 * q : 4 * q + 4, :].bitcast(I32),
             )
-        w4_raw = keep([P, PASSES, 2 * H], U8, "w4_raw")
-        nc.sync.dma_start(out=w4_raw[:].bitcast(I32), in_=w4_words.rearrange("a p n -> p a n").bitcast(I32))
-        w1_raw[1, 0] = load_weight(w1, 1, 0)
+        w1_raw = {(0, 0): load_weight(1, w1, 0, 0)}
+        table.append(load_table(2, 1))
         for q in range(4):
             nc.sync.dma_start(
                 out=w4_planes_raw[32 * q : 32 * q + 4, :].bitcast(I32).rearrange("r (a c) -> r a c", a=PASSES),
                 in_=w4_scales[:, 4 * q : 4 * q + 4, :].bitcast(I32).rearrange("a r c -> r a c"),
             )
-        table.append(load_table(1))
-        nc.vector.tensor_copy(v_planes[0][:], tab_planes[:].indirect(picks[:]))
-        for a in range(1, PASSES):
+        table.append(load_table(3, 2))
+        picked_planes = keep([P, S], U8, "picked_planes")
+        nc.vector.tensor_copy(picked_planes[:], tab_planes[:].indirect(picks[:]))
+
+        def move_plane(a):
+            first = PACKED_FROM + 4 * a
             nc.sync.dma_start(
-                out=v_planes[a][0:SHIFT_ROWS, :].bitcast(I32),
-                in_=v_planes[0][4 * a : 4 * a + SHIFT_ROWS, :].bitcast(I32),
+                out=v_planes[a][0:PLANE_ROWS, :].bitcast(I32),
+                in_=picked_planes[first : first + PLANE_ROWS, :].bitcast(I32),
             )
-        table.append(load_table(2))
-        wgs_sb = keep([P, S], F32, "wgs_sb")
-        nc.sync.dma_start(out=wgs_sb[:], in_=wgs)
-        w1_raw[2, 0] = load_weight(w1, 2, 0)
-        places = held.tile([P, S // 16], U16, name="places")
-        nc.sync.dma_start(places[:], offs2)
+
+        move_plane(0)
+        move_plane(1)
+        w1_raw[1, 0] = load_weight(4, w1, 1, 0)
+        move_plane(2)
+        w1_raw[2, 0] = load_weight(5, w1, 2, 0)
         dec_sb = keep([P, BLOCKS, PACK], F32, "dec_sb")
         nc.sync.dma_start(out=dec_sb[:], in_=dec.rearrange("(b p i) -> p b i", b=BLOCKS, i=PACK))
+        places = held.tile([P, S // 16], U16, name="places")
+        nc.sync.dma_start(places[:], offs2)
+        wgs_sb = keep([P, S], F32, "wgs_sb")
+        nc.sync.dma_start(out=wgs_sb[:], in_=wgs)
+        w4_raw.append(load_w4(1))
         for a in range(PASSES):
-            w1_raw[a, 1] = load_weight(w1, a, 1)
-        queue_sb = {(0, u): load_queue(0, u) for u in range(2)}
-        wf_raw = [load_weight(wf, b, 0) for b in range(BLOCKS)]
-        for u in range(2):
-            queue_sb[1, u] = load_queue(1, u)
+            w1_raw[a, 1] = load_weight((6, 7, 4)[a], w1, a, 1)
+        queue_sb = {(0, 0): load_queue("queue00", 0, 0), (0, 1): load_queue(0, 0, 1)}
+        wf_raw = [load_weight("wf%d" % b, wf, b, 0) for b in range(BLOCKS)]
+        for number, b, u in ((1, 1, 0), (5, 1, 1)):
+            queue_sb[b, u] = load_queue(number, b, u)
         bias_sb = keep([P, PACK], F32, "bias_sb")
         nc.sync.dma_start(out=bias_sb[:], in_=bf.rearrange("(p c) -> p c", c=PACK))
 
-        v_words = [keep([P, S], U32, "v_words%d" % a) for a in range(PASSES)]
+        def after_planes(place, name):
+            return over.tile([P, S], U32, name=name, offset=T * place, align_bytes=64)
 
-        def gather(a):
-            nc.vector.tensor_copy(v_words[a][:], table[a][:].bitcast(U32).indirect(picks[:]))
+        v_words = {}
+
+        def gather(a, tile):
+            v_words[a] = tile
+            nc.vector.tensor_copy(tile[:], table[a][:].bitcast(U32).indirect(picks[:]))
 
         def quantised(name):
             return keep([P, KP], U32, name + "_codes"), keep([P, KP], U8, name + "_plane")
@@ -127,14 +154,12 @@ def tile_list_fraud_residual_queue_kernel(
         def cast(copy, raw, t0, t1, tile):
             src = raw[:].rearrange("p j (m t) -> p m j t", t=PACK)
             dst = tile[:].rearrange("p (t m j) -> p m j t", m=P, j=PACK)
-            for t in range(t0, t1, 2):
-                n = min(2, t1 - t)
-                copy(dst[:, :, :, t - t0 : t - t0 + n], src[:, :, :, t : t + n])
+            copy(dst, src[:, :, :, t0:t1])
             return tile
 
-        def quantise(operand, c0, tile):
-            c1 = c0 + tile.shape[1] // PACK
-            nc.vector.quantize_mx(out=operand[0][:, c0:c1].bitcast(FP8X4), scales=operand[1][:, c0:c1], in_=tile[:])
+        def quantise(operand, c0, ap):
+            c1 = c0 + ap.shape[1] // PACK
+            nc.vector.quantize_mx(out=operand[0][:, c0:c1].bitcast(FP8X4), scales=operand[1][:, c0:c1], in_=ap)
 
         def staged(slot, width=PACK * KP, dtype=BF16):
             return held.tile([P, width], dtype, name="staged%d" % slot, align_bytes=64)
@@ -143,49 +168,50 @@ def tile_list_fraud_residual_queue_kernel(
         wf_q = [quantised("wf_%d" % b) for b in range(BLOCKS)]
         z_q = {(b, half): quantised("z_%d_%d" % (b, half)) for b in range(BLOCKS) for half in range(2)}
 
-        gather(0)
+        gather(0, keep([P, S], U32, "v_words0"))
         w4_codes = [keep([P, PASSES * 2 * KP], U8, "w4_codes%d" % b) for b in range(BLOCKS)]
-        w4_planes = [keep([P, PASSES * KP], U8, "w4_planes%d" % b) for b in range(BLOCKS)]
+        w4_planes = keep([P, BLOCKS * PASSES * KP], U8, "w4_planes")
 
-        def order_w4(b):
-            nc.vector.tensor_copy(
-                w4_planes[b][:].rearrange("p (a t m) -> p t a m", t=PACK, m=P),
-                w4_planes_raw[:].rearrange("p (a b m t) -> p b t a m", b=BLOCKS, t=PACK, m=P)[:, b],
-            )
+        def order_words(b):
             nc.vector.tensor_copy(
                 w4_codes[b][:].bitcast(U16).rearrange("p (a t m) -> p t a m", t=PACK, m=P),
-                w4_raw[:].bitcast(U16).rearrange("p a (b m t) -> p b t a m", b=BLOCKS, t=PACK)[:, b],
+                w4_raw[b][:].bitcast(U16).rearrange("p a (m t) -> p t a m", t=PACK),
             )
 
-        quantise(w1_q[0, 0], 0, cast(nc.scalar.copy, w1_raw[0, 0], 0, PACK, staged(0)))
-        order_w4(0)
-        quantise(w1_q[1, 0], 0, cast(nc.scalar.copy, w1_raw[1, 0], 0, PACK, staged(1)))
-        gather(1)
-        gather(2)
+        order_words(0)
+        gather(1, after_planes(0, "v_words1"))
+        nc.vector.tensor_copy(
+            w4_planes[:].rearrange("p (g t m) -> p g t m", t=PACK, m=P),
+            w4_planes_raw[:].rearrange("p (g m t) -> p g t m", t=PACK, m=P),
+        )
+        w1_q[0, 0] = (after_planes(1, "w1_first_codes"), w1_q[0, 0][1])
+        quantise(w1_q[0, 0], 0, cast(nc.scalar.copy, w1_raw[0, 0], 0, PACK, staged(0))[:])
+        gather(2, slot(2, [P, S], U32))
+        quantise(w1_q[1, 0], 0, cast(nc.vector.tensor_copy, w1_raw[1, 0], 0, PACK, slot(3, [P, PACK * KP], BF16))[:])
 
-        def encode(k, number, minus_enc=None):
+        def encode(k):
             b, i = divmod(k, PACK)
-            acc = bank(number)
+            acc = bank(ENCODE_BANK[k])
             for a in range(PASSES):
                 c0 = a * KP + i * P
                 nc.tensor.matmul_mx(
                     out=acc[:],
                     lhsT=w4_codes[b][:, 2 * c0 : 2 * (c0 + P)].bitcast(FP4X4),
-                    lhsT_scale=w4_planes[b][:, c0 : c0 + P],
+                    lhsT_scale=w4_planes[:, c0 + (a + b) * KP : c0 + (a + b) * KP + P],
                     rhs=v_words[a][:].bitcast(FP8X4),
                     rhs_scale=v_planes[a][:],
                     start=(a == 0),
                     stop=(a == PASSES - 1),
                 )
-            if minus_enc is None:
-                minus_enc = ring.tile([P, S], F32, name="minus_enc", bufs=7)
+            minus_enc = ring.tile([P, S], F32, name="minus_enc", bufs=2)
             nc.scalar.activation(minus_enc[:], acc[:], ACT.Tanh, scale=-1.0)
             return minus_enc
 
-        def place(k, number, minus_enc, h):
+        def linear(k):
             b, i = divmod(k, PACK)
-            acc = bank(number)
-            for a in range(PASSES):
+            acc = bank(LINEAR_BANK[k])
+            order = (2, 0, 1) if 0 < k < 3 else (0, 1, 2)
+            for a in order:
                 codes, plane = w1_q[a, b]
                 nc.tensor.matmul_mx(
                     out=acc[:],
@@ -193,25 +219,33 @@ def tile_list_fraud_residual_queue_kernel(
                     lhsT_scale=plane[:, i * P : (i + 1) * P],
                     rhs=v_words[a][:].bitcast(FP8X4),
                     rhs_scale=v_planes[a][:],
-                    start=(a == 0),
-                    stop=(a == PASSES - 1),
+                    start=(a == order[0]),
+                    stop=(a == order[-1]),
                 )
+            return acc
+
+        def place(k, minus_enc, h=None):
+            b, i = divmod(k, PACK)
+            acc = lin[k] if k in lin else linear(k)
+            if h is None:
+                h = ring.tile([P, S], F32, name="h")
             nc.vector.scalar_tensor_tensor(h[:], minus_enc[:], dec_sb[:, b, i : i + 1], acc[:], ALU.mult, ALU.add)
-            return h
+            nc.vector.tensor_tensor(pages[i][:].indirect(places[:]), h[:], wgs_sb[:], ALU.mult)
 
-        def scatter(k, h):
-            nc.vector.tensor_tensor(pages[k if k < PACK else PACK + k % 2][:].indirect(places[:]), h[:], wgs_sb[:], ALU.mult)
+        def pair_tile(q):
+            return ring.tile([P, BANK], BF16, name="pair", bufs=4, align_bytes=64)
 
-        def fresh_h():
-            return ring.tile([P, S], F32, name="h", bufs=2)
+        def pair_after_wf(q):
+            return over.tile([P, BANK], BF16, name="pair%d" % q, offset=OVER_AT["wf1"] + 2 * BANK * q, align_bytes=64)
 
-        def add_turned(b, u, numbers, copies):
-            accs = [bank(n) for n in numbers]
-            for step in range(3):
-                for q, acc in enumerate(accs):
+        def add_turned(b, u, banks, make_pair):
+            pairs = []
+            for q in range(4):
+                acc = bank(banks[q])
+                for step in range(2):
                     for mb in range(2):
                         cols = slice((2 * q + mb) * P, (2 * q + mb + 1) * P)
-                        for e in ((0, 1), (0,), (1,))[step]:
+                        for e in range(2):
                             source = queue_sb[b, u][:, e, cols] if step == 0 else pages[2 * u + e][:, cols]
                             nc.tensor.matmul(
                                 acc[:, (2 * mb + e) * P : (2 * mb + e + 1) * P],
@@ -219,100 +253,122 @@ def tile_list_fraud_residual_queue_kernel(
                                 rhs=identity[:],
                                 is_transpose=True,
                                 start=(step == 0 and mb == 0 and e == 0),
-                                stop=(step == 2 and mb == 1),
+                                stop=(step == 1 and mb == 1 and e == 1),
                             )
-            pairs = []
-            for q, acc in enumerate(accs):
-                pair = turned.tile([P, BANK], BF16, name="pair", align_bytes=64)
-                copies[q](
+                pair = make_pair(q)
+                nc.scalar.copy(
                     pair[:].rearrange("m (g p e) -> m g p e", g=2, e=2),
                     acc[:].rearrange("m (g e p) -> m g p e", g=2, e=2),
                 )
                 pairs.append(pair)
             return pairs
 
-        def turn_back(b, q, pairs, number, copy):
-            acc = bank(number)
+        def turn_back(q, pairs, z):
+            acc = bank(4 + q)
             for u in range(2):
                 words = pairs[u][q][:].bitcast(F32)
                 for mb in range(2):
                     nc.tensor.transpose(
                         acc[:, (2 * u + mb) * P : (2 * u + mb + 1) * P], words[:, mb * P : (mb + 1) * P], identity[:]
                     )
-            z = woven.tile([P, 2 * BANK], BF16, name="z", align_bytes=64)
-            copy(z[:].bitcast(F32).rearrange("p (m u) -> p m u", u=2), acc[:].rearrange("p (u m) -> p m u", u=2))
-            quantise(z_q[b, q // 2], (q % 2) * 256, z)
+            nc.scalar.copy(z[:].bitcast(F32).rearrange("p (m u) -> p m u", u=2), acc[:].rearrange("p (u m) -> p m u", u=2))
+            quantise(z_q[0, q // 2], (q % 2) * QUARTER, z[:])
 
-        def add_queue(k, rows):
-            b, i = divmod(k, PACK)
-            width = T2 // len(rows)
-            for part, tile in enumerate(rows):
-                cols = slice(part * width, (part + 1) * width)
-                nc.vector.tensor_tensor(
-                    tile[:, i, :], pages[k if k < PACK else PACK + k % 2][:, cols], queue_sb[b, i // 2][:, i % 2, cols], ALU.add
-                )
-
-        def weave(b, q, rows, copy):
-            width = T2 // len(rows)
-            c0 = q * QUARTER % width
-            z = woven.tile([P, PACK * QUARTER], BF16, name="z", align_bytes=64)
-            copy(
-                z[:].rearrange("p (c e i) -> p c i e", e=4, i=PACK),
-                rows[q * QUARTER // width][:, :, c0 : c0 + QUARTER].rearrange("p i (c e) -> p c i e", e=4),
+        def turn_back_rows(half, pairs, rows):
+            acc = bank((3, 0)[half])
+            for mb in range(4):
+                words = pairs[2 * half + mb // 2][:].bitcast(F32)
+                nc.tensor.transpose(acc[:, mb * P : (mb + 1) * P], words[:, (mb % 2) * P : (mb % 2 + 1) * P], identity[:])
+            nc.scalar.copy(
+                rows[:, 0:2, half * BANK : (half + 1) * BANK], acc[:].bitcast(BF16).rearrange("p (m e) -> p e m", e=2)
             )
-            quantise(z_q[b, q // 2], (q % 2) * QUARTER, z)
 
-        z_rows = [None, [keep([P, PACK, T2 // 2], BF16, "z_rows%d" % part) for part in range(2)]]
-
-        enc = {0: encode(0, 0, staged(2, S, F32)), 1: encode(1, 2)}
-        quantise(w1_q[2, 0], 0, cast(nc.vector.tensor_copy, w1_raw[2, 0], 0, 1, staged(0, KP)))
-        quantise(w1_q[2, 0], P, cast(nc.scalar.copy, w1_raw[2, 0], 1, 2, staged(1, KP)))
-        quantise(w1_q[2, 0], 2 * P, cast(nc.scalar.copy, w1_raw[2, 0], 2, 4, staged(3, 2 * KP)))
-        h = {0: place(0, 1, enc[0], fresh_h())}
-        scatter(0, h[0])
-        order_w4(1)
-        h[1] = place(1, 3, enc[1], fresh_h())
-        scatter(1, h[1])
-        for k in range(2, 4):
-            enc[k] = encode(k, [0,2,1,1,4,5,6,7][k])
+        lin = {}
+        enc = {0: encode(0)}
+        quantise(w1_q[2, 0], 0, cast(nc.vector.tensor_copy, w1_raw[2, 0], 0, 2, slot(3, [P, 2 * KP], BF16))[:])
+        lin[0] = linear(0)
+        lin[1] = linear(1)
+        quantise(w1_q[2, 0], 2 * P, cast(nc.scalar.copy, w1_raw[2, 0], 2, PACK, staged(0, 2 * KP))[:])
+        lin[2] = linear(2)
+        place(0, enc[0])
+        enc[1] = encode(1)
+        enc[2] = encode(2)
+        order_words(1)
+        place(1, enc[1])
+        lin[3] = linear(3)
+        enc[3] = encode(3)
         for a in range(PASSES):
-            quantise(w1_q[a, 1], 0, cast(nc.scalar.copy, w1_raw[a, 1], 0, PACK, staged((2, 0, 1)[a])))
-        for k in range(4, 8):
-            enc[k] = encode(k, [0,2,1,1,4,5,6,7][k])
-        pairs = []
-        for k in range(2, 8):
-            h[k] = place(k, [1,3,3,3,0,2,1,3][k], enc[k], staged(0, S, F32) if k == 2 else staged(1, S, F32) if k == 3 else fresh_h())
-            if k > 4:
-                add_queue(k - 1, z_rows[1])
-            scatter(k, h[k])
-        pairs = [add_turned(0, u, (4, 5, 6, 7), [nc.scalar.copy] * 4) for u in range(2)]
-        for q in range(4):
-            turn_back(0, q, pairs, 4 + q, nc.scalar.copy)
+            quantise(w1_q[a, 1], 0, cast(nc.scalar.copy, w1_raw[a, 1], 0, PACK, staged(4 + a))[:])
+        place(2, enc[2], staged(5, S, F32))
+        enc[4] = encode(4)
+        pairs0 = [add_turned(0, 0, (4, 5, 6, 7), pair_tile)]
+        lin[4] = linear(4)
+        place(3, enc[3], staged(6, S, F32))
+        lin[5] = linear(5)
+        enc[5] = encode(5)
         for b in range(BLOCKS):
-            quantise(wf_q[b], 0, cast(nc.scalar.copy, wf_raw[b], 0, PACK, staged(2 + b)))
-        add_queue(7, z_rows[1])
+            quantise(wf_q[b], 0, cast(nc.scalar.copy, wf_raw[b], 0, PACK, staged(5 + b))[:])
+        place(4, enc[4])
+        lin[6] = linear(6)
+        enc[6] = encode(6)
+        pairs0.append(add_turned(0, 1, (4, 5, 6, 7), pair_after_wf))
+        place(5, enc[5], staged(5, S, F32))
+        lin[7] = linear(7)
+        enc[7] = encode(7)
+        for q in range(4):
+            turn_back(q, pairs0, staged(10 + q, 2 * BANK))
+        pairs1 = add_turned(1, 0, (7, 6, 5, 4), pair_tile)
+        place(6, enc[6], staged(6, S, F32))
+        rows = keep([P, PACK, T2], BF16, "z_rows")
+        for half in range(2):
+            turn_back_rows(half, pairs1, rows)
+        nc.vector.tensor_tensor(rows[:, 2, :], pages[2][:], queue_sb[1, 1][:, 0, :], ALU.add)
+        place(7, enc[7], staged(13, S, F32))
+
+        def score(acc, b, q, c):
+            nc.tensor.matmul_mx(
+                out=acc[:, (c % 2) * QUARTER : (c % 2 + 1) * QUARTER],
+                lhsT=wf_q[b][0][:, c * P : (c + 1) * P].bitcast(FP8X4),
+                lhsT_scale=wf_q[b][1][:, c * P : (c + 1) * P],
+                rhs=z_q[b, q // 2][0][:, (q % 2) * QUARTER : (q % 2 + 1) * QUARTER].bitcast(FP8X4),
+                rhs_scale=z_q[b, q // 2][1][:, (q % 2) * QUARTER : (q % 2 + 1) * QUARTER],
+                start=(b == 0 and c % 2 == 0),
+                stop=(b == BLOCKS - 1 and c % 2 == 1),
+            )
+
+        SCORE_BANKS = ((7, 6), (5, 4), (3, 0), (2, 1))
+        accs = [[bank(n) for n in pair] for pair in SCORE_BANKS]
+        for q in range(4):
+            for c in range(PACK):
+                score(accs[q][c // 2], 0, q, c)
 
         out_rows = out.rearrange("(p c) m -> p c m", c=PACK)
-        score_banks = ((4, 5, 6, 7), (0, 2, 1, 3))
-        for half in range(2):
-            weave(1, 2 * half, z_rows[1], nc.scalar.copy)
-            weave(1, 2 * half + 1, z_rows[1], nc.vector.tensor_copy)
-        for half in range(2):
-            scores = big.tile([P, PACK, BANK], F32, name="big", align_bytes=64)
+        woven = []
+        for q in range(4):
+            cols = slice(q * QUARTER, (q + 1) * QUARTER)
+            nc.vector.tensor_tensor(rows[:, 3, cols], pages[3][:, cols], queue_sb[1, 1][:, 1, cols], ALU.add)
+            z = ring.tile([P, PACK * QUARTER], BF16, name="woven", bufs=4, align_bytes=64)
+            (nc.scalar.copy if q == 1 else nc.vector.tensor_copy)(
+                z[:].rearrange("p (c e i) -> p c i e", e=4, i=PACK),
+                rows[:, :, cols].rearrange("p i (c e) -> p c i e", e=4),
+            )
+            quantise(z_q[1, q // 2], (q % 2) * QUARTER, z[:])
             for c in range(PACK):
-                acc = bank(score_banks[half][c])
-                for b in range(BLOCKS):
-                    nc.tensor.matmul_mx(
-                        out=acc[:],
-                        lhsT=wf_q[b][0][:, c * P : (c + 1) * P].bitcast(FP8X4),
-                        lhsT_scale=wf_q[b][1][:, c * P : (c + 1) * P],
-                        rhs=z_q[b, half][0][:].bitcast(FP8X4),
-                        rhs_scale=z_q[b, half][1][:],
-                        start=(b == 0),
-                        stop=(b == BLOCKS - 1),
+                score(accs[q][c // 2], 1, q, c)
+            for pair in range(2):
+                scores = ring.tile([P, 2, QUARTER], F32, name="scores", bufs=8, align_bytes=64)
+                acc = accs[q][pair]
+                if q >= 2 and pair == 1:
+                    nc.vector.tensor_tensor(
+                        scores[:],
+                        acc[:].rearrange("p (c m) -> p c m", c=2),
+                        bias_sb[:, 2 * pair : 2 * pair + 2].unsqueeze(2).to_broadcast([P, 2, QUARTER]),
+                        ALU.add,
                     )
-                if c % 2 == 0:
-                    nc.scalar.activation(scores[:, c, :], acc[:], ACT.Identity, bias=bias_sb[:, c : c + 1])
                 else:
-                    nc.vector.tensor_scalar(scores[:, c, :], acc[:], bias_sb[:, c : c + 1], None, ALU.add)
-                nc.sync.dma_start(out=out_rows[:, c, half * BANK : (half + 1) * BANK], in_=scores[:, c, :])
+                    for e in range(2):
+                        c = 2 * pair + e
+                        nc.scalar.activation(
+                            scores[:, e, :], acc[:, e * QUARTER : (e + 1) * QUARTER], ACT.Identity, bias=bias_sb[:, c : c + 1]
+                        )
+                nc.sync.dma_start(out=out_rows[:, 2 * pair : 2 * pair + 2, cols], in_=scores[:])

@@ -154,7 +154,8 @@ def tile_list_fraud_residual_queue_kernel(
         def cast(copy, raw, t0, t1, tile):
             src = raw[:].rearrange("p j (m t) -> p m j t", t=PACK)
             dst = tile[:].rearrange("p (t m j) -> p m j t", m=P, j=PACK)
-            copy(dst, src[:, :, :, t0:t1])
+            for t in range(t0, t1, 2):
+                copy(dst[:, :, :, t - t0 : t - t0 + 2], src[:, :, :, t : t + 2])
             return tile
 
         def quantise(operand, c0, ap):

@@ -29,6 +29,7 @@ PLANE_ROWS = 100
 PACKED_FROM = 32 - 4 * PASSES
 ENCODE_BANK = (2, 0, 0, 0, 0, 0, 0, 0)
 LINEAR_BANK = (0, 1, 2, 1, 2, 1, 2, 1)
+TANH_SLOT = {2: 6, 3: 7, 4: 4}
 SLOT = 8192
 OVER_AT = {"wf0": 2 * T, "queue00": 2 * T + 2 * SLOT, "wf1": 2 * T + SLOT}
 
@@ -123,13 +124,13 @@ def tile_list_fraud_residual_queue_kernel(
         w1_raw[1, 0] = load_weight(4, w1, 1, 0)
         move_plane(2)
         w1_raw[2, 0] = load_weight(5, w1, 2, 0)
+        w4_raw.append(load_w4(1))
         dec_sb = keep([P, BLOCKS, PACK], F32, "dec_sb")
         nc.sync.dma_start(out=dec_sb[:], in_=dec.rearrange("(b p i) -> p b i", b=BLOCKS, i=PACK))
         places = held.tile([P, S // 16], U16, name="places")
         nc.sync.dma_start(places[:], offs2)
         wgs_sb = keep([P, S], F32, "wgs_sb")
         nc.sync.dma_start(out=wgs_sb[:], in_=wgs)
-        w4_raw.append(load_w4(1))
         for a in range(PASSES):
             w1_raw[a, 1] = load_weight((6, 7, 4)[a], w1, a, 1)
         queue_sb = {(0, 0): load_queue("queue00", 0, 0), (0, 1): load_queue(0, 0, 1)}
@@ -204,7 +205,10 @@ def tile_list_fraud_residual_queue_kernel(
                     start=(a == 0),
                     stop=(a == PASSES - 1),
                 )
-            minus_enc = ring.tile([P, S], F32, name="minus_enc", bufs=2)
+            if k in TANH_SLOT:
+                minus_enc = slot(TANH_SLOT[k], [P, S], F32)
+            else:
+                minus_enc = ring.tile([P, S], F32, name="minus_enc")
             nc.scalar.activation(minus_enc[:], acc[:], ACT.Tanh, scale=-1.0)
             return minus_enc
 
@@ -225,13 +229,16 @@ def tile_list_fraud_residual_queue_kernel(
                 )
             return acc
 
-        def place(k, minus_enc, h=None):
+        def residual(k, h=None):
             b, i = divmod(k, PACK)
-            acc = lin[k] if k in lin else linear(k)
+            acc = lin[k]
             if h is None:
-                h = ring.tile([P, S], F32, name="h")
-            nc.vector.scalar_tensor_tensor(h[:], minus_enc[:], dec_sb[:, b, i : i + 1], acc[:], ALU.mult, ALU.add)
-            nc.vector.tensor_tensor(pages[i][:].indirect(places[:]), h[:], wgs_sb[:], ALU.mult)
+                h = ring.tile([P, S], F32, name="h", bufs=3)
+            nc.vector.scalar_tensor_tensor(h[:], enc[k][:], dec_sb[:, b, i : i + 1], acc[:], ALU.mult, ALU.add)
+            return h
+
+        def scatter(page, h):
+            nc.vector.tensor_tensor(page[:].indirect(places[:]), h[:], wgs_sb[:], ALU.mult)
 
         def pair_tile(q):
             return ring.tile([P, BANK], BF16, name="pair", bufs=4, align_bytes=64)
@@ -284,47 +291,86 @@ def tile_list_fraud_residual_queue_kernel(
                 rows[:, 0:2, half * BANK : (half + 1) * BANK], acc[:].bitcast(BF16).rearrange("p (m e) -> p e m", e=2)
             )
 
+        def add_turned_row(rows):
+            pairs = []
+            for half in range(2):
+                acc = bank(7 - half)
+                for step in range(2):
+                    for mb in range(4):
+                        cols = slice((4 * half + mb) * P, (4 * half + mb + 1) * P)
+                        nc.tensor.matmul(
+                            acc[:, mb * P : (mb + 1) * P],
+                            lhsT=queue_sb[1, 1][:, 0, cols] if step == 0 else pages[2][:, cols],
+                            rhs=identity[:],
+                            is_transpose=True,
+                            start=(step == 0 and mb == 0),
+                            stop=(step == 1 and mb == 3),
+                        )
+                pair = pair_after_wf(half)
+                nc.scalar.copy(
+                    pair[:].rearrange("m (g p e) -> m g p e", g=2, e=2),
+                    acc[:].rearrange("m (g e p) -> m g p e", g=2, e=2),
+                )
+                pairs.append(pair)
+            for half in range(2):
+                acc = bank(5 - half)
+                words = pairs[half][:].bitcast(F32)
+                for g in range(2):
+                    nc.tensor.transpose(acc[:, g * P : (g + 1) * P], words[:, g * P : (g + 1) * P], identity[:])
+                nc.scalar.copy(
+                    rows[:, 2, half * BANK : (half + 1) * BANK].rearrange("p (g e m) -> p g e m", g=2, e=2),
+                    acc[:, 0 : 2 * P].bitcast(BF16).rearrange("p (g m e) -> p g e m", g=2, e=2),
+                )
+
         lin = {}
         enc = {0: encode(0)}
         quantise(w1_q[2, 0], 0, cast(nc.vector.tensor_copy, w1_raw[2, 0], 0, 2, slot(3, [P, 2 * KP], BF16))[:])
         lin[0] = linear(0)
         lin[1] = linear(1)
+        order_words(1)
+        h = {0: residual(0)}
         quantise(w1_q[2, 0], 2 * P, cast(nc.scalar.copy, w1_raw[2, 0], 2, PACK, staged(0, 2 * KP))[:])
         lin[2] = linear(2)
-        place(0, enc[0])
+        scatter(pages[0], h[0])
         enc[1] = encode(1)
-        enc[2] = encode(2)
-        order_words(1)
-        place(1, enc[1])
+        h[1] = residual(1)
+        scatter(pages[1], h[1])
         lin[3] = linear(3)
-        enc[3] = encode(3)
         for a in range(PASSES):
             quantise(w1_q[a, 1], 0, cast(nc.scalar.copy, w1_raw[a, 1], 0, PACK, staged(4 + a))[:])
-        place(2, enc[2], staged(5, S, F32))
+        enc[2] = encode(2)
+        enc[3] = encode(3)
+        h[2] = residual(2, staged(5, S, F32))
+        scatter(pages[2], h[2])
         enc[4] = encode(4)
         pairs0 = [add_turned(0, 0, (4, 5, 6, 7), pair_tile)]
         lin[4] = linear(4)
-        place(3, enc[3], staged(6, S, F32))
+        h[3] = residual(3, staged(6, S, F32))
+        scatter(pages[3], h[3])
         lin[5] = linear(5)
         enc[5] = encode(5)
         for b in range(BLOCKS):
-            quantise(wf_q[b], 0, cast(nc.scalar.copy, wf_raw[b], 0, PACK, staged(5 + b))[:])
-        place(4, enc[4])
+            quantise(wf_q[b], 0, cast(nc.scalar.copy, wf_raw[b], 0, PACK, staged(5 - b))[:])
+        h[4] = residual(4)
         lin[6] = linear(6)
         enc[6] = encode(6)
         pairs0.append(add_turned(0, 1, (4, 5, 6, 7), pair_after_wf))
-        place(5, enc[5], staged(5, S, F32))
+        h[5] = residual(5, staged(5, S, F32))
         lin[7] = linear(7)
         enc[7] = encode(7)
+        scatter(pages[0], h[4])
+        h[6] = residual(6, staged(4, S, F32))
+        scatter(pages[1], h[5])
         for q in range(4):
             turn_back(q, pairs0, staged(10 + q, 2 * BANK))
+        h[7] = residual(7, staged(13, S, F32))
         pairs1 = add_turned(1, 0, (7, 6, 5, 4), pair_tile)
-        place(6, enc[6], staged(6, S, F32))
+        scatter(pages[2], h[6])
         rows = keep([P, PACK, T2], BF16, "z_rows")
         for half in range(2):
             turn_back_rows(half, pairs1, rows)
-        nc.vector.tensor_tensor(rows[:, 2, :], pages[2][:], queue_sb[1, 1][:, 0, :], ALU.add)
-        place(7, enc[7], staged(13, S, F32))
+        add_turned_row(rows)
+        scatter(pages[3], h[7])
 
         def score(acc, b, q, c):
             nc.tensor.matmul_mx(
@@ -337,7 +383,7 @@ def tile_list_fraud_residual_queue_kernel(
                 stop=(b == BLOCKS - 1 and c % 2 == 1),
             )
 
-        SCORE_BANKS = ((7, 6), (5, 4), (3, 0), (2, 1))
+        SCORE_BANKS = ((3, 0), (2, 1), (7, 6), (5, 4))
         accs = [[bank(n) for n in pair] for pair in SCORE_BANKS]
         for q in range(4):
             for c in range(PACK):

@@ -27,11 +27,13 @@ BANK = 512
 QUARTER = T2 // 4
 PLANE_ROWS = 100
 PACKED_FROM = 32 - 4 * PASSES
-ENCODE_BANK = (2, 0, 0, 0, 0, 0, 0, 0)
-LINEAR_BANK = (0, 1, 2, 1, 2, 1, 2, 1)
-TANH_SLOT = {2: 6, 3: 7, 4: 4}
+ENCODE_BANK = (2, 3, 4, 0, 4, 5, 6, 7)
+LINEAR_BANK = (0, 1, 2, 3, 4, 5, 6, 7)
+ROW_BANKS = ((4, 5, 0), (2, 3, 1), (4, 5, 2))
+SCORE_BANKS = ((6, 7), (0, 1), (3, 4), (5, 2))
 SLOT = 8192
-OVER_AT = {"wf0": 2 * T, "queue00": 2 * T + 2 * SLOT, "wf1": 2 * T + SLOT}
+OVER_AT = {"wf1": 2 * T, "w1_20": 2 * T + SLOT, "w1_21": 2 * T + 2 * SLOT}
+TANH_AT = {1: ("w1_20", 0), 2: ("w1_20", 1), 4: ("w1_21", 0), 5: ("w1_21", 1), 6: ("w1_21", 2), 7: ("w1_21", 3)}
 
 
 def tile_list_fraud_residual_queue_kernel(
@@ -123,7 +125,7 @@ def tile_list_fraud_residual_queue_kernel(
         move_plane(1)
         w1_raw[1, 0] = load_weight(4, w1, 1, 0)
         move_plane(2)
-        w1_raw[2, 0] = load_weight(5, w1, 2, 0)
+        w1_raw[2, 0] = load_weight("w1_20", w1, 2, 0)
         w4_raw.append(load_w4(1))
         dec_sb = keep([P, BLOCKS, PACK], F32, "dec_sb")
         nc.sync.dma_start(out=dec_sb[:], in_=dec.rearrange("(b p i) -> p b i", b=BLOCKS, i=PACK))
@@ -132,10 +134,10 @@ def tile_list_fraud_residual_queue_kernel(
         wgs_sb = keep([P, S], F32, "wgs_sb")
         nc.sync.dma_start(out=wgs_sb[:], in_=wgs)
         for a in range(PASSES):
-            w1_raw[a, 1] = load_weight((6, 7, 4)[a], w1, a, 1)
-        queue_sb = {(0, 0): load_queue("queue00", 0, 0), (0, 1): load_queue(0, 0, 1)}
-        wf_raw = [load_weight("wf%d" % b, wf, b, 0) for b in range(BLOCKS)]
-        for number, b, u in ((1, 1, 0), (5, 1, 1)):
+            w1_raw[a, 1] = load_weight((6, 7, "w1_21")[a], w1, a, 1)
+        queue_sb = {(0, 0): load_queue(4, 0, 0), (0, 1): load_queue(0, 0, 1)}
+        wf_raw = [load_weight((5, "wf1")[b], wf, b, 0) for b in range(BLOCKS)]
+        for number, b, u in ((1, 1, 0), (6, 1, 1)):
             queue_sb[b, u] = load_queue(number, b, u)
         bias_sb = keep([P, PACK], F32, "bias_sb")
         nc.sync.dma_start(out=bias_sb[:], in_=bf.rearrange("(p c) -> p c", c=PACK))
@@ -149,8 +151,8 @@ def tile_list_fraud_residual_queue_kernel(
             v_words[a] = tile
             nc.vector.tensor_copy(tile[:], table[a][:].bitcast(U32).indirect(picks[:]))
 
-        def quantised(name):
-            return keep([P, KP], U32, name + "_codes"), keep([P, KP], U8, name + "_plane")
+        def quantised(name, width=KP):
+            return keep([P, width], U32, name + "_codes"), keep([P, width], U8, name + "_plane")
 
         def cast(copy, raw, t0, t1, tile):
             src = raw[:].rearrange("p j (m t) -> p m j t", t=PACK)
@@ -168,7 +170,7 @@ def tile_list_fraud_residual_queue_kernel(
 
         w1_q = {(a, b): quantised("w1_%d_%d" % (a, b)) for b in range(BLOCKS) for a in range(PASSES)}
         wf_q = [quantised("wf_%d" % b) for b in range(BLOCKS)]
-        z_q = {(b, half): quantised("z_%d_%d" % (b, half)) for b in range(BLOCKS) for half in range(2)}
+        z_q = {(b, q): quantised("z_%d_%d" % (b, q), QUARTER) for b in range(BLOCKS) for q in range(4)}
 
         gather(0, keep([P, S], U32, "v_words0"))
         w4_codes = [keep([P, PASSES * 2 * KP], U8, "w4_codes%d" % b) for b in range(BLOCKS)]
@@ -205,8 +207,9 @@ def tile_list_fraud_residual_queue_kernel(
                     start=(a == 0),
                     stop=(a == PASSES - 1),
                 )
-            if k in TANH_SLOT:
-                minus_enc = slot(TANH_SLOT[k], [P, S], F32)
+            if k in TANH_AT:
+                over_at, place = TANH_AT[k]
+                minus_enc = over.tile([P, S], F32, name="minus_enc%d" % k, offset=OVER_AT[over_at] + 4 * S * place, align_bytes=64)
             else:
                 minus_enc = ring.tile([P, S], F32, name="minus_enc")
             nc.scalar.activation(minus_enc[:], acc[:], ACT.Tanh, scale=-1.0)
@@ -215,7 +218,7 @@ def tile_list_fraud_residual_queue_kernel(
         def linear(k):
             b, i = divmod(k, PACK)
             acc = bank(LINEAR_BANK[k])
-            order = (2, 0, 1) if 0 < k < 3 else (0, 1, 2)
+            order = (2, 0, 1) if 0 < k < PACK else (0, 1, 2)
             for a in order:
                 codes, plane = w1_q[a, b]
                 nc.tensor.matmul_mx(
@@ -272,7 +275,7 @@ def tile_list_fraud_residual_queue_kernel(
             return pairs
 
         def turn_back(q, pairs, z):
-            acc = bank(4 + q)
+            acc = bank(q)
             for u in range(2):
                 words = pairs[u][q][:].bitcast(F32)
                 for mb in range(2):
@@ -280,47 +283,37 @@ def tile_list_fraud_residual_queue_kernel(
                         acc[:, (2 * u + mb) * P : (2 * u + mb + 1) * P], words[:, mb * P : (mb + 1) * P], identity[:]
                     )
             nc.scalar.copy(z[:].bitcast(F32).rearrange("p (m u) -> p m u", u=2), acc[:].rearrange("p (u m) -> p m u", u=2))
-            quantise(z_q[0, q // 2], (q % 2) * QUARTER, z[:])
+            quantise(z_q[0, q], 0, z[:])
 
-        def turn_back_rows(half, pairs, rows):
-            acc = bank((3, 0)[half])
-            for mb in range(4):
-                words = pairs[2 * half + mb // 2][:].bitcast(F32)
-                nc.tensor.transpose(acc[:, mb * P : (mb + 1) * P], words[:, (mb % 2) * P : (mb % 2 + 1) * P], identity[:])
-            nc.scalar.copy(
-                rows[:, 0:2, half * BANK : (half + 1) * BANK], acc[:].bitcast(BF16).rearrange("p (m e) -> p e m", e=2)
-            )
-
-        def add_turned_row(rows):
+        def add_turned_row(i, rows):
             pairs = []
             for half in range(2):
-                acc = bank(7 - half)
+                acc = bank(ROW_BANKS[i][half])
                 for step in range(2):
                     for mb in range(4):
                         cols = slice((4 * half + mb) * P, (4 * half + mb + 1) * P)
                         nc.tensor.matmul(
                             acc[:, mb * P : (mb + 1) * P],
-                            lhsT=queue_sb[1, 1][:, 0, cols] if step == 0 else pages[2][:, cols],
+                            lhsT=queue_sb[1, i // 2][:, i % 2, cols] if step == 0 else pages[i][:, cols],
                             rhs=identity[:],
                             is_transpose=True,
                             start=(step == 0 and mb == 0),
                             stop=(step == 1 and mb == 3),
                         )
-                pair = pair_after_wf(half)
+                pair = pair_tile(half)
                 nc.scalar.copy(
                     pair[:].rearrange("m (g p e) -> m g p e", g=2, e=2),
                     acc[:].rearrange("m (g e p) -> m g p e", g=2, e=2),
                 )
                 pairs.append(pair)
-            for half in range(2):
-                acc = bank(5 - half)
-                words = pairs[half][:].bitcast(F32)
-                for g in range(2):
-                    nc.tensor.transpose(acc[:, g * P : (g + 1) * P], words[:, g * P : (g + 1) * P], identity[:])
-                nc.scalar.copy(
-                    rows[:, 2, half * BANK : (half + 1) * BANK].rearrange("p (g e m) -> p g e m", g=2, e=2),
-                    acc[:, 0 : 2 * P].bitcast(BF16).rearrange("p (g m e) -> p g e m", g=2, e=2),
-                )
+            acc = bank(ROW_BANKS[i][2])
+            for g in range(4):
+                words = pairs[g // 2][:].bitcast(F32)
+                nc.tensor.transpose(acc[:, g * P : (g + 1) * P], words[:, (g % 2) * P : (g % 2 + 1) * P], identity[:])
+            nc.scalar.copy(
+                rows[:, i, :].rearrange("p (g e m) -> p g e m", g=4, e=2),
+                acc[:].bitcast(BF16).rearrange("p (g m e) -> p g e m", g=4, e=2),
+            )
 
         lin = {}
         enc = {0: encode(0)}
@@ -330,46 +323,41 @@ def tile_list_fraud_residual_queue_kernel(
         order_words(1)
         h = {0: residual(0)}
         quantise(w1_q[2, 0], 2 * P, cast(nc.scalar.copy, w1_raw[2, 0], 2, PACK, staged(0, 2 * KP))[:])
-        lin[2] = linear(2)
-        scatter(pages[0], h[0])
         enc[1] = encode(1)
+        enc[2] = encode(2)
+        lin[2] = linear(2)
+        lin[3] = linear(3)
+        enc[3] = encode(3)
+        scatter(pages[0], h[0])
         h[1] = residual(1)
         scatter(pages[1], h[1])
-        lin[3] = linear(3)
         for a in range(PASSES):
             quantise(w1_q[a, 1], 0, cast(nc.scalar.copy, w1_raw[a, 1], 0, PACK, staged(4 + a))[:])
-        enc[2] = encode(2)
-        enc[3] = encode(3)
         h[2] = residual(2, staged(5, S, F32))
         scatter(pages[2], h[2])
-        enc[4] = encode(4)
-        pairs0 = [add_turned(0, 0, (4, 5, 6, 7), pair_tile)]
-        lin[4] = linear(4)
         h[3] = residual(3, staged(6, S, F32))
+        for k in range(PACK, TILES):
+            enc[k] = encode(k)
+        pairs0 = [add_turned(0, 0, (4, 5, 6, 7), pair_tile)]
+        for k in range(PACK, TILES):
+            lin[k] = linear(k)
         scatter(pages[3], h[3])
-        lin[5] = linear(5)
-        enc[5] = encode(5)
-        for b in range(BLOCKS):
-            quantise(wf_q[b], 0, cast(nc.scalar.copy, wf_raw[b], 0, PACK, staged(5 - b))[:])
         h[4] = residual(4)
-        lin[6] = linear(6)
-        enc[6] = encode(6)
-        pairs0.append(add_turned(0, 1, (4, 5, 6, 7), pair_after_wf))
-        h[5] = residual(5, staged(5, S, F32))
-        lin[7] = linear(7)
-        enc[7] = encode(7)
+        h[5] = residual(5)
+        for b in range(BLOCKS):
+            quantise(wf_q[b], 0, cast(nc.scalar.copy, wf_raw[b], 0, PACK, slot(4, [P, PACK * KP], BF16) if b == 0 else staged(5))[:])
+        pairs0.append(add_turned(0, 1, (0, 1, 2, 3), pair_after_wf))
         scatter(pages[0], h[4])
-        h[6] = residual(6, staged(4, S, F32))
+        h[6] = residual(6)
         scatter(pages[1], h[5])
         for q in range(4):
             turn_back(q, pairs0, staged(10 + q, 2 * BANK))
         h[7] = residual(7, staged(13, S, F32))
-        pairs1 = add_turned(1, 0, (7, 6, 5, 4), pair_tile)
-        scatter(pages[2], h[6])
         rows = keep([P, PACK, T2], BF16, "z_rows")
-        for half in range(2):
-            turn_back_rows(half, pairs1, rows)
-        add_turned_row(rows)
+        add_turned_row(0, rows)
+        add_turned_row(1, rows)
+        scatter(pages[2], h[6])
+        add_turned_row(2, rows)
         scatter(pages[3], h[7])
 
         def score(acc, b, q, c):
@@ -377,20 +365,37 @@ def tile_list_fraud_residual_queue_kernel(
                 out=acc[:, (c % 2) * QUARTER : (c % 2 + 1) * QUARTER],
                 lhsT=wf_q[b][0][:, c * P : (c + 1) * P].bitcast(FP8X4),
                 lhsT_scale=wf_q[b][1][:, c * P : (c + 1) * P],
-                rhs=z_q[b, q // 2][0][:, (q % 2) * QUARTER : (q % 2 + 1) * QUARTER].bitcast(FP8X4),
-                rhs_scale=z_q[b, q // 2][1][:, (q % 2) * QUARTER : (q % 2 + 1) * QUARTER],
+                rhs=z_q[b, q][0][:].bitcast(FP8X4),
+                rhs_scale=z_q[b, q][1][:],
                 start=(b == 0 and c % 2 == 0),
                 stop=(b == BLOCKS - 1 and c % 2 == 1),
             )
 
-        SCORE_BANKS = ((3, 0), (2, 1), (7, 6), (5, 4))
         accs = [[bank(n) for n in pair] for pair in SCORE_BANKS]
         for q in range(4):
             for c in range(PACK):
                 score(accs[q][c // 2], 0, q, c)
 
         out_rows = out.rearrange("(p c) m -> p c m", c=PACK)
-        woven = []
+
+        def store(q, pair, on_vector):
+            scores = ring.tile([P, 2, QUARTER], F32, name="scores", bufs=8, align_bytes=64)
+            acc = accs[q][pair]
+            if on_vector:
+                nc.vector.tensor_tensor(
+                    scores[:],
+                    acc[:].rearrange("p (c m) -> p c m", c=2),
+                    bias_sb[:, 2 * pair : 2 * pair + 2].unsqueeze(2).to_broadcast([P, 2, QUARTER]),
+                    ALU.add,
+                )
+            else:
+                for e in range(2):
+                    c = 2 * pair + e
+                    nc.scalar.activation(
+                        scores[:, e, :], acc[:, e * QUARTER : (e + 1) * QUARTER], ACT.Identity, bias=bias_sb[:, c : c + 1]
+                    )
+            nc.sync.dma_start(out=out_rows[:, 2 * pair : 2 * pair + 2, q * QUARTER : (q + 1) * QUARTER], in_=scores[:])
+
         for q in range(4):
             cols = slice(q * QUARTER, (q + 1) * QUARTER)
             nc.vector.tensor_tensor(rows[:, 3, cols], pages[3][:, cols], queue_sb[1, 1][:, 1, cols], ALU.add)
@@ -399,23 +404,9 @@ def tile_list_fraud_residual_queue_kernel(
                 z[:].rearrange("p (c e i) -> p c i e", e=4, i=PACK),
                 rows[:, :, cols].rearrange("p i (c e) -> p c i e", e=4),
             )
-            quantise(z_q[1, q // 2], (q % 2) * QUARTER, z[:])
+            quantise(z_q[1, q], 0, z[:])
             for c in range(PACK):
                 score(accs[q][c // 2], 1, q, c)
+        for q in range(4):
             for pair in range(2):
-                scores = ring.tile([P, 2, QUARTER], F32, name="scores", bufs=8, align_bytes=64)
-                acc = accs[q][pair]
-                if q >= 2 and pair == 1:
-                    nc.vector.tensor_tensor(
-                        scores[:],
-                        acc[:].rearrange("p (c m) -> p c m", c=2),
-                        bias_sb[:, 2 * pair : 2 * pair + 2].unsqueeze(2).to_broadcast([P, 2, QUARTER]),
-                        ALU.add,
-                    )
-                else:
-                    for e in range(2):
-                        c = 2 * pair + e
-                        nc.scalar.activation(
-                            scores[:, e, :], acc[:, e * QUARTER : (e + 1) * QUARTER], ACT.Identity, bias=bias_sb[:, c : c + 1]
-                        )
-                nc.sync.dma_start(out=out_rows[:, 2 * pair : 2 * pair + 2, cols], in_=scores[:])
+                store(q, pair, q >= 2 and pair == 1)

@@ -32,6 +32,7 @@ LINEAR_BANK = (0, 1, 2, 3, 4, 5, 6, 7)
 ROW_BANKS = ((4, 5, 0), (2, 3, 1), (4, 5, 2))
 SCORE_BANKS = ((6, 7), (0, 1), (3, 4), (5, 2))
 SLOT = 8192
+STAGE_AT = 2 * T + 3 * SLOT
 OVER_AT = {"wf1": 2 * T, "w1_20": 2 * T + SLOT, "w1_21": 2 * T + 2 * SLOT}
 TANH_AT = {1: ("w1_20", 0), 2: ("w1_20", 1), 4: ("w1_21", 0), 5: ("w1_21", 1), 6: ("w1_21", 2), 7: ("w1_21", 3)}
 
@@ -168,9 +169,13 @@ def tile_list_fraud_residual_queue_kernel(
         def staged(slot, width=PACK * KP, dtype=BF16):
             return held.tile([P, width], dtype, name="staged%d" % slot, align_bytes=64)
 
-        w1_q = {(a, b): quantised("w1_%d_%d" % (a, b)) for b in range(BLOCKS) for a in range(PASSES)}
+        def last_stage(name, width, dtype, place=0):
+            return over.tile([P, width], dtype, name=name, offset=STAGE_AT + 4 * S * place, align_bytes=64)
+
+        w1_q = {(a, b): quantised("w1_%d_%d" % (a, b)) for a, b in ((0, 0), (1, 0), (2, 0), (2, 1))}
         wf_q = [quantised("wf_%d" % b) for b in range(BLOCKS)]
-        z_q = {(b, q): quantised("z_%d_%d" % (b, q), QUARTER) for b in range(BLOCKS) for q in range(4)}
+        z_first = quantised("z_first", T2)
+        z_q = {(1, q): quantised("z_last%d" % q, QUARTER) for q in range(4)}
 
         gather(0, keep([P, S], U32, "v_words0"))
         w4_codes = [keep([P, PASSES * 2 * KP], U8, "w4_codes%d" % b) for b in range(BLOCKS)]
@@ -274,7 +279,8 @@ def tile_list_fraud_residual_queue_kernel(
                 pairs.append(pair)
             return pairs
 
-        def turn_back(q, pairs, z):
+        def turn_back(q, pairs, whole):
+            z = whole[:, q * 2 * BANK : (q + 1) * 2 * BANK]
             acc = bank(q)
             for u in range(2):
                 words = pairs[u][q][:].bitcast(F32)
@@ -282,8 +288,7 @@ def tile_list_fraud_residual_queue_kernel(
                     nc.tensor.transpose(
                         acc[:, (2 * u + mb) * P : (2 * u + mb + 1) * P], words[:, mb * P : (mb + 1) * P], identity[:]
                     )
-            nc.scalar.copy(z[:].bitcast(F32).rearrange("p (m u) -> p m u", u=2), acc[:].rearrange("p (u m) -> p m u", u=2))
-            quantise(z_q[0, q], 0, z[:])
+            nc.scalar.copy(z.bitcast(F32).rearrange("p (m u) -> p m u", u=2), acc[:].rearrange("p (u m) -> p m u", u=2))
 
         def add_turned_row(i, rows):
             pairs = []
@@ -331,11 +336,17 @@ def tile_list_fraud_residual_queue_kernel(
         scatter(pages[0], h[0])
         h[1] = residual(1)
         scatter(pages[1], h[1])
-        for a in range(PASSES):
-            quantise(w1_q[a, 1], 0, cast(nc.scalar.copy, w1_raw[a, 1], 0, PACK, staged(4 + a))[:])
-        h[2] = residual(2, staged(5, S, F32))
+        two = staged(5, 2 * PACK * KP)
+        for a in range(2):
+            cast(nc.scalar.copy, w1_raw[a, 1], 0, PACK, two[:, a * PACK * KP : (a + 1) * PACK * KP])
+        both = quantised("w1_two", 2 * KP)
+        quantise(both, 0, two[:])
+        for a in range(2):
+            w1_q[a, 1] = tuple(t[:, a * KP : (a + 1) * KP] for t in both)
+        quantise(w1_q[2, 1], 0, cast(nc.scalar.copy, w1_raw[2, 1], 0, PACK, last_stage("w1_last", PACK * KP, BF16))[:])
+        h[2] = residual(2, last_stage("h2", S, F32, 0))
+        h[3] = residual(3, last_stage("h3", S, F32, 1))
         scatter(pages[2], h[2])
-        h[3] = residual(3, staged(6, S, F32))
         for k in range(PACK, TILES):
             enc[k] = encode(k)
         pairs0 = [add_turned(0, 0, (4, 5, 6, 7), pair_tile)]
@@ -345,28 +356,34 @@ def tile_list_fraud_residual_queue_kernel(
         h[4] = residual(4)
         h[5] = residual(5)
         for b in range(BLOCKS):
-            quantise(wf_q[b], 0, cast(nc.scalar.copy, wf_raw[b], 0, PACK, slot(4, [P, PACK * KP], BF16) if b == 0 else staged(5))[:])
+            quantise(wf_q[b], 0, cast(nc.scalar.copy, wf_raw[b], 0, PACK, slot(4, [P, PACK * KP], BF16) if b == 0 else last_stage("wf_last", PACK * KP, BF16))[:])
         pairs0.append(add_turned(0, 1, (0, 1, 2, 3), pair_after_wf))
         scatter(pages[0], h[4])
         h[6] = residual(6)
         scatter(pages[1], h[5])
+        h[7] = residual(7)
+        z_whole = staged(10, PACK * T2)
         for q in range(4):
-            turn_back(q, pairs0, staged(10 + q, 2 * BANK))
-        h[7] = residual(7, staged(13, S, F32))
+            turn_back(q, pairs0, z_whole)
+        quantise(z_first, 0, z_whole[:])
         rows = keep([P, PACK, T2], BF16, "z_rows")
         add_turned_row(0, rows)
         add_turned_row(1, rows)
         scatter(pages[2], h[6])
         add_turned_row(2, rows)
-        scatter(pages[3], h[7])
+        scatter(pages[1], h[7])
 
         def score(acc, b, q, c):
+            if b == 0:
+                codes, plane = (t[:, q * QUARTER : (q + 1) * QUARTER] for t in z_first)
+            else:
+                codes, plane = (t[:] for t in z_q[1, q])
             nc.tensor.matmul_mx(
                 out=acc[:, (c % 2) * QUARTER : (c % 2 + 1) * QUARTER],
                 lhsT=wf_q[b][0][:, c * P : (c + 1) * P].bitcast(FP8X4),
                 lhsT_scale=wf_q[b][1][:, c * P : (c + 1) * P],
-                rhs=z_q[b, q][0][:].bitcast(FP8X4),
-                rhs_scale=z_q[b, q][1][:],
+                rhs=codes.bitcast(FP8X4),
+                rhs_scale=plane,
                 start=(b == 0 and c % 2 == 0),
                 stop=(b == BLOCKS - 1 and c % 2 == 1),
             )
@@ -398,7 +415,7 @@ def tile_list_fraud_residual_queue_kernel(
 
         for q in range(4):
             cols = slice(q * QUARTER, (q + 1) * QUARTER)
-            nc.vector.tensor_tensor(rows[:, 3, cols], pages[3][:, cols], queue_sb[1, 1][:, 1, cols], ALU.add)
+            nc.vector.tensor_tensor(rows[:, 3, cols], pages[1][:, cols], queue_sb[1, 1][:, 1, cols], ALU.add)
             z = ring.tile([P, PACK * QUARTER], BF16, name="woven", bufs=4, align_bytes=64)
             (nc.scalar.copy if q == 1 else nc.vector.tensor_copy)(
                 z[:].rearrange("p (c e i) -> p c i e", e=4, i=PACK),

@@ -29,8 +29,8 @@ PLANE_ROWS = 100
 PACKED_FROM = 32 - 4 * PASSES
 ENCODE_BANK = (2, 3, 4, 0, 4, 5, 6, 7)
 LINEAR_BANK = (0, 1, 2, 3, 4, 5, 6, 7)
-ROW_BANKS = ((4, 5, 0), (2, 3, 1), (4, 5, 2))
-SCORE_BANKS = ((6, 7), (0, 1), (3, 4), (5, 2))
+ROW_BANKS = (((4, 5), (0,)), ((2, 3), (1,)), ((4, 5, 6, 7), (2, 3)))
+SCORE_BANKS = ((4, 5), (6, 7), (2, 3), (0, 1))
 SLOT = 8192
 STAGE_AT = 2 * T + 3 * SLOT
 OVER_AT = {"wf1": 2 * T, "w1_20": 2 * T + SLOT, "w1_21": 2 * T + 2 * SLOT}
@@ -291,34 +291,38 @@ def tile_list_fraud_residual_queue_kernel(
             nc.scalar.copy(z.bitcast(F32).rearrange("p (m u) -> p m u", u=2), acc[:].rearrange("p (u m) -> p m u", u=2))
 
         def add_turned_row(i, rows):
-            pairs = []
-            for half in range(2):
-                acc = bank(ROW_BANKS[i][half])
+            sum_banks, back_banks = ROW_BANKS[i]
+            words = []
+            groups = 4 // len(sum_banks)
+            for part, number in enumerate(sum_banks):
+                acc = bank(number)
+                blocks = range(2 * groups * part, 2 * groups * (part + 1))
                 for step in range(2):
-                    for mb in range(4):
-                        cols = slice((4 * half + mb) * P, (4 * half + mb + 1) * P)
+                    for mb in blocks:
+                        cols = slice(mb * P, (mb + 1) * P)
                         nc.tensor.matmul(
-                            acc[:, mb * P : (mb + 1) * P],
+                            acc[:, (mb - blocks[0]) * P : (mb - blocks[0] + 1) * P],
                             lhsT=queue_sb[1, i // 2][:, i % 2, cols] if step == 0 else pages[i][:, cols],
                             rhs=identity[:],
                             is_transpose=True,
-                            start=(step == 0 and mb == 0),
-                            stop=(step == 1 and mb == 3),
+                            start=(step == 0 and mb == blocks[0]),
+                            stop=(step == 1 and mb == blocks[-1]),
                         )
-                pair = pair_tile(half)
+                pair = pair_tile(part)
                 nc.scalar.copy(
-                    pair[:].rearrange("m (g p e) -> m g p e", g=2, e=2),
-                    acc[:].rearrange("m (g e p) -> m g p e", g=2, e=2),
+                    pair[:, 0 : groups * 2 * P].rearrange("m (g p e) -> m g p e", g=groups, e=2),
+                    acc[:, 0 : groups * 2 * P].rearrange("m (g e p) -> m g p e", g=groups, e=2),
                 )
-                pairs.append(pair)
-            acc = bank(ROW_BANKS[i][2])
-            for g in range(4):
-                words = pairs[g // 2][:].bitcast(F32)
-                nc.tensor.transpose(acc[:, g * P : (g + 1) * P], words[:, (g % 2) * P : (g % 2 + 1) * P], identity[:])
-            nc.scalar.copy(
-                rows[:, i, :].rearrange("p (g e m) -> p g e m", g=4, e=2),
-                acc[:].bitcast(BF16).rearrange("p (g m e) -> p g e m", g=4, e=2),
-            )
+                words.extend(pair[:].bitcast(F32)[:, g * P : (g + 1) * P] for g in range(groups))
+            groups = 4 // len(back_banks)
+            for part, number in enumerate(back_banks):
+                acc = bank(number)
+                for g in range(groups):
+                    nc.tensor.transpose(acc[:, g * P : (g + 1) * P], words[groups * part + g], identity[:])
+                nc.scalar.copy(
+                    rows[:, i, part * groups * 2 * P : (part + 1) * groups * 2 * P].rearrange("p (g e m) -> p g e m", g=groups, e=2),
+                    acc[:, 0 : groups * P].bitcast(BF16).rearrange("p (g m e) -> p g e m", g=groups, e=2),
+                )
 
         lin = {}
         enc = {0: encode(0)}

@@ -27,14 +27,14 @@ BANK = 512
 QUARTER = T2 // 4
 PLANE_ROWS = 100
 PACKED_FROM = 32 - 4 * PASSES
-ENCODE_BANK = (2, 3, 4, 0, 4, 5, 6, 7)
-LINEAR_BANK = (0, 1, 2, 3, 4, 5, 6, 7)
-ROW_BANKS = (((4, 5), (0,)), ((2, 3), (1,)), ((4, 5, 6, 7), (2, 3)))
-SCORE_BANKS = ((4, 5), (6, 7), (2, 3), (0, 1))
+ENCODE_BANK = (2, 3, 4, 5, 4, 5, 6, 7)
+LINEAR_BANK = (0, 1, 2, 3, 0, 1, 6, 7)
+ROW_BANKS = (((0, 1), (2,)), ((4, 5), (3,)), ((0, 1, 6, 7), (4, 5)))
+SCORE_BANKS = ((0, 1), (6, 7), (4, 5), (2, 3))
 SLOT = 8192
 STAGE_AT = 2 * T + 3 * SLOT
 OVER_AT = {"wf1": 2 * T, "w1_20": 2 * T + SLOT, "w1_21": 2 * T + 2 * SLOT}
-TANH_AT = {1: ("w1_20", 0), 2: ("w1_20", 1), 4: ("w1_21", 0), 5: ("w1_21", 1), 6: ("w1_21", 2), 7: ("w1_21", 3)}
+TANH_AT = {1: ("w1_20", 0), 2: ("w1_20", 1), 3: ("w1_20", 2), 4: ("w1_21", 0), 5: ("w1_21", 1), 6: ("w1_21", 2), 7: ("w1_21", 3)}
 
 
 def tile_list_fraud_residual_queue_kernel(
@@ -281,7 +281,7 @@ def tile_list_fraud_residual_queue_kernel(
 
         def turn_back(q, pairs, whole):
             z = whole[:, q * 2 * BANK : (q + 1) * 2 * BANK]
-            acc = bank(q)
+            acc = bank(2 + q)
             for u in range(2):
                 words = pairs[u][q][:].bitcast(F32)
                 for mb in range(2):
@@ -334,9 +334,9 @@ def tile_list_fraud_residual_queue_kernel(
         quantise(w1_q[2, 0], 2 * P, cast(nc.scalar.copy, w1_raw[2, 0], 2, PACK, staged(0, 2 * KP))[:])
         enc[1] = encode(1)
         enc[2] = encode(2)
+        enc[3] = encode(3)
         lin[2] = linear(2)
         lin[3] = linear(3)
-        enc[3] = encode(3)
         scatter(pages[0], h[0])
         h[1] = residual(1)
         scatter(pages[1], h[1])
@@ -353,15 +353,17 @@ def tile_list_fraud_residual_queue_kernel(
         scatter(pages[2], h[2])
         for k in range(PACK, TILES):
             enc[k] = encode(k)
+        lin[4] = linear(4)
+        lin[5] = linear(5)
         pairs0 = [add_turned(0, 0, (4, 5, 6, 7), pair_tile)]
-        for k in range(PACK, TILES):
-            lin[k] = linear(k)
+        lin[6] = linear(6)
+        lin[7] = linear(7)
         scatter(pages[3], h[3])
         h[4] = residual(4)
         h[5] = residual(5)
         for b in range(BLOCKS):
             quantise(wf_q[b], 0, cast(nc.scalar.copy, wf_raw[b], 0, PACK, slot(4, [P, PACK * KP], BF16) if b == 0 else last_stage("wf_last", PACK * KP, BF16))[:])
-        pairs0.append(add_turned(0, 1, (0, 1, 2, 3), pair_after_wf))
+        pairs0.append(add_turned(0, 1, (2, 3, 4, 5), pair_after_wf))
         scatter(pages[0], h[4])
         h[6] = residual(6)
         scatter(pages[1], h[5])

@@ -201,7 +201,8 @@ def tile_list_fraud_residual_queue_kernel(
         def encode(k):
             b, i = divmod(k, PACK)
             acc = bank(ENCODE_BANK[k])
-            for a in range(PASSES):
+            order = (2, 0, 1) if 0 < k < PACK else (0, 1, 2)
+            for a in order:
                 c0 = a * KP + i * P
                 nc.tensor.matmul_mx(
                     out=acc[:],
@@ -209,8 +210,8 @@ def tile_list_fraud_residual_queue_kernel(
                     lhsT_scale=w4_planes[:, c0 + (a + b) * KP : c0 + (a + b) * KP + P],
                     rhs=v_words[a][:].bitcast(FP8X4),
                     rhs_scale=v_planes[a][:],
-                    start=(a == 0),
-                    stop=(a == PASSES - 1),
+                    start=(a == order[0]),
+                    stop=(a == order[-1]),
                 )
             if k in TANH_AT:
                 over_at, place = TANH_AT[k]
@@ -362,7 +363,7 @@ def tile_list_fraud_residual_queue_kernel(
         h[4] = residual(4)
         h[5] = residual(5)
         for b in range(BLOCKS):
-            quantise(wf_q[b], 0, cast(nc.scalar.copy, wf_raw[b], 0, PACK, slot(4, [P, PACK * KP], BF16) if b == 0 else last_stage("wf_last", PACK * KP, BF16))[:])
+            quantise(wf_q[b], 0, cast(nc.scalar.copy, wf_raw[b], 0, PACK, slot(4, [P, PACK * KP], BF16) if b == 0 else staged(5))[:])
         pairs0.append(add_turned(0, 1, (2, 3, 4, 5), pair_after_wf))
         scatter(pages[0], h[4])
         h[6] = residual(6)

@@ -105,12 +105,12 @@ def tile_list_fraud_residual_queue_kernel(
                 in_=tab_scales[:, 4 * q : 4 * q + 4, :].bitcast(I32),
             )
         w1_raw = {(0, 0): load_weight(1, w1, 0, 0)}
-        table.append(load_table(2, 1))
         for q in range(4):
             nc.sync.dma_start(
                 out=w4_planes_raw[32 * q : 32 * q + 4, :].bitcast(I32).rearrange("r (a c) -> r a c", a=PASSES),
                 in_=w4_scales[:, 4 * q : 4 * q + 4, :].bitcast(I32).rearrange("a r c -> r a c"),
             )
+        table.append(load_table(2, 1))
         table.append(load_table(3, 2))
         picked_planes = keep([P, S], U8, "picked_planes")
         nc.vector.tensor_copy(picked_planes[:], tab_planes[:].indirect(picks[:]))
@@ -188,15 +188,16 @@ def tile_list_fraud_residual_queue_kernel(
             )
 
         order_words(0)
-        gather(1, after_planes(0, "v_words1"))
         nc.vector.tensor_copy(
             w4_planes[:].rearrange("p (g t m) -> p g t m", t=PACK, m=P),
             w4_planes_raw[:].rearrange("p (g m t) -> p g t m", t=PACK, m=P),
         )
+        gather(1, after_planes(0, "v_words1"))
         w1_q[0, 0] = (after_planes(1, "w1_first_codes"), w1_q[0, 0][1])
         quantise(w1_q[0, 0], 0, cast(nc.scalar.copy, w1_raw[0, 0], 0, PACK, staged(0))[:])
         gather(2, slot(2, [P, S], U32))
-        quantise(w1_q[1, 0], 0, cast(nc.vector.tensor_copy, w1_raw[1, 0], 0, PACK, slot(3, [P, PACK * KP], BF16))[:])
+        quantise(w1_q[1, 0], 0, cast(nc.vector.tensor_copy, w1_raw[1, 0], 0, 2, slot(3, [P, 2 * KP], BF16))[:])
+        quantise(w1_q[1, 0], 2 * P, cast(nc.scalar.copy, w1_raw[1, 0], 2, PACK, staged(0, 2 * KP))[:])
 
         def encode(k):
             b, i = divmod(k, PACK)

@@ -24,17 +24,25 @@ PASSES = K // KP
 BLOCKS = H // KP
 TILES = BLOCKS * PACK
 BANK = 512
-QUARTER = T2 // 4
-PLANE_ROWS = 100
-PACKED_FROM = 32 - 4 * PASSES
+QUADRANT = 32
+QUADRANTS = P // QUADRANT
+QUARTERS = 4
+QUARTER = T2 // QUARTERS
+PLANE_ROWS = 3 * QUADRANT + 4
+PACKED_FROM = QUADRANT - 4 * PASSES
+
 ENCODE_BANK = (2, 3, 4, 5, 4, 5, 6, 7)
 LINEAR_BANK = (0, 1, 2, 3, 0, 1, 6, 7)
-ROW_BANKS = (((0, 1), (2,)), ((4, 5), (3,)), ((0, 1, 6, 7), (4, 5)))
+PAIR_BANKS = ((4, 5, 6, 7), (2, 3, 4, 5))
+ROW_BANKS = (((0, 1), (2,)), ((4, 5), (0, 1, 6, 7)), ((0, 1, 6, 7), (4, 5, 2, 3)))
 SCORE_BANKS = ((0, 1), (6, 7), (4, 5), (2, 3))
-SLOT = 8192
-STAGE_AT = 2 * T + 3 * SLOT
-OVER_AT = {"wf1": 2 * T, "w1_20": 2 * T + SLOT, "w1_21": 2 * T + 2 * SLOT}
-TANH_AT = {1: ("w1_20", 0), 2: ("w1_20", 1), 3: ("w1_20", 2), 4: ("w1_21", 0), 5: ("w1_21", 1), 6: ("w1_21", 2), 7: ("w1_21", 3)}
+
+SLOT = 4 * PACK * KP
+ROW = 4 * S
+PLANES_AT = 0
+WF_LAST_AT = 2 * ROW
+W1_LAST_AT = (WF_LAST_AT + SLOT, WF_LAST_AT + 2 * SLOT)
+STAGE_AT = WF_LAST_AT + 3 * SLOT
 
 
 def tile_list_fraud_residual_queue_kernel(
@@ -50,42 +58,43 @@ def tile_list_fraud_residual_queue_kernel(
         def keep(shape, dtype, name):
             return held.tile(shape, dtype, name=name, align_bytes=64)
 
-        def bank(number):
-            return psum.tile([P, BANK], F32, name="bank%d" % number)
-
         def slot(number, shape, dtype):
             return keep(shape, dtype, "slot%d" % number)
 
-        def load_big(number, shape, dtype, source):
-            if number in OVER_AT:
-                t = over.tile(shape, dtype, name=number, offset=OVER_AT[number], align_bytes=64)
-            else:
-                t = slot(number, shape, dtype)
-            nc.sync.dma_start(out=t[:], in_=source)
-            return t
+        def placed(name, offset, shape, dtype):
+            return over.tile(shape, dtype, name=name, offset=offset, align_bytes=64)
+
+        def bank(number):
+            return psum.tile([P, BANK], F32, name="bank%d" % number)
+
+        def load(tile, source):
+            nc.sync.dma_start(out=tile[:], in_=source)
+            return tile
 
         def load_table(number, a):
-            return load_big(number, [P, T], I32, tab_words[a].rearrange("p t i -> p (t i)").bitcast(I32))
+            return load(slot(number, [P, T], I32), tab_words[a].rearrange("p t i -> p (t i)").bitcast(I32))
 
-        def load_weight(number, w, a, b):
+        weight_shape = [P, PACK, KP]
+
+        def load_weight(tile, w, a, b):
             rows = w[a * KP : (a + 1) * KP, b * KP : (b + 1) * KP]
-            return load_big(number, [P, PACK, KP], F32, rows.rearrange("(p j) c -> p j c", j=PACK))
+            return load(tile, rows.rearrange("(p j) c -> p j c", j=PACK))
 
         def load_w4(b):
-            t = keep([P, PASSES, 2 * KP], U8, "w4_raw%d" % b)
+            tile = keep([P, PASSES, 2 * KP], U8, "w4_raw%d" % b)
             words = w4_words[:, :, b * 2 * KP : (b + 1) * 2 * KP].rearrange("a p n -> p a n")
-            nc.sync.dma_start(out=t[:].bitcast(I32), in_=words.bitcast(I32))
-            return t
+            nc.sync.dma_start(out=tile[:].bitcast(I32), in_=words.bitcast(I32))
+            return tile
 
         def load_queue(number, b, u):
             rows = queue[b * KP : (b + 1) * KP, :].rearrange("(p i) m -> p i m", i=PACK)
-            return load_big(number, [P, 2, T2], F32, rows[:, 2 * u : 2 * u + 2, :])
+            return load(slot(number, [P, 2, T2], F32), rows[:, 2 * u : 2 * u + 2, :])
 
         w4_planes_raw = keep([P, PASSES * H], U8, "w4_planes_raw")
         nc.gpsimd.memset(w4_planes_raw[:].bitcast(I32), 0)
-        tab_planes = over.tile([P, T], U8, name="tab_planes", offset=T // 2, align_bytes=64)
-        for q in range(4):
-            nc.vector.memset(tab_planes[32 * q : 32 * q + PACKED_FROM, :].bitcast(I32), 0)
+        tab_planes = placed("tab_planes", PLANES_AT + ROW // 2, [P, T], U8)
+        for q in range(QUADRANTS):
+            nc.vector.memset(tab_planes[QUADRANT * q : QUADRANT * q + PACKED_FROM, :].bitcast(I32), 0)
         v_planes = [keep([P, S], U8, "v_plane%d" % a) for a in range(PASSES)]
         for plane in v_planes:
             nc.vector.memset(plane[:].bitcast(I32), 0)
@@ -99,19 +108,20 @@ def tile_list_fraud_residual_queue_kernel(
         picks = held.tile([P, S // 16], U16, name="picks")
         nc.sync.dma_start(picks[:], offs)
         w4_raw = [load_w4(0)]
-        for q in range(4):
+        for q in range(QUADRANTS):
             nc.sync.dma_start(
-                out=tab_planes[32 * q + PACKED_FROM : 32 * (q + 1), :].bitcast(I32),
+                out=tab_planes[QUADRANT * q + PACKED_FROM : QUADRANT * (q + 1), :].bitcast(I32),
                 in_=tab_scales[:, 4 * q : 4 * q + 4, :].bitcast(I32),
             )
-        w1_raw = {(0, 0): load_weight(1, w1, 0, 0)}
-        for q in range(4):
+        w1_raw = {(0, 0): load_weight(slot(1, weight_shape, F32), w1, 0, 0)}
+        for q in range(QUADRANTS):
             nc.sync.dma_start(
-                out=w4_planes_raw[32 * q : 32 * q + 4, :].bitcast(I32).rearrange("r (a c) -> r a c", a=PASSES),
+                out=w4_planes_raw[QUADRANT * q : QUADRANT * q + 4, :].bitcast(I32).rearrange("r (a c) -> r a c", a=PASSES),
                 in_=w4_scales[:, 4 * q : 4 * q + 4, :].bitcast(I32).rearrange("a r c -> r a c"),
             )
         table.append(load_table(2, 1))
         table.append(load_table(3, 2))
+
         picked_planes = keep([P, S], U8, "picked_planes")
         nc.vector.tensor_copy(picked_planes[:], tab_planes[:].indirect(picks[:]))
 
@@ -124,27 +134,26 @@ def tile_list_fraud_residual_queue_kernel(
 
         move_plane(0)
         move_plane(1)
-        w1_raw[1, 0] = load_weight(4, w1, 1, 0)
+        w1_raw[1, 0] = load_weight(slot(4, weight_shape, F32), w1, 1, 0)
         move_plane(2)
-        w1_raw[2, 0] = load_weight("w1_20", w1, 2, 0)
+        w1_raw[2, 0] = load_weight(placed("w1_last0", W1_LAST_AT[0], weight_shape, F32), w1, 2, 0)
         w4_raw.append(load_w4(1))
-        dec_sb = keep([P, BLOCKS, PACK], F32, "dec_sb")
-        nc.sync.dma_start(out=dec_sb[:], in_=dec.rearrange("(b p i) -> p b i", b=BLOCKS, i=PACK))
+        dec_sb = load(keep([P, BLOCKS, PACK], F32, "dec_sb"), dec.rearrange("(b p i) -> p b i", b=BLOCKS, i=PACK))
         places = held.tile([P, S // 16], U16, name="places")
         nc.sync.dma_start(places[:], offs2)
-        wgs_sb = keep([P, S], F32, "wgs_sb")
-        nc.sync.dma_start(out=wgs_sb[:], in_=wgs)
-        for a in range(PASSES):
-            w1_raw[a, 1] = load_weight((6, 7, "w1_21")[a], w1, a, 1)
-        queue_sb = {(0, 0): load_queue(4, 0, 0), (0, 1): load_queue(0, 0, 1)}
-        wf_raw = [load_weight((5, "wf1")[b], wf, b, 0) for b in range(BLOCKS)]
-        for number, b, u in ((1, 1, 0), (6, 1, 1)):
-            queue_sb[b, u] = load_queue(number, b, u)
-        bias_sb = keep([P, PACK], F32, "bias_sb")
-        nc.sync.dma_start(out=bias_sb[:], in_=bf.rearrange("(p c) -> p c", c=PACK))
-
-        def after_planes(place, name):
-            return over.tile([P, S], U32, name=name, offset=T * place, align_bytes=64)
+        wgs_sb = load(keep([P, S], F32, "wgs_sb"), wgs)
+        w1_raw[0, 1] = load_weight(slot(6, weight_shape, F32), w1, 0, 1)
+        w1_raw[1, 1] = load_weight(slot(7, weight_shape, F32), w1, 1, 1)
+        w1_raw[2, 1] = load_weight(placed("w1_last1", W1_LAST_AT[1], weight_shape, F32), w1, 2, 1)
+        queue_sb = {(0, 0): load_queue(4, 0, 0)}
+        wf_raw = [
+            load_weight(slot(5, weight_shape, F32), wf, 0, 0),
+            load_weight(placed("wf_last", WF_LAST_AT, weight_shape, F32), wf, 1, 0),
+        ]
+        queue_sb[0, 1] = load_queue(0, 0, 1)
+        queue_sb[1, 0] = load_queue(1, 1, 0)
+        queue_sb[1, 1] = load_queue(6, 1, 1)
+        bias_sb = load(keep([P, PACK], F32, "bias_sb"), bf.rearrange("(p c) -> p c", c=PACK))
 
         v_words = {}
 
@@ -152,7 +161,7 @@ def tile_list_fraud_residual_queue_kernel(
             v_words[a] = tile
             nc.vector.tensor_copy(tile[:], table[a][:].bitcast(U32).indirect(picks[:]))
 
-        def quantised(name, width=KP):
+        def operand(name, width=KP):
             return keep([P, width], U32, name + "_codes"), keep([P, width], U8, name + "_plane")
 
         def cast(copy, raw, t0, t1, tile):
@@ -162,24 +171,26 @@ def tile_list_fraud_residual_queue_kernel(
                 copy(dst[:, :, :, t - t0 : t - t0 + 2], src[:, :, :, t : t + 2])
             return tile
 
-        def quantise(operand, c0, ap):
-            c1 = c0 + ap.shape[1] // PACK
-            nc.vector.quantize_mx(out=operand[0][:, c0:c1].bitcast(FP8X4), scales=operand[1][:, c0:c1], in_=ap)
+        def quantise(target, c0, values):
+            c1 = c0 + values.shape[1] // PACK
+            nc.vector.quantize_mx(out=target[0][:, c0:c1].bitcast(FP8X4), scales=target[1][:, c0:c1], in_=values)
 
-        def staged(slot, width=PACK * KP, dtype=BF16):
-            return held.tile([P, width], dtype, name="staged%d" % slot, align_bytes=64)
+        def staging(name, width=PACK * KP):
+            return keep([P, width], BF16, name)
 
-        def last_stage(name, width, dtype, place=0):
-            return over.tile([P, width], dtype, name=name, offset=STAGE_AT + 4 * S * place, align_bytes=64)
-
-        w1_q = {(a, b): quantised("w1_%d_%d" % (a, b)) for a, b in ((0, 0), (1, 0), (2, 0), (2, 1))}
-        wf_q = [quantised("wf_%d" % b) for b in range(BLOCKS)]
-        z_first = quantised("z_first", T2)
-        z_q = {(1, q): quantised("z_last%d" % q, QUARTER) for q in range(4)}
+        w1_q = {
+            (0, 0): (placed("w1_first_codes", PLANES_AT + ROW, [P, KP], U32), keep([P, KP], U8, "w1_first_plane")),
+            (1, 0): operand("w1_1_0"),
+            (2, 0): operand("w1_2_0"),
+            (2, 1): operand("w1_2_1"),
+        }
+        wf_q = [operand("wf_%d" % b) for b in range(BLOCKS)]
+        z_first = operand("z_first", T2)
+        z_last = [operand("z_last%d" % q, QUARTER) for q in range(QUARTERS)]
 
         gather(0, keep([P, S], U32, "v_words0"))
         w4_codes = [keep([P, PASSES * 2 * KP], U8, "w4_codes%d" % b) for b in range(BLOCKS)]
-        w4_planes = keep([P, BLOCKS * PASSES * KP], U8, "w4_planes")
+        w4_planes = keep([P, PASSES * H], U8, "w4_planes")
 
         def order_words(b):
             nc.vector.tensor_copy(
@@ -192,40 +203,51 @@ def tile_list_fraud_residual_queue_kernel(
             w4_planes[:].rearrange("p (g t m) -> p g t m", t=PACK, m=P),
             w4_planes_raw[:].rearrange("p (g m t) -> p g t m", t=PACK, m=P),
         )
-        gather(1, after_planes(0, "v_words1"))
-        w1_q[0, 0] = (after_planes(1, "w1_first_codes"), w1_q[0, 0][1])
-        quantise(w1_q[0, 0], 0, cast(nc.scalar.copy, w1_raw[0, 0], 0, PACK, staged(0))[:])
+
+        gather(1, placed("v_words1", PLANES_AT, [P, S], U32))
+        quantise(w1_q[0, 0], 0, cast(nc.scalar.copy, w1_raw[0, 0], 0, PACK, staging("head_stage"))[:])
         gather(2, slot(2, [P, S], U32))
-        quantise(w1_q[1, 0], 0, cast(nc.vector.tensor_copy, w1_raw[1, 0], 0, 2, slot(3, [P, 2 * KP], BF16))[:])
-        quantise(w1_q[1, 0], 2 * P, cast(nc.scalar.copy, w1_raw[1, 0], 2, PACK, staged(0, 2 * KP))[:])
+
+        def quantise_first_half(a):
+            quantise(w1_q[a, 0], 0, cast(nc.vector.tensor_copy, w1_raw[a, 0], 0, 2, slot(3, [P, 2 * KP], BF16))[:])
+
+        def quantise_second_half(a):
+            quantise(w1_q[a, 0], 2 * P, cast(nc.scalar.copy, w1_raw[a, 0], 2, PACK, staging("head_stage", 2 * KP))[:])
+
+        quantise_first_half(1)
+        quantise_second_half(1)
+
+        def pass_order(k):
+            return (2, 0, 1) if 0 < k < PACK else (0, 1, 2)
 
         def encode(k):
             b, i = divmod(k, PACK)
             acc = bank(ENCODE_BANK[k])
-            order = (2, 0, 1) if 0 < k < PACK else (0, 1, 2)
+            order = pass_order(k)
             for a in order:
-                c0 = a * KP + i * P
+                word0 = a * KP + i * P
+                byte0 = a * H + b * KP + i * P
                 nc.tensor.matmul_mx(
                     out=acc[:],
-                    lhsT=w4_codes[b][:, 2 * c0 : 2 * (c0 + P)].bitcast(FP4X4),
-                    lhsT_scale=w4_planes[:, c0 + (a + b) * KP : c0 + (a + b) * KP + P],
+                    lhsT=w4_codes[b][:, 2 * word0 : 2 * (word0 + P)].bitcast(FP4X4),
+                    lhsT_scale=w4_planes[:, byte0 : byte0 + P],
                     rhs=v_words[a][:].bitcast(FP8X4),
                     rhs_scale=v_planes[a][:],
                     start=(a == order[0]),
                     stop=(a == order[-1]),
                 )
-            if k in TANH_AT:
-                over_at, place = TANH_AT[k]
-                minus_enc = over.tile([P, S], F32, name="minus_enc%d" % k, offset=OVER_AT[over_at] + 4 * S * place, align_bytes=64)
+            if k == 0:
+                result = ring.tile([P, S], F32, name="minus_enc")
             else:
-                minus_enc = ring.tile([P, S], F32, name="minus_enc")
-            nc.scalar.activation(minus_enc[:], acc[:], ACT.Tanh, scale=-1.0)
-            return minus_enc
+                place = i - 1 if b == 0 else i
+                result = placed("minus_enc%d" % k, W1_LAST_AT[b] + ROW * place, [P, S], F32)
+            nc.scalar.activation(result[:], acc[:], ACT.Tanh, scale=-1.0)
+            return result
 
         def linear(k):
             b, i = divmod(k, PACK)
             acc = bank(LINEAR_BANK[k])
-            order = (2, 0, 1) if 0 < k < PACK else (0, 1, 2)
+            order = pass_order(k)
             for a in order:
                 codes, plane = w1_q[a, b]
                 nc.tensor.matmul_mx(
@@ -239,199 +261,182 @@ def tile_list_fraud_residual_queue_kernel(
                 )
             return acc
 
-        def residual(k, h=None):
+        def residual(k, tile):
             b, i = divmod(k, PACK)
-            acc = lin[k]
-            if h is None:
-                h = ring.tile([P, S], F32, name="h", bufs=3)
-            nc.vector.scalar_tensor_tensor(h[:], enc[k][:], dec_sb[:, b, i : i + 1], acc[:], ALU.mult, ALU.add)
-            return h
+            nc.vector.scalar_tensor_tensor(tile[:], minus_enc[k][:], dec_sb[:, b, i : i + 1], lin[k][:], ALU.mult, ALU.add)
+            return tile
 
-        def scatter(page, h):
-            nc.vector.tensor_tensor(page[:].indirect(places[:]), h[:], wgs_sb[:], ALU.mult)
+        def h_tile():
+            return ring.tile([P, S], F32, name="h", bufs=3)
 
-        def pair_tile(q):
-            return ring.tile([P, BANK], BF16, name="pair", bufs=4, align_bytes=64)
+        def scatter(page, values):
+            nc.vector.tensor_tensor(page[:].indirect(places[:]), values[:], wgs_sb[:], ALU.mult)
 
-        def pair_after_wf(q):
-            return over.tile([P, BANK], BF16, name="pair%d" % q, offset=OVER_AT["wf1"] + 2 * BANK * q, align_bytes=64)
+        def add_turned(acc, column, source, start, stop):
+            nc.tensor.matmul(
+                acc[:, column * P : (column + 1) * P], lhsT=source, rhs=identity[:], is_transpose=True, start=start, stop=stop
+            )
 
-        def add_turned(b, u, banks, make_pair):
-            pairs = []
-            for q in range(4):
-                acc = bank(banks[q])
+        def round_in_pairs(acc, groups, tile):
+            nc.scalar.copy(
+                tile[:, 0 : groups * 2 * P].rearrange("m (g p e) -> m g p e", g=groups, e=2),
+                acc[:, 0 : groups * 2 * P].rearrange("m (g e p) -> m g p e", g=groups, e=2),
+            )
+            return tile
+
+        def pair_tile():
+            return ring.tile([P, BANK], BF16, name="pair", bufs=QUARTERS, align_bytes=64)
+
+        def sum_pair(u, make_tile):
+            tiles = []
+            for q in range(QUARTERS):
+                acc = bank(PAIR_BANKS[u][q])
                 for step in range(2):
-                    for mb in range(2):
-                        cols = slice((2 * q + mb) * P, (2 * q + mb + 1) * P)
+                    for piece in range(2):
+                        cols = slice((2 * q + piece) * P, (2 * q + piece + 1) * P)
                         for e in range(2):
-                            source = queue_sb[b, u][:, e, cols] if step == 0 else pages[2 * u + e][:, cols]
-                            nc.tensor.matmul(
-                                acc[:, (2 * mb + e) * P : (2 * mb + e + 1) * P],
-                                lhsT=source,
-                                rhs=identity[:],
-                                is_transpose=True,
-                                start=(step == 0 and mb == 0 and e == 0),
-                                stop=(step == 1 and mb == 1 and e == 1),
-                            )
-                pair = make_pair(q)
-                nc.scalar.copy(
-                    pair[:].rearrange("m (g p e) -> m g p e", g=2, e=2),
-                    acc[:].rearrange("m (g e p) -> m g p e", g=2, e=2),
-                )
-                pairs.append(pair)
-            return pairs
+                            source = queue_sb[0, u][:, e, cols] if step == 0 else pages[2 * u + e][:, cols]
+                            add_turned(acc, 2 * piece + e, source, step + piece + e == 0, step + piece + e == 3)
+                tiles.append(round_in_pairs(acc, 2, make_tile(q)))
+            return tiles
 
-        def turn_back(q, pairs, whole):
-            z = whole[:, q * 2 * BANK : (q + 1) * 2 * BANK]
-            acc = bank(2 + q)
+        def turn_back(q, pairs, z):
+            acc = bank(PAIR_BANKS[1][q])
             for u in range(2):
                 words = pairs[u][q][:].bitcast(F32)
-                for mb in range(2):
-                    nc.tensor.transpose(
-                        acc[:, (2 * u + mb) * P : (2 * u + mb + 1) * P], words[:, mb * P : (mb + 1) * P], identity[:]
-                    )
-            nc.scalar.copy(z.bitcast(F32).rearrange("p (m u) -> p m u", u=2), acc[:].rearrange("p (u m) -> p m u", u=2))
+                for piece in range(2):
+                    column = 2 * u + piece
+                    nc.tensor.transpose(acc[:, column * P : (column + 1) * P], words[:, piece * P : (piece + 1) * P], identity[:])
+            target = z[:, q * PACK * QUARTER : (q + 1) * PACK * QUARTER]
+            nc.scalar.copy(target.bitcast(F32).rearrange("p (m u) -> p m u", u=2), acc[:].rearrange("p (u m) -> p m u", u=2))
 
-        def add_turned_row(i, rows):
+        def sum_row(i, rows):
             sum_banks, back_banks = ROW_BANKS[i]
             words = []
-            groups = 4 // len(sum_banks)
+            groups = QUARTERS // len(sum_banks)
             for part, number in enumerate(sum_banks):
                 acc = bank(number)
-                blocks = range(2 * groups * part, 2 * groups * (part + 1))
                 for step in range(2):
-                    for mb in blocks:
-                        cols = slice(mb * P, (mb + 1) * P)
-                        nc.tensor.matmul(
-                            acc[:, (mb - blocks[0]) * P : (mb - blocks[0] + 1) * P],
-                            lhsT=queue_sb[1, i // 2][:, i % 2, cols] if step == 0 else pages[i][:, cols],
-                            rhs=identity[:],
-                            is_transpose=True,
-                            start=(step == 0 and mb == blocks[0]),
-                            stop=(step == 1 and mb == blocks[-1]),
-                        )
-                pair = pair_tile(part)
-                nc.scalar.copy(
-                    pair[:, 0 : groups * 2 * P].rearrange("m (g p e) -> m g p e", g=groups, e=2),
-                    acc[:, 0 : groups * 2 * P].rearrange("m (g e p) -> m g p e", g=groups, e=2),
-                )
-                words.extend(pair[:].bitcast(F32)[:, g * P : (g + 1) * P] for g in range(groups))
-            groups = 4 // len(back_banks)
+                    for piece in range(2 * groups):
+                        first = (2 * groups * part + piece) * P
+                        cols = slice(first, first + P)
+                        source = queue_sb[1, i // 2][:, i % 2, cols] if step == 0 else pages[i][:, cols]
+                        add_turned(acc, piece, source, step == 0 and piece == 0, step == 1 and piece == 2 * groups - 1)
+                tile = round_in_pairs(acc, groups, pair_tile())
+                words.extend(tile[:].bitcast(F32)[:, g * P : (g + 1) * P] for g in range(groups))
+            groups = QUARTERS // len(back_banks)
             for part, number in enumerate(back_banks):
                 acc = bank(number)
                 for g in range(groups):
                     nc.tensor.transpose(acc[:, g * P : (g + 1) * P], words[groups * part + g], identity[:])
+                target = rows[:, i, part * groups * QUARTER : (part + 1) * groups * QUARTER]
                 nc.scalar.copy(
-                    rows[:, i, part * groups * 2 * P : (part + 1) * groups * 2 * P].rearrange("p (g e m) -> p g e m", g=groups, e=2),
+                    target.rearrange("p (g e m) -> p g e m", g=groups, e=2),
                     acc[:, 0 : groups * P].bitcast(BF16).rearrange("p (g m e) -> p g e m", g=groups, e=2),
                 )
 
-        lin = {}
-        enc = {0: encode(0)}
-        quantise(w1_q[2, 0], 0, cast(nc.vector.tensor_copy, w1_raw[2, 0], 0, 2, slot(3, [P, 2 * KP], BF16))[:])
-        lin[0] = linear(0)
-        lin[1] = linear(1)
+        minus_enc = {0: encode(0)}
+        quantise_first_half(2)
+        lin = {0: linear(0), 1: linear(1)}
         order_words(1)
-        h = {0: residual(0)}
-        quantise(w1_q[2, 0], 2 * P, cast(nc.scalar.copy, w1_raw[2, 0], 2, PACK, staged(0, 2 * KP))[:])
-        enc[1] = encode(1)
-        enc[2] = encode(2)
-        enc[3] = encode(3)
+        h = {0: residual(0, h_tile())}
+        quantise_second_half(2)
+        for k in range(1, PACK):
+            minus_enc[k] = encode(k)
         lin[2] = linear(2)
         lin[3] = linear(3)
         scatter(pages[0], h[0])
-        h[1] = residual(1)
+        h[1] = residual(1, h_tile())
         scatter(pages[1], h[1])
-        two = staged(5, 2 * PACK * KP)
+
+        two_passes = placed("w1_two_stage", STAGE_AT, [P, 2 * PACK * KP], BF16)
         for a in range(2):
-            cast(nc.scalar.copy, w1_raw[a, 1], 0, PACK, two[:, a * PACK * KP : (a + 1) * PACK * KP])
-        both = quantised("w1_two", 2 * KP)
-        quantise(both, 0, two[:])
+            cast(nc.scalar.copy, w1_raw[a, 1], 0, PACK, two_passes[:, a * PACK * KP : (a + 1) * PACK * KP])
+        two_q = operand("w1_two", 2 * KP)
+        quantise(two_q, 0, two_passes[:])
         for a in range(2):
-            w1_q[a, 1] = tuple(t[:, a * KP : (a + 1) * KP] for t in both)
-        quantise(w1_q[2, 1], 0, cast(nc.scalar.copy, w1_raw[2, 1], 0, PACK, last_stage("w1_last", PACK * KP, BF16))[:])
-        h[2] = residual(2, last_stage("h2", S, F32, 0))
-        h[3] = residual(3, last_stage("h3", S, F32, 1))
+            w1_q[a, 1] = tuple(part[:, a * KP : (a + 1) * KP] for part in two_q)
+        last_pass = cast(nc.scalar.copy, w1_raw[2, 1], 0, PACK, staging("late_stage"))
+        for k in (2, 3):
+            h[k] = residual(k, placed("h%d" % k, STAGE_AT + ROW * (k - 2), [P, S], F32))
         scatter(pages[2], h[2])
+        quantise(w1_q[2, 1], 0, last_pass[:])
         for k in range(PACK, TILES):
-            enc[k] = encode(k)
-        lin[4] = linear(4)
-        lin[5] = linear(5)
-        pairs0 = [add_turned(0, 0, (4, 5, 6, 7), pair_tile)]
-        lin[6] = linear(6)
-        lin[7] = linear(7)
+            minus_enc[k] = encode(k)
+        pairs = [sum_pair(0, lambda q: pair_tile())]
+        for k in range(PACK, TILES):
+            lin[k] = linear(k)
         scatter(pages[3], h[3])
-        h[4] = residual(4)
-        h[5] = residual(5)
-        for b in range(BLOCKS):
-            quantise(wf_q[b], 0, cast(nc.scalar.copy, wf_raw[b], 0, PACK, slot(4, [P, PACK * KP], BF16) if b == 0 else staged(5))[:])
-        pairs0.append(add_turned(0, 1, (2, 3, 4, 5), pair_after_wf))
+
+        h[4] = residual(4, h_tile())
+        h[5] = residual(5, h_tile())
+        quantise(wf_q[0], 0, cast(nc.scalar.copy, wf_raw[0], 0, PACK, slot(4, [P, PACK * KP], BF16))[:])
+        quantise(wf_q[1], 0, cast(nc.scalar.copy, wf_raw[1], 0, PACK, staging("late_stage"))[:])
+        pairs.append(sum_pair(1, lambda q: placed("pair%d" % q, WF_LAST_AT + 2 * BANK * q, [P, BANK], BF16)))
         scatter(pages[0], h[4])
-        h[6] = residual(6)
+        h[6] = residual(6, h_tile())
         scatter(pages[1], h[5])
-        h[7] = residual(7)
-        z_whole = staged(10, PACK * T2)
-        for q in range(4):
-            turn_back(q, pairs0, z_whole)
-        quantise(z_first, 0, z_whole[:])
+        h[7] = residual(7, h_tile())
+        z_block = staging("z_block", PACK * T2)
+        for q in range(QUARTERS):
+            turn_back(q, pairs, z_block)
+        quantise(z_first, 0, z_block[:])
         rows = keep([P, PACK, T2], BF16, "z_rows")
-        add_turned_row(0, rows)
-        add_turned_row(1, rows)
+        sum_row(0, rows)
+        sum_row(1, rows)
         scatter(pages[2], h[6])
-        add_turned_row(2, rows)
-        scatter(pages[1], h[7])
+        sum_row(2, rows)
+        last_page = pages[1]
+        scatter(last_page, h[7])
 
-        def score(acc, b, q, c):
+        def score(b, q):
             if b == 0:
-                codes, plane = (t[:, q * QUARTER : (q + 1) * QUARTER] for t in z_first)
+                codes, plane = (part[:, q * QUARTER : (q + 1) * QUARTER] for part in z_first)
             else:
-                codes, plane = (t[:] for t in z_q[1, q])
-            nc.tensor.matmul_mx(
-                out=acc[:, (c % 2) * QUARTER : (c % 2 + 1) * QUARTER],
-                lhsT=wf_q[b][0][:, c * P : (c + 1) * P].bitcast(FP8X4),
-                lhsT_scale=wf_q[b][1][:, c * P : (c + 1) * P],
-                rhs=codes.bitcast(FP8X4),
-                rhs_scale=plane,
-                start=(b == 0 and c % 2 == 0),
-                stop=(b == BLOCKS - 1 and c % 2 == 1),
-            )
-
-        accs = [[bank(n) for n in pair] for pair in SCORE_BANKS]
-        for q in range(4):
+                codes, plane = (part[:] for part in z_last[q])
             for c in range(PACK):
-                score(accs[q][c // 2], 0, q, c)
-
-        out_rows = out.rearrange("(p c) m -> p c m", c=PACK)
-
-        def store(q, pair, on_vector):
-            scores = ring.tile([P, 2, QUARTER], F32, name="scores", bufs=8, align_bytes=64)
-            acc = accs[q][pair]
-            if on_vector:
-                nc.vector.tensor_tensor(
-                    scores[:],
-                    acc[:].rearrange("p (c m) -> p c m", c=2),
-                    bias_sb[:, 2 * pair : 2 * pair + 2].unsqueeze(2).to_broadcast([P, 2, QUARTER]),
-                    ALU.add,
+                nc.tensor.matmul_mx(
+                    out=scores_in[q][c // 2][:, (c % 2) * QUARTER : (c % 2 + 1) * QUARTER],
+                    lhsT=wf_q[b][0][:, c * P : (c + 1) * P].bitcast(FP8X4),
+                    lhsT_scale=wf_q[b][1][:, c * P : (c + 1) * P],
+                    rhs=codes.bitcast(FP8X4),
+                    rhs_scale=plane,
+                    start=(b == 0 and c % 2 == 0),
+                    stop=(b == BLOCKS - 1 and c % 2 == 1),
                 )
-            else:
-                for e in range(2):
-                    c = 2 * pair + e
-                    nc.scalar.activation(
-                        scores[:, e, :], acc[:, e * QUARTER : (e + 1) * QUARTER], ACT.Identity, bias=bias_sb[:, c : c + 1]
-                    )
-            nc.sync.dma_start(out=out_rows[:, 2 * pair : 2 * pair + 2, q * QUARTER : (q + 1) * QUARTER], in_=scores[:])
 
-        for q in range(4):
+        scores_in = [[bank(number) for number in numbers] for numbers in SCORE_BANKS]
+        for q in range(QUARTERS):
+            score(0, q)
+
+        for q in range(QUARTERS):
             cols = slice(q * QUARTER, (q + 1) * QUARTER)
-            nc.vector.tensor_tensor(rows[:, 3, cols], pages[1][:, cols], queue_sb[1, 1][:, 1, cols], ALU.add)
-            z = ring.tile([P, PACK * QUARTER], BF16, name="woven", bufs=4, align_bytes=64)
-            (nc.scalar.copy if q == 1 else nc.vector.tensor_copy)(
-                z[:].rearrange("p (c e i) -> p c i e", e=4, i=PACK),
+            nc.vector.tensor_tensor(rows[:, PACK - 1, cols], last_page[:, cols], queue_sb[1, 1][:, 1, cols], ALU.add)
+            woven = ring.tile([P, PACK * QUARTER], BF16, name="woven", bufs=QUARTERS, align_bytes=64)
+            nc.vector.tensor_copy(
+                woven[:].rearrange("p (c e i) -> p c i e", e=4, i=PACK),
                 rows[:, :, cols].rearrange("p i (c e) -> p c i e", e=4),
             )
-            quantise(z_q[1, q], 0, z[:])
-            for c in range(PACK):
-                score(accs[q][c // 2], 1, q, c)
-        for q in range(4):
-            for pair in range(2):
-                store(q, pair, q >= 2 and pair == 1)
+            quantise(z_last[q], 0, woven[:])
+            score(1, q)
+
+        out_rows = out.rearrange("(p c) m -> p c m", c=PACK)
+        for q in range(QUARTERS):
+            for half in range(2):
+                acc = scores_in[q][half]
+                channels = slice(2 * half, 2 * half + 2)
+                scores = ring.tile([P, 2, QUARTER], F32, name="scores", bufs=2 * QUARTERS, align_bytes=64)
+                if q == QUARTERS - 1 and half == 1:
+                    nc.vector.tensor_tensor(
+                        scores[:],
+                        acc[:].rearrange("p (c m) -> p c m", c=2),
+                        bias_sb[:, channels].unsqueeze(2).to_broadcast([P, 2, QUARTER]),
+                        ALU.add,
+                    )
+                else:
+                    for e in range(2):
+                        c = 2 * half + e
+                        nc.scalar.activation(
+                            scores[:, e, :], acc[:, e * QUARTER : (e + 1) * QUARTER], ACT.Identity, bias=bias_sb[:, c : c + 1]
+                        )
+                nc.sync.dma_start(out=out_rows[:, channels, q * QUARTER : (q + 1) * QUARTER], in_=scores[:])

@@ -28,8 +28,7 @@ QUADRANT = 32
 QUADRANTS = P // QUADRANT
 QUARTERS = 4
 QUARTER = T2 // QUARTERS
-PLANE_ROWS = 3 * QUADRANT + 4
-PACKED_FROM = QUADRANT - 4 * PASSES
+ROWS_FROM = P - 16 * PASSES
 
 ENCODE_BANK = (2, 3, 4, 5, 4, 5, 6, 7)
 LINEAR_BANK = (0, 1, 2, 3, 0, 1, 6, 7)
@@ -92,55 +91,48 @@ def tile_list_fraud_residual_queue_kernel(
 
         w4_planes_raw = keep([P, PASSES * H], U8, "w4_planes_raw")
         nc.gpsimd.memset(w4_planes_raw[:].bitcast(I32), 0)
-        tab_planes = placed("tab_planes", PLANES_AT + ROW // 2, [P, T], U8)
         for q in range(QUADRANTS):
-            nc.vector.memset(tab_planes[QUADRANT * q : QUADRANT * q + PACKED_FROM, :].bitcast(I32), 0)
-        v_planes = [keep([P, S], U8, "v_plane%d" % a) for a in range(PASSES)]
-        for plane in v_planes:
-            nc.vector.memset(plane[:].bitcast(I32), 0)
-        pages = [keep([P, T2], F32, "page%d" % i) for i in range(PACK)]
-        for page in pages:
-            nc.gpsimd.memset(page[:], 0.0)
-        identity = keep([P, P], F32, "identity")
-        make_identity(nc, identity[:])
-
-        table = [load_table(0, 0)]
-        picks = held.tile([P, S // 16], U16, name="picks")
-        nc.sync.dma_start(picks[:], offs)
-        w4_raw = [load_w4(0)]
-        for q in range(QUADRANTS):
-            nc.sync.dma_start(
-                out=tab_planes[QUADRANT * q + PACKED_FROM : QUADRANT * (q + 1), :].bitcast(I32),
-                in_=tab_scales[:, 4 * q : 4 * q + 4, :].bitcast(I32),
-            )
-        w1_raw = {(0, 0): load_weight(slot(1, weight_shape, F32), w1, 0, 0)}
-        for q in range(QUADRANTS):
-            nc.sync.dma_start(
+            nc.gpsimd.dma_start(
                 out=w4_planes_raw[QUADRANT * q : QUADRANT * q + 4, :].bitcast(I32).rearrange("r (a c) -> r a c", a=PASSES),
                 in_=w4_scales[:, 4 * q : 4 * q + 4, :].bitcast(I32).rearrange("a r c -> r a c"),
             )
-        table.append(load_table(2, 1))
-        table.append(load_table(3, 2))
+        tab_planes = placed("tab_planes", PLANES_AT + ROW // 2, [P, T], U8)
+        nc.vector.memset(tab_planes[0:ROWS_FROM, :].bitcast(I32), 0)
+        v_plane_tile = keep([P, PASSES * S], U8, "v_planes")
+        nc.vector.memset(v_plane_tile[:].bitcast(I32), 0)
+        v_planes = [v_plane_tile[:, a * S : (a + 1) * S] for a in range(PASSES)]
+        pages = [keep([P, T2], F32, "page%d" % i) for i in range(PACK)]
+        for page in pages[:2]:
+            nc.vector.memset(page[:], 0.0)
+        identity = keep([P, P], F32, "identity")
+        make_identity(nc, identity[:])
+        for page in pages[2:]:
+            nc.gpsimd.memset(page[:], 0.0)
 
-        picked_planes = keep([P, S], U8, "picked_planes")
-        nc.vector.tensor_copy(picked_planes[:], tab_planes[:].indirect(picks[:]))
-
-        def move_plane(a):
-            first = PACKED_FROM + 4 * a
-            nc.sync.dma_start(
-                out=v_planes[a][0:PLANE_ROWS, :].bitcast(I32),
-                in_=picked_planes[first : first + PLANE_ROWS, :].bitcast(I32),
-            )
-
-        move_plane(0)
-        move_plane(1)
-        w1_raw[1, 0] = load_weight(slot(4, weight_shape, F32), w1, 1, 0)
-        move_plane(2)
-        w1_raw[2, 0] = load_weight(placed("w1_last0", W1_LAST_AT[0], weight_shape, F32), w1, 2, 0)
-        w4_raw.append(load_w4(1))
+        picks = held.tile([P, S // 16], U16, name="picks")
+        nc.sync.dma_start(picks[:], offs)
+        for a in range(PASSES):
+            nc.sync.dma_start(out=tab_planes[ROWS_FROM + a : P : PASSES, :].bitcast(I32), in_=tab_scales[a].bitcast(I32))
+        table = [load_table(0, 0)]
+        w4_raw = [load_w4(0)]
         dec_sb = load(keep([P, BLOCKS, PACK], F32, "dec_sb"), dec.rearrange("(b p i) -> p b i", b=BLOCKS, i=PACK))
         places = held.tile([P, S // 16], U16, name="places")
         nc.sync.dma_start(places[:], offs2)
+        w1_raw = {(0, 0): load_weight(slot(1, weight_shape, F32), w1, 0, 0)}
+        table.append(load_table(2, 1))
+        table.append(load_table(3, 2))
+        w1_raw[1, 0] = load_weight(slot(4, weight_shape, F32), w1, 1, 0)
+
+        picked_planes = keep([P, S], U8, "picked_planes")
+        nc.vector.tensor_copy(picked_planes[:], tab_planes[:].indirect(picks[:]))
+        for q in range(QUADRANTS):
+            first = ROWS_FROM + 4 * PASSES * q
+            nc.scalar.dma_start(
+                out=v_plane_tile[QUADRANT * q : QUADRANT * q + 4, :].bitcast(I32),
+                in_=picked_planes[first : first + 4 * PASSES, :].bitcast(I32),
+            )
+        w1_raw[2, 0] = load_weight(placed("w1_last0", W1_LAST_AT[0], weight_shape, F32), w1, 2, 0)
+        w4_raw.append(load_w4(1))
         wgs_sb = load(keep([P, S], F32, "wgs_sb"), wgs)
         w1_raw[0, 1] = load_weight(slot(6, weight_shape, F32), w1, 0, 1)
         w1_raw[1, 1] = load_weight(slot(7, weight_shape, F32), w1, 1, 1)
@@ -190,7 +182,6 @@ def tile_list_fraud_residual_queue_kernel(
 
         gather(0, keep([P, S], U32, "v_words0"))
         w4_codes = [keep([P, PASSES * 2 * KP], U8, "w4_codes%d" % b) for b in range(BLOCKS)]
-        w4_planes = keep([P, PASSES * H], U8, "w4_planes")
 
         def order_words(b):
             nc.vector.tensor_copy(
@@ -199,6 +190,7 @@ def tile_list_fraud_residual_queue_kernel(
             )
 
         order_words(0)
+        w4_planes = keep([P, PASSES * H], U8, "w4_raw0")
         nc.vector.tensor_copy(
             w4_planes[:].rearrange("p (g t m) -> p g t m", t=PACK, m=P),
             w4_planes_raw[:].rearrange("p (g m t) -> p g t m", t=PACK, m=P),
@@ -232,7 +224,7 @@ def tile_list_fraud_residual_queue_kernel(
                     lhsT=w4_codes[b][:, 2 * word0 : 2 * (word0 + P)].bitcast(FP4X4),
                     lhsT_scale=w4_planes[:, byte0 : byte0 + P],
                     rhs=v_words[a][:].bitcast(FP8X4),
-                    rhs_scale=v_planes[a][:],
+                    rhs_scale=v_planes[a],
                     start=(a == order[0]),
                     stop=(a == order[-1]),
                 )
@@ -255,7 +247,7 @@ def tile_list_fraud_residual_queue_kernel(
                     lhsT=codes[:, i * P : (i + 1) * P].bitcast(FP8X4),
                     lhsT_scale=plane[:, i * P : (i + 1) * P],
                     rhs=v_words[a][:].bitcast(FP8X4),
-                    rhs_scale=v_planes[a][:],
+                    rhs_scale=v_planes[a],
                     start=(a == order[0]),
                     stop=(a == order[-1]),
                 )

@@ -33,8 +33,8 @@ ROWS_FROM = P - 16 * PASSES
 ENCODE_BANK = (2, 3, 4, 5, 4, 5, 6, 7)
 LINEAR_BANK = (0, 1, 2, 3, 0, 1, 6, 7)
 PAIR_BANKS = ((4, 5, 6, 7), (2, 3, 4, 5))
-ROW_BANKS = (((0, 1), (2,)), ((4, 5), (0, 1, 6, 7)), ((0, 1, 6, 7), (4, 5, 2, 3)))
-SCORE_BANKS = ((0, 1), (6, 7), (4, 5), (2, 3))
+ROW_BANKS = (((2, 3), (2,)), ((4, 5), (4, 5)), ((0, 1), (0, 1)))
+SCORE_BANKS = ((6, 7), (2, 3), (4, 5), (0, 1))
 
 SLOT = 4 * PACK * KP
 ROW = 4 * S
@@ -280,17 +280,13 @@ def tile_list_fraud_residual_queue_kernel(
             return ring.tile([P, BANK], BF16, name="pair", bufs=QUARTERS, align_bytes=64)
 
         def sum_pair(u, make_tile):
-            tiles = []
-            for q in range(QUARTERS):
-                acc = bank(PAIR_BANKS[u][q])
-                for step in range(2):
-                    for piece in range(2):
-                        cols = slice((2 * q + piece) * P, (2 * q + piece + 1) * P)
-                        for e in range(2):
-                            source = queue_sb[0, u][:, e, cols] if step == 0 else pages[2 * u + e][:, cols]
-                            add_turned(acc, 2 * piece + e, source, step + piece + e == 0, step + piece + e == 3)
-                tiles.append(round_in_pairs(acc, 2, make_tile(q)))
-            return tiles
+            accs = [bank(number) for number in PAIR_BANKS[u]]
+            sources = [(e, queue_sb[0, u][:, e, :]) for e in range(2)] + [(e, pages[2 * u + e][:]) for e in range(2)]
+            for step, (e, source) in enumerate(sources):
+                for piece in range(2 * QUARTERS):
+                    first, last = step == 0 and piece % 2 == 0, step == 3 and piece % 2 == 1
+                    add_turned(accs[piece // 2], 2 * (piece % 2) + e, source[:, piece * P : (piece + 1) * P], first, last)
+            return [round_in_pairs(accs[q], 2, make_tile(q)) for q in range(QUARTERS)]
 
         def turn_back(q, pairs, z):
             acc = bank(PAIR_BANKS[1][q])
@@ -302,18 +298,17 @@ def tile_list_fraud_residual_queue_kernel(
             target = z[:, q * PACK * QUARTER : (q + 1) * PACK * QUARTER]
             nc.scalar.copy(target.bitcast(F32).rearrange("p (m u) -> p m u", u=2), acc[:].rearrange("p (u m) -> p m u", u=2))
 
-        def sum_row(i, rows):
+        def sum_row(i, page, rows):
             sum_banks, back_banks = ROW_BANKS[i]
             words = []
             groups = QUARTERS // len(sum_banks)
-            for part, number in enumerate(sum_banks):
-                acc = bank(number)
-                for step in range(2):
-                    for piece in range(2 * groups):
-                        first = (2 * groups * part + piece) * P
-                        cols = slice(first, first + P)
-                        source = queue_sb[1, i // 2][:, i % 2, cols] if step == 0 else pages[i][:, cols]
-                        add_turned(acc, piece, source, step == 0 and piece == 0, step == 1 and piece == 2 * groups - 1)
+            accs = [bank(number) for number in sum_banks]
+            for step, source in enumerate((queue_sb[1, i // 2][:, i % 2, :], page[:])):
+                for piece in range(2 * QUARTERS):
+                    part, column = divmod(piece, 2 * groups)
+                    first, last = step == 0 and column == 0, step == 1 and column == 2 * groups - 1
+                    add_turned(accs[part], column, source[:, piece * P : (piece + 1) * P], first, last)
+            for acc in accs:
                 tile = round_in_pairs(acc, groups, pair_tile())
                 words.extend(tile[:].bitcast(F32)[:, g * P : (g + 1) * P] for g in range(groups))
             groups = QUARTERS // len(back_banks)
@@ -362,7 +357,7 @@ def tile_list_fraud_residual_queue_kernel(
 
         h[4] = residual(4, h_tile())
         h[5] = residual(5, h_tile())
-        quantise(wf_q[0], 0, cast(nc.scalar.copy, wf_raw[0], 0, PACK, slot(4, [P, PACK * KP], BF16))[:])
+        quantise(wf_q[0], 0, cast(nc.scalar.copy, wf_raw[0], 0, PACK, staging("head_stage"))[:])
         quantise(wf_q[1], 0, cast(nc.scalar.copy, wf_raw[1], 0, PACK, staging("late_stage"))[:])
         pairs.append(sum_pair(1, lambda q: placed("pair%d" % q, WF_LAST_AT + 2 * BANK * q, [P, BANK], BF16)))
         scatter(pages[0], h[4])
@@ -374,10 +369,10 @@ def tile_list_fraud_residual_queue_kernel(
             turn_back(q, pairs, z_block)
         quantise(z_first, 0, z_block[:])
         rows = keep([P, PACK, T2], BF16, "z_rows")
-        sum_row(0, rows)
-        sum_row(1, rows)
-        scatter(pages[2], h[6])
-        sum_row(2, rows)
+        sum_row(0, pages[0], rows)
+        sum_row(1, pages[1], rows)
+        scatter(pages[0], h[6])
+        sum_row(2, pages[0], rows)
         last_page = pages[1]
         scatter(last_page, h[7])
 

@@ -30,11 +30,12 @@ QUARTERS = 4
 QUARTER = T2 // QUARTERS
 ROWS_FROM = P - 16 * PASSES
 
-ENCODE_BANK = (2, 3, 4, 5, 4, 5, 6, 7)
+ENCODE_BANK = (2, 3, 4, 5, 0, 1, 0, 1)
 LINEAR_BANK = (0, 1, 2, 3, 0, 1, 6, 7)
-PAIR_BANKS = ((4, 5, 6, 7), (2, 3, 4, 5))
-ROW_BANKS = (((2, 3), (2,)), ((4, 5), (4, 5)), ((0, 1), (0, 1)))
-SCORE_BANKS = ((6, 7), (2, 3), (4, 5), (0, 1))
+PAIR_BANKS = ((4, 7, 5, 6), (2, 3, 4, 5))
+BACK_ORDER = (0, 2, 3, 1)
+ROW_BANKS = (((2, 4), (2,)), ((5, 3), (5, 3)), ((5, 3), (5, 3)))
+SCORE_BANKS = ((0, 1), (6, 7), (4, 2), (5, 3))
 
 SLOT = 4 * PACK * KP
 ROW = 4 * S
@@ -42,6 +43,8 @@ PLANES_AT = 0
 WF_LAST_AT = 2 * ROW
 W1_LAST_AT = (WF_LAST_AT + SLOT, WF_LAST_AT + 2 * SLOT)
 STAGE_AT = WF_LAST_AT + 3 * SLOT
+W1_MID_AT = STAGE_AT + SLOT
+TANH_AT = (W1_LAST_AT[0], W1_LAST_AT[0] + ROW, W1_LAST_AT[0] + 2 * ROW, W1_MID_AT, W1_MID_AT + ROW, W1_LAST_AT[1], W1_LAST_AT[1] + ROW)
 
 
 def tile_list_fraud_residual_queue_kernel(
@@ -135,14 +138,12 @@ def tile_list_fraud_residual_queue_kernel(
         w4_raw.append(load_w4(1))
         wgs_sb = load(keep([P, S], F32, "wgs_sb"), wgs)
         w1_raw[0, 1] = load_weight(slot(6, weight_shape, F32), w1, 0, 1)
-        w1_raw[1, 1] = load_weight(slot(7, weight_shape, F32), w1, 1, 1)
+        w1_raw[1, 1] = load_weight(placed("w1_mid", W1_MID_AT, weight_shape, F32), w1, 1, 1)
+        queue_sb = {(0, 0): load_queue(7, 0, 0)}
         w1_raw[2, 1] = load_weight(placed("w1_last1", W1_LAST_AT[1], weight_shape, F32), w1, 2, 1)
-        queue_sb = {(0, 0): load_queue(4, 0, 0)}
-        wf_raw = [
-            load_weight(slot(5, weight_shape, F32), wf, 0, 0),
-            load_weight(placed("wf_last", WF_LAST_AT, weight_shape, F32), wf, 1, 0),
-        ]
+        wf_raw = [load_weight(slot(5, weight_shape, F32), wf, 0, 0)]
         queue_sb[0, 1] = load_queue(0, 0, 1)
+        wf_raw.append(load_weight(placed("wf_last", WF_LAST_AT, weight_shape, F32), wf, 1, 0))
         queue_sb[1, 0] = load_queue(1, 1, 0)
         queue_sb[1, 1] = load_queue(6, 1, 1)
         bias_sb = load(keep([P, PACK], F32, "bias_sb"), bf.rearrange("(p c) -> p c", c=PACK))
@@ -231,16 +232,17 @@ def tile_list_fraud_residual_queue_kernel(
             if k == 0:
                 result = ring.tile([P, S], F32, name="minus_enc")
             else:
-                place = i - 1 if b == 0 else i
-                result = placed("minus_enc%d" % k, W1_LAST_AT[b] + ROW * place, [P, S], F32)
+                result = placed("minus_enc%d" % k, TANH_AT[k - 1], [P, S], F32)
             nc.scalar.activation(result[:], acc[:], ACT.Tanh, scale=-1.0)
             return result
 
-        def linear(k):
-            b, i = divmod(k, PACK)
-            acc = bank(LINEAR_BANK[k])
-            order = pass_order(k)
-            for a in order:
+        def linear(*tiles):
+            order = pass_order(3) if tiles == (3,) else range(PASSES)
+            for k in tiles:
+                lin[k] = bank(LINEAR_BANK[k])
+            for a, k in [(a, k) for a in order for k in tiles]:
+                b, i = divmod(k, PACK)
+                acc = lin[k]
                 codes, plane = w1_q[a, b]
                 nc.tensor.matmul_mx(
                     out=acc[:],
@@ -251,7 +253,6 @@ def tile_list_fraud_residual_queue_kernel(
                     start=(a == order[0]),
                     stop=(a == order[-1]),
                 )
-            return acc
 
         def residual(k, tile):
             b, i = divmod(k, PACK)
@@ -279,14 +280,20 @@ def tile_list_fraud_residual_queue_kernel(
         def pair_tile():
             return ring.tile([P, BANK], BF16, name="pair", bufs=QUARTERS, align_bytes=64)
 
-        def sum_pair(u, make_tile):
-            accs = [bank(number) for number in PAIR_BANKS[u]]
+        def pair_banks(u):
+            return [bank(number) for number in PAIR_BANKS[u]]
+
+        def sum_pair(u, accs, phases):
             sources = [(e, queue_sb[0, u][:, e, :]) for e in range(2)] + [(e, pages[2 * u + e][:]) for e in range(2)]
-            for step, (e, source) in enumerate(sources):
-                for piece in range(2 * QUARTERS):
-                    first, last = step == 0 and piece % 2 == 0, step == 3 and piece % 2 == 1
-                    add_turned(accs[piece // 2], 2 * (piece % 2) + e, source[:, piece * P : (piece + 1) * P], first, last)
-            return [round_in_pairs(accs[q], 2, make_tile(q)) for q in range(QUARTERS)]
+            for steps in phases:
+                for q in BACK_ORDER:
+                    for step in steps:
+                        e, source = sources[step]
+                        for piece in range(2):
+                            cols = slice((2 * q + piece) * P, (2 * q + piece + 1) * P)
+                            first, last = step == 0 and piece == 0, step == 3 and piece == 1
+                            add_turned(accs[q], 2 * piece + e, source[:, cols], first, last)
+            return accs
 
         def turn_back(q, pairs, z):
             acc = bank(PAIR_BANKS[1][q])
@@ -295,10 +302,10 @@ def tile_list_fraud_residual_queue_kernel(
                 for piece in range(2):
                     column = 2 * u + piece
                     nc.tensor.transpose(acc[:, column * P : (column + 1) * P], words[:, piece * P : (piece + 1) * P], identity[:])
-            target = z[:, q * PACK * QUARTER : (q + 1) * PACK * QUARTER]
+            target = z[q // 2][:, q % 2 * PACK * QUARTER : (q % 2 + 1) * PACK * QUARTER]
             nc.scalar.copy(target.bitcast(F32).rearrange("p (m u) -> p m u", u=2), acc[:].rearrange("p (u m) -> p m u", u=2))
 
-        def sum_row(i, page, rows):
+        def sum_row(i, page):
             sum_banks, back_banks = ROW_BANKS[i]
             words = []
             groups = QUARTERS // len(sum_banks)
@@ -316,64 +323,76 @@ def tile_list_fraud_residual_queue_kernel(
                 acc = bank(number)
                 for g in range(groups):
                     nc.tensor.transpose(acc[:, g * P : (g + 1) * P], words[groups * part + g], identity[:])
-                target = rows[:, i, part * groups * QUARTER : (part + 1) * groups * QUARTER]
-                nc.scalar.copy(
-                    target.rearrange("p (g e m) -> p g e m", g=groups, e=2),
-                    acc[:, 0 : groups * P].bitcast(BF16).rearrange("p (g m e) -> p g e m", g=groups, e=2),
-                )
+                for g in range(groups):
+                    nc.scalar.copy(
+                        rows[groups * part + g][:, i, :].rearrange("p (e m) -> p e m", e=2),
+                        acc[:, g * P : (g + 1) * P].bitcast(BF16).rearrange("p (m e) -> p e m", e=2),
+                    )
 
         minus_enc = {0: encode(0)}
         quantise_first_half(2)
-        lin = {0: linear(0), 1: linear(1)}
+        lin = {}
+        linear(0)
+        linear(1)
         order_words(1)
         h = {0: residual(0, h_tile())}
         quantise_second_half(2)
         for k in range(1, PACK):
             minus_enc[k] = encode(k)
-        lin[2] = linear(2)
-        lin[3] = linear(3)
-        scatter(pages[0], h[0])
+        linear(2)
+        linear(3)
         h[1] = residual(1, h_tile())
+        scatter(pages[0], h[0])
+        h[2] = residual(2, h_tile())
         scatter(pages[1], h[1])
-
-        two_passes = placed("w1_two_stage", STAGE_AT, [P, 2 * PACK * KP], BF16)
-        for a in range(2):
-            cast(nc.scalar.copy, w1_raw[a, 1], 0, PACK, two_passes[:, a * PACK * KP : (a + 1) * PACK * KP])
-        two_q = operand("w1_two", 2 * KP)
-        quantise(two_q, 0, two_passes[:])
-        for a in range(2):
-            w1_q[a, 1] = tuple(part[:, a * KP : (a + 1) * KP] for part in two_q)
-        last_pass = cast(nc.scalar.copy, w1_raw[2, 1], 0, PACK, staging("late_stage"))
-        for k in (2, 3):
-            h[k] = residual(k, placed("h%d" % k, STAGE_AT + ROW * (k - 2), [P, S], F32))
         scatter(pages[2], h[2])
-        quantise(w1_q[2, 1], 0, last_pass[:])
-        for k in range(PACK, TILES):
-            minus_enc[k] = encode(k)
-        pairs = [sum_pair(0, lambda q: pair_tile())]
-        for k in range(PACK, TILES):
-            lin[k] = linear(k)
+
+        staged = []
+        for a in range(2):
+            tile = placed("w1_stage%d" % a, STAGE_AT + 2 * ROW * a, [P, PACK * KP], BF16)
+            staged.append(cast(nc.scalar.copy, w1_raw[a, 1], 0, PACK, tile))
+        minus_enc[4] = encode(4)
+        minus_enc[5] = encode(5)
+        staged.append(cast(nc.scalar.copy, w1_raw[2, 1], 0, PACK, staging("late_stage")))
+        minus_enc[6] = encode(6)
+        minus_enc[7] = encode(7)
+        for a in range(2):
+            codes = placed("w1_codes%d" % a, W1_LAST_AT[1] + (2 + a) * ROW, [P, KP], U32)
+            w1_q[a, 1] = (codes, keep([P, KP], U8, "w1_plane%d" % a))
+            quantise(w1_q[a, 1], 0, staged[a][:])
+        h[3] = residual(3, placed("h3", STAGE_AT, [P, S], F32))
+        quantise(w1_q[2, 1], 0, staged[2][:])
         scatter(pages[3], h[3])
+        first = sum_pair(0, pair_banks(0), [(0, 1, 2), (3,)])
+        pairs = [{q: round_in_pairs(first[q], 2, pair_tile()) for q in BACK_ORDER}]
+        linear(4, 5)
+        second = sum_pair(1, pair_banks(1), [(0, 1, 2)])
 
         h[4] = residual(4, h_tile())
         h[5] = residual(5, h_tile())
         quantise(wf_q[0], 0, cast(nc.scalar.copy, wf_raw[0], 0, PACK, staging("head_stage"))[:])
         quantise(wf_q[1], 0, cast(nc.scalar.copy, wf_raw[1], 0, PACK, staging("late_stage"))[:])
-        pairs.append(sum_pair(1, lambda q: placed("pair%d" % q, WF_LAST_AT + 2 * BANK * q, [P, BANK], BF16)))
+        sum_pair(1, second, [(3,)])
+        linear(6, 7)
+        pairs.append({})
+        for q in BACK_ORDER:
+            pairs[1][q] = round_in_pairs(second[q], 2, placed("pair%d" % q, WF_LAST_AT + 2 * BANK * q, [P, BANK], BF16))
         scatter(pages[0], h[4])
-        h[6] = residual(6, h_tile())
         scatter(pages[1], h[5])
-        h[7] = residual(7, h_tile())
-        z_block = staging("z_block", PACK * T2)
-        for q in range(QUARTERS):
-            turn_back(q, pairs, z_block)
-        quantise(z_first, 0, z_block[:])
-        rows = keep([P, PACK, T2], BF16, "z_rows")
-        sum_row(0, pages[0], rows)
-        sum_row(1, pages[1], rows)
-        scatter(pages[0], h[6])
-        sum_row(2, pages[0], rows)
-        last_page = pages[1]
+        z_halves = [placed("z_half%d" % u, STAGE_AT + 2 * ROW * u, [P, 2 * PACK * QUARTER], BF16) for u in range(2)]
+        for q in BACK_ORDER:
+            turn_back(q, pairs, z_halves)
+        for u in (1, 0):
+            quantise(z_first, u * 2 * QUARTER, z_halves[u][:])
+        for k in (6, 7):
+            h[k] = residual(k, placed("h%d" % k, STAGE_AT + ROW * (k - 4), [P, S], F32))
+        row_tiles = [keep([P, 13, QUARTER], BF16, "z_rows%d" % u) for u in range(2)]
+        rows = [tile[:, 9:13, :] for tile in row_tiles] + [tile[:, 0:13:4, :] for tile in row_tiles]
+        sum_row(0, pages[0])
+        sum_row(1, pages[1])
+        scatter(pages[2], h[6])
+        sum_row(2, pages[2])
+        last_page = pages[3]
         scatter(last_page, h[7])
 
         def score(b, q):
@@ -398,11 +417,11 @@ def tile_list_fraud_residual_queue_kernel(
 
         for q in range(QUARTERS):
             cols = slice(q * QUARTER, (q + 1) * QUARTER)
-            nc.vector.tensor_tensor(rows[:, PACK - 1, cols], last_page[:, cols], queue_sb[1, 1][:, 1, cols], ALU.add)
+            nc.vector.tensor_tensor(rows[q][:, PACK - 1, :], last_page[:, cols], queue_sb[1, 1][:, 1, cols], ALU.add)
             woven = ring.tile([P, PACK * QUARTER], BF16, name="woven", bufs=QUARTERS, align_bytes=64)
             nc.vector.tensor_copy(
                 woven[:].rearrange("p (c e i) -> p c i e", e=4, i=PACK),
-                rows[:, :, cols].rearrange("p i (c e) -> p c i e", e=4),
+                rows[q].rearrange("p i (c e) -> p c i e", e=4),
             )
             quantise(z_last[q], 0, woven[:])
             score(1, q)
@@ -413,7 +432,7 @@ def tile_list_fraud_residual_queue_kernel(
                 acc = scores_in[q][half]
                 channels = slice(2 * half, 2 * half + 2)
                 scores = ring.tile([P, 2, QUARTER], F32, name="scores", bufs=2 * QUARTERS, align_bytes=64)
-                if q == QUARTERS - 1 and half == 1:
+                if q >= 2 and half == 1:
                     nc.vector.tensor_tensor(
                         scores[:],
                         acc[:].rearrange("p (c m) -> p c m", c=2),

@@ -146,7 +146,7 @@ def tile_list_fraud_residual_queue_kernel(
         wf_raw.append(load_weight(placed("wf_last", WF_LAST_AT, weight_shape, F32), wf, 1, 0))
         queue_sb[1, 0] = load_queue(1, 1, 0)
         queue_sb[1, 1] = load_queue(6, 1, 1)
-        bias_sb = load(keep([P, PACK], F32, "bias_sb"), bf.rearrange("(p c) -> p c", c=PACK))
+        bias_sb = load(keep([P, PACK, 1], F32, "bias_sb"), bf.rearrange("(c p o) -> p c o", p=P, o=1))
 
         v_words = {}
 
@@ -164,6 +164,12 @@ def tile_list_fraud_residual_queue_kernel(
                 copy(dst[:, :, :, t - t0 : t - t0 + 2], src[:, :, :, t : t + 2])
             return tile
 
+        def cast_straight(raw, tile):
+            nc.scalar.copy(
+                tile[:].rearrange("p (c e j) -> p c j e", e=4, j=PACK), raw[:].rearrange("p j (c e) -> p c j e", e=4)
+            )
+            return tile
+
         def quantise(target, c0, values):
             c1 = c0 + values.shape[1] // PACK
             nc.vector.quantize_mx(out=target[0][:, c0:c1].bitcast(FP8X4), scales=target[1][:, c0:c1], in_=values)
@@ -177,7 +183,7 @@ def tile_list_fraud_residual_queue_kernel(
             (2, 0): operand("w1_2_0"),
             (2, 1): operand("w1_2_1"),
         }
-        wf_q = [operand("wf_%d" % b) for b in range(BLOCKS)]
+        wf_q = [operand("wf_0")]
         z_first = operand("z_first", T2)
         z_last = [operand("z_last%d" % q, QUARTER) for q in range(QUARTERS)]
 
@@ -370,8 +376,8 @@ def tile_list_fraud_residual_queue_kernel(
 
         h[4] = residual(4, h_tile())
         h[5] = residual(5, h_tile())
-        quantise(wf_q[0], 0, cast(nc.scalar.copy, wf_raw[0], 0, PACK, staging("head_stage"))[:])
-        quantise(wf_q[1], 0, cast(nc.scalar.copy, wf_raw[1], 0, PACK, staging("late_stage"))[:])
+        quantise(wf_q[0], 0, cast_straight(wf_raw[0], staging("head_stage"))[:])
+        wf_last = cast_straight(wf_raw[1], staging("late_stage"))
         sum_pair(1, second, [(3,)])
         linear(6, 7)
         pairs.append({})
@@ -394,6 +400,8 @@ def tile_list_fraud_residual_queue_kernel(
         sum_row(2, pages[2])
         last_page = pages[3]
         scatter(last_page, h[7])
+        wf_q.append((placed("wf_1_codes", STAGE_AT + 2 * ROW, [P, KP], U32), keep([P, KP], U8, "wf_1_plane")))
+        quantise(wf_q[1], 0, wf_last[:])
 
         def score(b, q):
             if b == 0:
@@ -426,7 +434,7 @@ def tile_list_fraud_residual_queue_kernel(
             quantise(z_last[q], 0, woven[:])
             score(1, q)
 
-        out_rows = out.rearrange("(p c) m -> p c m", c=PACK)
+        out_rows = out.rearrange("(c p) m -> p c m", p=P)
         for q in range(QUARTERS):
             for half in range(2):
                 acc = scores_in[q][half]
@@ -436,13 +444,13 @@ def tile_list_fraud_residual_queue_kernel(
                     nc.vector.tensor_tensor(
                         scores[:],
                         acc[:].rearrange("p (c m) -> p c m", c=2),
-                        bias_sb[:, channels].unsqueeze(2).to_broadcast([P, 2, QUARTER]),
+                        bias_sb[:, channels, :].to_broadcast([P, 2, QUARTER]),
                         ALU.add,
                     )
                 else:
                     for e in range(2):
                         c = 2 * half + e
                         nc.scalar.activation(
-                            scores[:, e, :], acc[:, e * QUARTER : (e + 1) * QUARTER], ACT.Identity, bias=bias_sb[:, c : c + 1]
+                            scores[:, e, :], acc[:, e * QUARTER : (e + 1) * QUARTER], ACT.Identity, bias=bias_sb[:, c, :]
                         )
                 nc.sync.dma_start(out=out_rows[:, channels, q * QUARTER : (q + 1) * QUARTER], in_=scores[:])

@@ -82,10 +82,11 @@ def tile_list_fraud_residual_queue_kernel(
             rows = w[a * KP : (a + 1) * KP, b * KP : (b + 1) * KP]
             return load(tile, rows.rearrange("(p j) c -> p j c", j=PACK))
 
-        def load_w4(b):
+        def load_w4(b, parts):
             tile = keep([P, PASSES, 2 * KP], U8, "w4_raw%d" % b)
             words = w4_words[:, :, b * 2 * KP : (b + 1) * 2 * KP].rearrange("a p n -> p a n")
-            nc.sync.dma_start(out=tile[:].bitcast(I32), in_=words.bitcast(I32))
+            for passes in parts:
+                nc.sync.dma_start(out=tile[:, passes, :].bitcast(I32), in_=words[:, passes, :].bitcast(I32))
             return tile
 
         def load_queue(number, b, u):
@@ -117,10 +118,7 @@ def tile_list_fraud_residual_queue_kernel(
         for a in range(PASSES):
             nc.sync.dma_start(out=tab_planes[ROWS_FROM + a : P : PASSES, :].bitcast(I32), in_=tab_scales[a].bitcast(I32))
         table = [load_table(0, 0)]
-        w4_raw = [load_w4(0)]
-        dec_sb = load(keep([P, BLOCKS, PACK], F32, "dec_sb"), dec.rearrange("(b p i) -> p b i", b=BLOCKS, i=PACK))
-        places = held.tile([P, S // 16], U16, name="places")
-        nc.sync.dma_start(places[:], offs2)
+        w4_raw = [load_w4(0, range(PASSES))]
         w1_raw = {(0, 0): load_weight(slot(1, weight_shape, F32), w1, 0, 0)}
         table.append(load_table(2, 1))
         table.append(load_table(3, 2))
@@ -135,7 +133,10 @@ def tile_list_fraud_residual_queue_kernel(
                 in_=picked_planes[first : first + 4 * PASSES, :].bitcast(I32),
             )
         w1_raw[2, 0] = load_weight(placed("w1_last0", W1_LAST_AT[0], weight_shape, F32), w1, 2, 0)
-        w4_raw.append(load_w4(1))
+        w4_raw.append(load_w4(1, [slice(0, PASSES)]))
+        dec_sb = load(keep([P, BLOCKS, PACK], F32, "dec_sb"), dec.rearrange("(b p i) -> p b i", b=BLOCKS, i=PACK))
+        places = held.tile([P, S // 16], U16, name="places")
+        nc.sync.dma_start(places[:], offs2)
         wgs_sb = load(keep([P, S], F32, "wgs_sb"), wgs)
         w1_raw[0, 1] = load_weight(slot(6, weight_shape, F32), w1, 0, 1)
         w1_raw[1, 1] = load_weight(placed("w1_mid", W1_MID_AT, weight_shape, F32), w1, 1, 1)

@@ -30,7 +30,7 @@ QUARTERS = 4
 QUARTER = T2 // QUARTERS
 ROWS_FROM = P - 16 * PASSES
 
-ENCODE_BANK = (2, 3, 4, 5, 0, 1, 0, 1)
+ENCODE_BANK = (2, 3, 4, 5, 0, 1, 6, 7)
 LINEAR_BANK = (0, 1, 2, 3, 0, 1, 6, 7)
 PAIR_BANKS = ((4, 7, 5, 6), (2, 3, 4, 5))
 BACK_ORDER = (0, 2, 3, 1)
@@ -44,7 +44,7 @@ WF_LAST_AT = 2 * ROW
 W1_LAST_AT = (WF_LAST_AT + SLOT, WF_LAST_AT + 2 * SLOT)
 STAGE_AT = WF_LAST_AT + 3 * SLOT
 W1_MID_AT = STAGE_AT + SLOT
-TANH_AT = (W1_LAST_AT[0], W1_LAST_AT[0] + ROW, W1_LAST_AT[0] + 2 * ROW, W1_MID_AT, W1_MID_AT + ROW, W1_LAST_AT[1], W1_LAST_AT[1] + ROW)
+TANH_AT = (W1_LAST_AT[0], W1_LAST_AT[0] + ROW, W1_LAST_AT[0] + 2 * ROW, W1_MID_AT, W1_MID_AT + ROW, WF_LAST_AT + 2 * ROW, WF_LAST_AT + 3 * ROW)
 
 
 def tile_list_fraud_residual_queue_kernel(
@@ -140,8 +140,8 @@ def tile_list_fraud_residual_queue_kernel(
         wgs_sb = load(keep([P, S], F32, "wgs_sb"), wgs)
         w1_raw[0, 1] = load_weight(slot(6, weight_shape, F32), w1, 0, 1)
         w1_raw[1, 1] = load_weight(placed("w1_mid", W1_MID_AT, weight_shape, F32), w1, 1, 1)
-        queue_sb = {(0, 0): load_queue(7, 0, 0)}
         w1_raw[2, 1] = load_weight(placed("w1_last1", W1_LAST_AT[1], weight_shape, F32), w1, 2, 1)
+        queue_sb = {(0, 0): load_queue(7, 0, 0)}
         wf_raw = [load_weight(slot(5, weight_shape, F32), wf, 0, 0)]
         queue_sb[0, 1] = load_queue(0, 0, 1)
         wf_raw.append(load_weight(placed("wf_last", WF_LAST_AT, weight_shape, F32), wf, 1, 0))
@@ -361,8 +361,6 @@ def tile_list_fraud_residual_queue_kernel(
         minus_enc[4] = encode(4)
         minus_enc[5] = encode(5)
         staged.append(cast(nc.scalar.copy, w1_raw[2, 1], 0, PACK, staging("late_stage")))
-        minus_enc[6] = encode(6)
-        minus_enc[7] = encode(7)
         for a in range(2):
             codes = placed("w1_codes%d" % a, W1_LAST_AT[1] + (2 + a) * ROW, [P, KP], U32)
             w1_q[a, 1] = (codes, keep([P, KP], U8, "w1_plane%d" % a))
@@ -380,10 +378,12 @@ def tile_list_fraud_residual_queue_kernel(
         quantise(wf_q[0], 0, cast_straight(wf_raw[0], staging("head_stage"))[:])
         wf_last = cast_straight(wf_raw[1], staging("late_stage"))
         sum_pair(1, second, [(3,)])
-        linear(6, 7)
         pairs.append({})
         for q in BACK_ORDER:
             pairs[1][q] = round_in_pairs(second[q], 2, placed("pair%d" % q, WF_LAST_AT + 2 * BANK * q, [P, BANK], BF16))
+        minus_enc[6] = encode(6)
+        minus_enc[7] = encode(7)
+        linear(6, 7)
         scatter(pages[0], h[4])
         scatter(pages[1], h[5])
         z_halves = [placed("z_half%d" % u, STAGE_AT + 2 * ROW * u, [P, 2 * PACK * QUARTER], BF16) for u in range(2)]

@@ -393,8 +393,8 @@ def tile_list_fraud_residual_queue_kernel(
             quantise(z_first, u * 2 * QUARTER, z_halves[u][:])
         for k in (6, 7):
             h[k] = residual(k, placed("h%d" % k, STAGE_AT + ROW * (k - 4), [P, S], F32))
-        row_tiles = [keep([P, 13, QUARTER], BF16, "z_rows%d" % u) for u in range(2)]
-        rows = [tile[:, 9:13, :] for tile in row_tiles] + [tile[:, 0:13:4, :] for tile in row_tiles]
+        shared = keep([P, 16, QUARTER], BF16, "z_rows")
+        rows = [shared[:, 12:16, :], keep([P, PACK, QUARTER], BF16, "z_rows1")[:], shared[:, 2:16:4, :], shared[:, 3:16:4, :]]
         sum_row(0, pages[0])
         sum_row(1, pages[1])
         scatter(pages[2], h[6])
@@ -428,10 +428,12 @@ def tile_list_fraud_residual_queue_kernel(
             cols = slice(q * QUARTER, (q + 1) * QUARTER)
             nc.vector.tensor_tensor(rows[q][:, PACK - 1, :], last_page[:, cols], queue_sb[1, 1][:, 1, cols], ALU.add)
             woven = ring.tile([P, PACK * QUARTER], BF16, name="woven", bufs=QUARTERS, align_bytes=64)
-            nc.vector.tensor_copy(
-                woven[:].rearrange("p (c e i) -> p c i e", e=4, i=PACK),
-                rows[q].rearrange("p i (c e) -> p c i e", e=4),
-            )
+            target = woven[:].rearrange("p (c e i) -> p c i e", e=4, i=PACK)
+            source = rows[q].rearrange("p i (c e) -> p c i e", e=4)
+            own = QUARTER // 8 if q == 1 else QUARTER // 4
+            nc.vector.tensor_copy(target[:, 0:own], source[:, 0:own])
+            if q == 1:
+                nc.scalar.copy(target[:, own:], source[:, own:])
             quantise(z_last[q], 0, woven[:])
             score(1, q)
 

@@ -22,29 +22,25 @@ PACK = 4
 KP = P * PACK
 PASSES = K // KP
 BLOCKS = H // KP
-TILES = BLOCKS * PACK
 BANK = 512
 QUADRANT = 32
 QUADRANTS = P // QUADRANT
 QUARTERS = 4
 QUARTER = T2 // QUARTERS
 ROWS_FROM = P - 16 * PASSES
-
-ENCODE_BANK = (2, 3, 4, 5, 0, 1, 6, 7)
-LINEAR_BANK = (0, 1, 2, 3, 0, 1, 6, 7)
-PAIR_BANKS = ((4, 7, 5, 6), (2, 3, 4, 5))
-BACK_ORDER = (0, 2, 3, 1)
-ROW_BANKS = (((2, 4), (2,)), ((5, 3), (5, 3)), ((5, 3), (5, 3)))
-SCORE_BANKS = ((0, 1), (6, 7), (4, 2), (5, 3))
-
 SLOT = 4 * PACK * KP
+
 ROW = 4 * S
-PLANES_AT = 0
-WF_LAST_AT = 2 * ROW
-W1_LAST_AT = (WF_LAST_AT + SLOT, WF_LAST_AT + 2 * SLOT)
-STAGE_AT = WF_LAST_AT + 3 * SLOT
-W1_MID_AT = STAGE_AT + SLOT
-TANH_AT = (W1_LAST_AT[0], W1_LAST_AT[0] + ROW, W1_LAST_AT[0] + 2 * ROW, W1_MID_AT, W1_MID_AT + ROW, WF_LAST_AT + 2 * ROW, WF_LAST_AT + 3 * ROW)
+
+ENCODE_BANK = (0, 1, 2, 3, 0, 1, 4, 5)
+LINEAR_BANK = (4, 5, 6, 7, 4, 5, 6, 7)
+PAIR_BANKS = ((4, 5, 6, 7), (0, 1, 2, 3), (0, 1, 2, 3))
+BACK_BANKS = ((0, 1, 2, 3), (0, 1, 6, 7))
+LONE_BANKS = (2, 3)
+ORDER = (0, 1, 2, 3)
+SCORE_BANKS = ((4, 5), (2, 0), (3, 1), (6, 7))
+TANH_AT = ((4, 0), (4, ROW), (3, 0), (3, ROW), (9, 2 * ROW), (9, 3 * ROW), (8, 2 * ROW), (8, 3 * ROW))
+H_AT = ((10, 2 * ROW), (10, 3 * ROW), (11, 0), (11, ROW), (11, 2 * ROW), (11, 3 * ROW), (10, 0), (10, ROW))
 
 
 def tile_list_fraud_residual_queue_kernel(
@@ -54,17 +50,13 @@ def tile_list_fraud_residual_queue_kernel(
     with ExitStack() as ctx:
         held = ctx.enter_context(tc.tile_pool(name="held", bufs=1))
         over = ctx.enter_context(tc.tile_pool(name="over", bufs=1))
-        ring = ctx.enter_context(tc.tile_pool(name="ring", bufs=2))
         psum = ctx.enter_context(tc.psum_pool(name="psum", bufs=1))
 
         def keep(shape, dtype, name):
             return held.tile(shape, dtype, name=name, align_bytes=64)
 
-        def slot(number, shape, dtype):
-            return keep(shape, dtype, "slot%d" % number)
-
-        def placed(name, offset, shape, dtype):
-            return over.tile(shape, dtype, name=name, offset=offset, align_bytes=64)
+        def slot(number, name, shape, dtype, at=0):
+            return over.tile(shape, dtype, name=name, offset=number * SLOT + at, align_bytes=64)
 
         def bank(number):
             return psum.tile([P, BANK], F32, name="bank%d" % number)
@@ -74,13 +66,11 @@ def tile_list_fraud_residual_queue_kernel(
             return tile
 
         def load_table(number, a):
-            return load(slot(number, [P, T], I32), tab_words[a].rearrange("p t i -> p (t i)").bitcast(I32))
+            return load(slot(number, "table%d" % a, [P, T], I32), tab_words[a].rearrange("p t i -> p (t i)").bitcast(I32))
 
-        weight_shape = [P, PACK, KP]
-
-        def load_weight(tile, w, a, b):
+        def load_weight(number, name, w, a, b):
             rows = w[a * KP : (a + 1) * KP, b * KP : (b + 1) * KP]
-            return load(tile, rows.rearrange("(p j) c -> p j c", j=PACK))
+            return load(slot(number, name, [P, PACK, KP], F32), rows.rearrange("(p j) c -> p j c", j=PACK))
 
         def load_w4(b, parts):
             tile = keep([P, PASSES, 2 * KP], U8, "w4_raw%d" % b)
@@ -89,9 +79,10 @@ def tile_list_fraud_residual_queue_kernel(
                 nc.sync.dma_start(out=tile[:, passes, :].bitcast(I32), in_=words[:, passes, :].bitcast(I32))
             return tile
 
-        def load_queue(number, b, u):
+        def load_queue(number, pair):
+            b, u = divmod(pair, 2)
             rows = queue[b * KP : (b + 1) * KP, :].rearrange("(p i) m -> p i m", i=PACK)
-            return load(slot(number, [P, 2, T2], F32), rows[:, 2 * u : 2 * u + 2, :])
+            return load(slot(number, "queue%d" % pair, [P, 2, T2], F32), rows[:, 2 * u : 2 * u + 2, :])
 
         w4_planes_raw = keep([P, PASSES * H], U8, "w4_planes_raw")
         nc.gpsimd.memset(w4_planes_raw[:].bitcast(I32), 0)
@@ -100,18 +91,17 @@ def tile_list_fraud_residual_queue_kernel(
                 out=w4_planes_raw[QUADRANT * q : QUADRANT * q + 4, :].bitcast(I32).rearrange("r (a c) -> r a c", a=PASSES),
                 in_=w4_scales[:, 4 * q : 4 * q + 4, :].bitcast(I32).rearrange("a r c -> r a c"),
             )
-        tab_planes = placed("tab_planes", PLANES_AT + ROW // 2, [P, T], U8)
+        tab_planes = keep([P, T], U8, "tab_planes")
         nc.vector.memset(tab_planes[0:ROWS_FROM, :].bitcast(I32), 0)
         v_plane_tile = keep([P, PASSES * S], U8, "v_planes")
         nc.vector.memset(v_plane_tile[:].bitcast(I32), 0)
         v_planes = [v_plane_tile[:, a * S : (a + 1) * S] for a in range(PASSES)]
-        pages = [keep([P, T2], F32, "page%d" % i) for i in range(PACK)]
+        pages = [keep([P, T2], F32, "page%d" % i) for i in range(PACK - 1)]
         for page in pages[:2]:
             nc.vector.memset(page[:], 0.0)
         identity = keep([P, P], F32, "identity")
         make_identity(nc, identity[:])
-        for page in pages[2:]:
-            nc.gpsimd.memset(page[:], 0.0)
+        nc.gpsimd.memset(pages[2][:], 0.0)
 
         picks = held.tile([P, S // 16], U16, name="picks")
         nc.sync.dma_start(picks[:], offs)
@@ -119,10 +109,10 @@ def tile_list_fraud_residual_queue_kernel(
             nc.sync.dma_start(out=tab_planes[ROWS_FROM + a : P : PASSES, :].bitcast(I32), in_=tab_scales[a].bitcast(I32))
         table = [load_table(0, 0)]
         w4_raw = [load_w4(0, range(PASSES))]
-        w1_raw = {(0, 0): load_weight(slot(1, weight_shape, F32), w1, 0, 0)}
+        w1_raw = {(0, 0): load_weight(1, "w1_00", w1, 0, 0)}
         table.append(load_table(2, 1))
-        table.append(load_table(3, 2))
-        w1_raw[1, 0] = load_weight(slot(4, weight_shape, F32), w1, 1, 0)
+        table.append(load_table(5, 2))
+        w1_raw[1, 0] = load_weight(4, "w1_10", w1, 1, 0)
 
         picked_planes = keep([P, S], U8, "picked_planes")
         nc.vector.tensor_copy(picked_planes[:], tab_planes[:].indirect(picks[:]))
@@ -132,22 +122,16 @@ def tile_list_fraud_residual_queue_kernel(
                 out=v_plane_tile[QUADRANT * q : QUADRANT * q + 4, :].bitcast(I32),
                 in_=picked_planes[first : first + 4 * PASSES, :].bitcast(I32),
             )
-        w1_raw[2, 0] = load_weight(placed("w1_last0", W1_LAST_AT[0], weight_shape, F32), w1, 2, 0)
+        w1_raw[2, 0] = load_weight(3, "w1_20", w1, 2, 0)
         w4_raw.append(load_w4(1, [slice(0, PASSES)]))
         dec_sb = load(keep([P, BLOCKS, PACK], F32, "dec_sb"), dec.rearrange("(b p i) -> p b i", b=BLOCKS, i=PACK))
         places = held.tile([P, S // 16], U16, name="places")
         nc.sync.dma_start(places[:], offs2)
         wgs_sb = load(keep([P, S], F32, "wgs_sb"), wgs)
-        w1_raw[0, 1] = load_weight(slot(6, weight_shape, F32), w1, 0, 1)
-        w1_raw[1, 1] = load_weight(placed("w1_mid", W1_MID_AT, weight_shape, F32), w1, 1, 1)
-        w1_raw[2, 1] = load_weight(placed("w1_last1", W1_LAST_AT[1], weight_shape, F32), w1, 2, 1)
-        queue_sb = {(0, 0): load_queue(7, 0, 0)}
-        wf_raw = [load_weight(slot(5, weight_shape, F32), wf, 0, 0)]
-        queue_sb[0, 1] = load_queue(0, 0, 1)
-        wf_raw.append(load_weight(placed("wf_last", WF_LAST_AT, weight_shape, F32), wf, 1, 0))
-        queue_sb[1, 0] = load_queue(1, 1, 0)
-        queue_sb[1, 1] = load_queue(6, 1, 1)
-        bias_sb = load(keep([P, PACK, 1], F32, "bias_sb"), bf.rearrange("(c p o) -> p c o", p=P, o=1))
+        w1_raw[0, 1] = load_weight(6, "w1_01", w1, 0, 1)
+        w1_raw[1, 1] = load_weight(7, "w1_11", w1, 1, 1)
+        queue_sb = [load_queue(14, 0)]
+        w1_raw[2, 1] = load_weight(8, "w1_21", w1, 2, 1)
 
         v_words = {}
 
@@ -178,238 +162,266 @@ def tile_list_fraud_residual_queue_kernel(
         def staging(name, width=PACK * KP):
             return keep([P, width], BF16, name)
 
-        w1_q = {
-            (0, 0): (placed("w1_first_codes", PLANES_AT + ROW, [P, KP], U32), keep([P, KP], U8, "w1_first_plane")),
-            (1, 0): operand("w1_1_0"),
-            (2, 0): operand("w1_2_0"),
-            (2, 1): operand("w1_2_1"),
-        }
-        wf_q = [operand("wf_0")]
-        z_first = operand("z_first", T2)
+        w1_q = {(a, 0): operand("w1_%d0" % a) for a in range(1, PASSES)}
         z_last = [operand("z_last%d" % q, QUARTER) for q in range(QUARTERS)]
+        w4_codes = {}
 
-        gather(0, keep([P, S], U32, "v_words0"))
-        w4_codes = [keep([P, PASSES * 2 * KP], U8, "w4_codes%d" % b) for b in range(BLOCKS)]
-
-        def order_words(b):
+        def order_words(b, tile):
+            w4_codes[b] = tile
             nc.vector.tensor_copy(
                 w4_codes[b][:].bitcast(U16).rearrange("p (a t m) -> p t a m", t=PACK, m=P),
                 w4_raw[b][:].bitcast(U16).rearrange("p a (m t) -> p t a m", t=PACK),
             )
 
-        order_words(0)
+        gather(0, keep([P, S], U32, "tab_planes"))
+        order_words(0, keep([P, PASSES * 2 * KP], U8, "w4_codes0"))
         w4_planes = keep([P, PASSES * H], U8, "w4_raw0")
         nc.vector.tensor_copy(
             w4_planes[:].rearrange("p (g t m) -> p g t m", t=PACK, m=P),
             w4_planes_raw[:].rearrange("p (g m t) -> p g t m", t=PACK, m=P),
         )
+        gather(1, keep([P, S], U32, "w4_planes_raw"))
+        w1_q[0, 0] = (slot(2, "w1_00_codes", [P, KP], U32), keep([P, KP], U8, "w1_00_plane"))
+        quantise(w1_q[0, 0], 0, cast(nc.scalar.copy, w1_raw[0, 0], 0, PACK, staging("stage0"))[:])
+        gather(2, keep([P, S], U32, "stage0"))
 
-        gather(1, placed("v_words1", PLANES_AT, [P, S], U32))
-        quantise(w1_q[0, 0], 0, cast(nc.scalar.copy, w1_raw[0, 0], 0, PACK, staging("head_stage"))[:])
-        gather(2, slot(2, [P, S], U32))
+        def quantise_half(a, half, copy, tile):
+            quantise(w1_q[a, 0], 2 * half * P, cast(copy, w1_raw[a, 0], 2 * half, 2 * half + 2, tile)[:])
 
-        def quantise_first_half(a):
-            quantise(w1_q[a, 0], 0, cast(nc.vector.tensor_copy, w1_raw[a, 0], 0, 2, slot(3, [P, 2 * KP], BF16))[:])
+        quantise_half(1, 0, nc.vector.tensor_copy, slot(5, "stage_10", [P, 2 * KP], BF16))
+        quantise_half(1, 1, nc.scalar.copy, staging("stage1", 2 * KP))
 
-        def quantise_second_half(a):
-            quantise(w1_q[a, 0], 2 * P, cast(nc.scalar.copy, w1_raw[a, 0], 2, PACK, staging("head_stage", 2 * KP))[:])
-
-        quantise_first_half(1)
-        quantise_second_half(1)
-
-        def pass_order(k):
-            return (2, 0, 1) if 0 < k < PACK else (0, 1, 2)
-
-        def encode(k):
+        def encode_pass(k, a, acc):
             b, i = divmod(k, PACK)
-            acc = bank(ENCODE_BANK[k])
-            order = pass_order(k)
-            for a in order:
-                word0 = a * KP + i * P
-                byte0 = a * H + b * KP + i * P
-                nc.tensor.matmul_mx(
-                    out=acc[:],
-                    lhsT=w4_codes[b][:, 2 * word0 : 2 * (word0 + P)].bitcast(FP4X4),
-                    lhsT_scale=w4_planes[:, byte0 : byte0 + P],
-                    rhs=v_words[a][:].bitcast(FP8X4),
-                    rhs_scale=v_planes[a],
-                    start=(a == order[0]),
-                    stop=(a == order[-1]),
-                )
-            if k == 0:
-                result = ring.tile([P, S], F32, name="minus_enc")
-            else:
-                result = placed("minus_enc%d" % k, TANH_AT[k - 1], [P, S], F32)
-            nc.scalar.activation(result[:], acc[:], ACT.Tanh, scale=-1.0)
-            return result
+            word0 = a * KP + i * P
+            byte0 = a * H + b * KP + i * P
+            nc.tensor.matmul_mx(
+                out=acc[:],
+                lhsT=w4_codes[b][:, 2 * word0 : 2 * (word0 + P)].bitcast(FP4X4),
+                lhsT_scale=w4_planes[:, byte0 : byte0 + P],
+                rhs=v_words[a][:].bitcast(FP8X4),
+                rhs_scale=v_planes[a],
+                start=(a == 0),
+                stop=(a == PASSES - 1),
+            )
 
-        def linear(*tiles):
-            order = pass_order(3) if tiles == (3,) else range(PASSES)
-            for k in tiles:
-                lin[k] = bank(LINEAR_BANK[k])
-            for a, k in [(a, k) for a in order for k in tiles]:
-                b, i = divmod(k, PACK)
-                acc = lin[k]
-                codes, plane = w1_q[a, b]
-                nc.tensor.matmul_mx(
-                    out=acc[:],
-                    lhsT=codes[:, i * P : (i + 1) * P].bitcast(FP8X4),
-                    lhsT_scale=plane[:, i * P : (i + 1) * P],
-                    rhs=v_words[a][:].bitcast(FP8X4),
-                    rhs_scale=v_planes[a],
-                    start=(a == order[0]),
-                    stop=(a == order[-1]),
-                )
-
-        def residual(k, tile):
+        def linear_pass(k, a, acc):
             b, i = divmod(k, PACK)
-            nc.vector.scalar_tensor_tensor(tile[:], minus_enc[k][:], dec_sb[:, b, i : i + 1], lin[k][:], ALU.mult, ALU.add)
-            return tile
+            codes, plane = w1_q[a, b]
+            nc.tensor.matmul_mx(
+                out=acc[:],
+                lhsT=codes[:, i * P : (i + 1) * P].bitcast(FP8X4),
+                lhsT_scale=plane[:, i * P : (i + 1) * P],
+                rhs=v_words[a][:].bitcast(FP8X4),
+                rhs_scale=v_planes[a],
+                start=(a == 0),
+                stop=(a == PASSES - 1),
+            )
 
-        def h_tile():
-            return ring.tile([P, S], F32, name="h", bufs=3)
+        minus_enc = {}
 
-        def scatter(page, values):
-            nc.vector.tensor_tensor(page[:].indirect(places[:]), values[:], wgs_sb[:], ALU.mult)
+        def saturate(k, acc):
+            minus_enc[k] = slot(TANH_AT[k][0], "minus_enc%d" % k, [P, S], F32, TANH_AT[k][1])
+            nc.scalar.activation(minus_enc[k][:], acc[:], ACT.Tanh, scale=-1.0)
 
-        def add_turned(acc, column, source, start, stop):
+        h = {}
+
+        def residual(k):
+            b, i = divmod(k, PACK)
+            h[k] = slot(H_AT[k][0], "h%d" % k, [P, S], F32, H_AT[k][1])
+            nc.vector.scalar_tensor_tensor(h[k][:], minus_enc[k][:], dec_sb[:, b, i : i + 1], lin[k][:], ALU.mult, ALU.add)
+
+        page_of = {}
+
+        def scatter(k, page):
+            page_of[k] = page
+            nc.vector.tensor_tensor(page[:].indirect(places[:]), h[k][:], wgs_sb[:], ALU.mult)
+
+        def add_turned(acc, column, source, piece, start, stop):
             nc.tensor.matmul(
-                acc[:, column * P : (column + 1) * P], lhsT=source, rhs=identity[:], is_transpose=True, start=start, stop=stop
+                acc[:, column * P : (column + 1) * P],
+                lhsT=source[:, piece * P : (piece + 1) * P],
+                rhs=identity[:],
+                is_transpose=True,
+                start=start,
+                stop=stop,
             )
 
-        def round_in_pairs(acc, groups, tile):
+        def sum_pair(pair, accs, steps):
+            for q, acc in accs.items():
+                for step in steps:
+                    e = step % 2
+                    source = queue_sb[pair][:, e, :] if step < 2 else page_of[2 * pair + e][:]
+                    for piece in range(2):
+                        add_turned(acc, 2 * piece + e, source, 2 * q + piece, step == 0 and piece == 0, step == 3 and piece == 1)
+
+        def round_pair(acc, target):
             nc.scalar.copy(
-                tile[:, 0 : groups * 2 * P].rearrange("m (g p e) -> m g p e", g=groups, e=2),
-                acc[:, 0 : groups * 2 * P].rearrange("m (g e p) -> m g p e", g=groups, e=2),
+                target.rearrange("m (g p e) -> m g p e", g=2, e=2), acc[:].rearrange("m (g e p) -> m g p e", g=2, e=2)
             )
-            return tile
 
-        def pair_tile():
-            return ring.tile([P, BANK], BF16, name="pair", bufs=QUARTERS, align_bytes=64)
+        def word_tiles(pair, number, at):
+            halves = [slot(number, "words%d_%d" % (pair, half), [P, 2 * BANK], BF16, at + half * ROW) for half in range(2)]
+            return halves, [halves[q // 2][:, q % 2 * BANK : (q % 2 + 1) * BANK] for q in range(QUARTERS)]
 
-        def pair_banks(u):
-            return [bank(number) for number in PAIR_BANKS[u]]
+        def turn_words(acc, u, words):
+            for piece in range(2):
+                column = 2 * u + piece
+                nc.tensor.transpose(
+                    acc[:, column * P : (column + 1) * P], words.bitcast(F32)[:, piece * P : (piece + 1) * P], identity[:]
+                )
 
-        def sum_pair(u, accs, phases):
-            sources = [(e, queue_sb[0, u][:, e, :]) for e in range(2)] + [(e, pages[2 * u + e][:]) for e in range(2)]
-            for steps in phases:
-                for q in BACK_ORDER:
-                    for step in steps:
-                        e, source = sources[step]
-                        for piece in range(2):
-                            cols = slice((2 * q + piece) * P, (2 * q + piece + 1) * P)
-                            first, last = step == 0 and piece == 0, step == 3 and piece == 1
-                            add_turned(accs[q], 2 * piece + e, source[:, cols], first, last)
-            return accs
-
-        def turn_back(q, pairs, z):
-            acc = bank(PAIR_BANKS[1][q])
-            for u in range(2):
-                words = pairs[u][q][:].bitcast(F32)
-                for piece in range(2):
-                    column = 2 * u + piece
-                    nc.tensor.transpose(acc[:, column * P : (column + 1) * P], words[:, piece * P : (piece + 1) * P], identity[:])
-            target = z[q // 2][:, q % 2 * PACK * QUARTER : (q % 2 + 1) * PACK * QUARTER]
+        def weave(acc, target):
             nc.scalar.copy(target.bitcast(F32).rearrange("p (m u) -> p m u", u=2), acc[:].rearrange("p (u m) -> p m u", u=2))
 
-        def sum_row(i, page):
-            sum_banks, back_banks = ROW_BANKS[i]
-            words = []
-            groups = QUARTERS // len(sum_banks)
-            accs = [bank(number) for number in sum_banks]
-            for step, source in enumerate((queue_sb[1, i // 2][:, i % 2, :], page[:])):
-                for piece in range(2 * QUARTERS):
-                    part, column = divmod(piece, 2 * groups)
-                    first, last = step == 0 and column == 0, step == 1 and column == 2 * groups - 1
-                    add_turned(accs[part], column, source[:, piece * P : (piece + 1) * P], first, last)
-            for acc in accs:
-                tile = round_in_pairs(acc, groups, pair_tile())
-                words.extend(tile[:].bitcast(F32)[:, g * P : (g + 1) * P] for g in range(groups))
-            groups = QUARTERS // len(back_banks)
-            for part, number in enumerate(back_banks):
-                acc = bank(number)
-                for g in range(groups):
-                    nc.tensor.transpose(acc[:, g * P : (g + 1) * P], words[groups * part + g], identity[:])
-                for g in range(groups):
-                    nc.scalar.copy(
-                        rows[groups * part + g][:, i, :].rearrange("p (e m) -> p e m", e=2),
-                        acc[:, g * P : (g + 1) * P].bitcast(BF16).rearrange("p (m e) -> p e m", e=2),
-                    )
+        enc = {k: bank(ENCODE_BANK[k]) for k in range(PACK)}
+        lin = {k: bank(LINEAR_BANK[k]) for k in range(PACK)}
+        for a in range(PASSES - 1):
+            for k in range(PACK):
+                encode_pass(k, a, enc[k])
+            for k in range(PACK):
+                linear_pass(k, a, lin[k])
+        for k in range(PACK):
+            encode_pass(k, PASSES - 1, enc[k])
+        saturate(0, enc[0])
+        saturate(1, enc[1])
+        quantise_half(2, 0, nc.vector.tensor_copy, staging("stage1", 2 * KP))
+        for k in range(2):
+            linear_pass(k, PASSES - 1, lin[k])
+        order_words(1, keep([P, PASSES * 2 * KP], U8, "w4_codes1"))
+        residual(0)
+        quantise_half(2, 1, nc.scalar.copy, staging("stage2", 2 * KP))
+        for k in range(2, PACK):
+            linear_pass(k, PASSES - 1, lin[k])
+        saturate(2, enc[2])
+        saturate(3, enc[3])
+        queue_sb.append(load_queue(2, 1))
+        wf_raw = [load_weight(1, "wf_0", wf, 0, 0)]
+        wf_raw.append(load_weight(15, "wf_1", wf, 1, 0))
+        queue_sb.append(load_queue(16, 2))
+        queue_sb.append(load_queue(0, 3))
+        bias_sb = load(keep([P, PACK, 1], F32, "bias_sb"), bf.rearrange("(c p o) -> p c o", p=P, o=1))
+        residual(1)
+        scatter(0, pages[0])
+        residual(2)
+        residual(3)
+        scatter(1, pages[1])
+        scatter(2, pages[2])
 
-        minus_enc = {0: encode(0)}
-        quantise_first_half(2)
-        lin = {}
-        linear(0)
-        linear(1)
-        order_words(1)
-        h = {0: residual(0, h_tile())}
-        quantise_second_half(2)
-        for k in range(1, PACK):
-            minus_enc[k] = encode(k)
-        linear(2)
-        linear(3)
-        h[1] = residual(1, h_tile())
-        scatter(pages[0], h[0])
-        h[2] = residual(2, h_tile())
-        scatter(pages[1], h[1])
-        scatter(pages[2], h[2])
+        for a, number in enumerate((4, 6, 7)):
+            plane = slot(H_AT[1][0], "w1_%d1_plane" % a, [P, KP], U8, H_AT[1][1] + a * KP)
+            w1_q[a, 1] = (keep([P, KP], U32, "w1_%d1_codes" % a), plane)
+            staged = slot(number, "stage_%d1" % a, [P, PACK * KP], BF16)
+            quantise(w1_q[a, 1], 0, cast(nc.scalar.copy, w1_raw[a, 1], 0, PACK, staged)[:])
+        late_page = slot(8, "page3", [P, T2], F32)
+        nc.gpsimd.memset(late_page[:], 0.0)
+        scatter(3, late_page)
 
-        staged = []
-        for a in range(2):
-            tile = placed("w1_stage%d" % a, STAGE_AT + 2 * ROW * a, [P, PACK * KP], BF16)
-            staged.append(cast(nc.scalar.copy, w1_raw[a, 1], 0, PACK, tile))
-        minus_enc[4] = encode(4)
-        minus_enc[5] = encode(5)
-        staged.append(cast(nc.scalar.copy, w1_raw[2, 1], 0, PACK, staging("late_stage")))
-        for a in range(2):
-            codes = placed("w1_codes%d" % a, W1_LAST_AT[1] + (2 + a) * ROW, [P, KP], U32)
-            w1_q[a, 1] = (codes, keep([P, KP], U8, "w1_plane%d" % a))
-            quantise(w1_q[a, 1], 0, staged[a][:])
-        h[3] = residual(3, placed("h3", STAGE_AT, [P, S], F32))
-        quantise(w1_q[2, 1], 0, staged[2][:])
-        scatter(pages[3], h[3])
-        first = sum_pair(0, pair_banks(0), [(0, 1, 2), (3,)])
-        pairs = [{q: round_in_pairs(first[q], 2, pair_tile()) for q in BACK_ORDER}]
+        def encode(k):
+            enc[k] = bank(ENCODE_BANK[k])
+            for a in range(PASSES):
+                encode_pass(k, a, enc[k])
+            saturate(k, enc[k])
+
+        encode(4)
+        encode(5)
+
+        def linear(*tiles):
+            for k in tiles:
+                lin[k] = bank(LINEAR_BANK[k])
+            for a in range(PASSES):
+                for k in tiles:
+                    linear_pass(k, a, lin[k])
+
+        def pair_banks(pair):
+            return {q: bank(number) for q, number in enumerate(PAIR_BANKS[pair])}
+
+        halves0, words0 = word_tiles(0, 8, 2 * ROW)
+        accs = pair_banks(0)
+        for steps in ((0, 1), (2,), (3,)):
+            sum_pair(0, accs, steps)
+        for q in range(QUARTERS):
+            round_pair(accs[q], words0[q])
         linear(4, 5)
-        second = sum_pair(1, pair_banks(1), [(0, 1, 2)])
-
-        h[4] = residual(4, h_tile())
-        h[5] = residual(5, h_tile())
-        quantise(wf_q[0], 0, cast_straight(wf_raw[0], staging("head_stage"))[:])
-        wf_last = cast_straight(wf_raw[1], staging("late_stage"))
-        sum_pair(1, second, [(3,)])
-        pairs.append({})
-        for q in BACK_ORDER:
-            pairs[1][q] = round_in_pairs(second[q], 2, placed("pair%d" % q, WF_LAST_AT + 2 * BANK * q, [P, BANK], BF16))
-        minus_enc[6] = encode(6)
-        minus_enc[7] = encode(7)
+        accs = pair_banks(1)
+        accs = {q: accs[q] for q in ORDER}
+        sum_pair(1, accs, (0, 1))
+        sum_pair(1, accs, (2,))
         linear(6, 7)
-        scatter(pages[0], h[4])
-        scatter(pages[1], h[5])
-        z_halves = [placed("z_half%d" % u, STAGE_AT + 2 * ROW * u, [P, 2 * PACK * QUARTER], BF16) for u in range(2)]
-        for q in BACK_ORDER:
-            turn_back(q, pairs, z_halves)
-        for u in (1, 0):
-            quantise(z_first, u * 2 * QUARTER, z_halves[u][:])
-        for k in (6, 7):
-            h[k] = residual(k, placed("h%d" % k, STAGE_AT + ROW * (k - 4), [P, S], F32))
-        shared = keep([P, 16, QUARTER], BF16, "z_rows")
-        rows = [shared[:, 12:16, :], keep([P, PACK, QUARTER], BF16, "z_rows1")[:], shared[:, 2:16:4, :], shared[:, 3:16:4, :]]
-        sum_row(0, pages[0])
-        sum_row(1, pages[1])
-        scatter(pages[2], h[6])
-        sum_row(2, pages[2])
-        last_page = pages[3]
-        scatter(last_page, h[7])
-        wf_q.append((placed("wf_1_codes", STAGE_AT + 2 * ROW, [P, KP], U32), keep([P, KP], U8, "wf_1_plane")))
+        residual(4)
+        residual(5)
+        wf_first = cast_straight(wf_raw[0], slot(14, "stage_wf0", [P, PACK * KP], BF16))
+        wf_last = cast_straight(wf_raw[1], slot(1, "stage_wf1", [P, PACK * KP], BF16))
+        sum_pair(1, accs, (3,))
+        halves1, words1 = word_tiles(1, 13, 0)
+        for q in ORDER:
+            round_pair(accs[q], words1[q])
+        scatter(4, pages[0])
+        scatter(5, pages[1])
+        wf_q = [(keep([P, KP], U32, "wf_0_codes"), slot(H_AT[4][0], "wf_0_plane", [P, KP], U8, H_AT[4][1]))]
+        quantise(wf_q[0], 0, wf_first[:])
+        z_halves = [slot(12, "z_half%d" % u, [P, PACK * KP], BF16, u * 2 * ROW) for u in range(2)]
+        for n, q in enumerate(ORDER):
+            acc = bank(BACK_BANKS[0][q])
+            turn_words(acc, 0, words0[q])
+            turn_words(acc, 1, words1[q])
+            weave(acc, z_halves[n // 2][:, n % 2 * PACK * QUARTER : (n % 2 + 1) * PACK * QUARTER])
+        encode(6)
+        encode(7)
+        z_first = [operand("z_first%d" % u, 2 * QUARTER) for u in range(2)]
+        for u in range(2):
+            quantise(z_first[u], 0, z_halves[u][:])
+        residual(6)
+        residual(7)
+        scatter(6, pages[2])
+        scatter(7, late_page)
+        wf_q.append((keep([P, KP], U32, "wf_1_codes"), slot(H_AT[6][0], "wf_1_plane", [P, KP], U8, H_AT[6][1])))
         quantise(wf_q[1], 0, wf_last[:])
 
-        def score(b, q):
+        halves2, words2 = word_tiles(2, 13, 2 * ROW)
+        accs = pair_banks(2)
+        for steps in ((0, 1), (2,), (3,)):
+            sum_pair(2, accs, steps)
+        for q in range(QUARTERS):
+            round_pair(accs[q], words2[q])
+
+        def sum_lone(acc, k, pieces, step):
+            source = queue_sb[3][:, k % 2, :] if step == 0 else page_of[k][:]
+            for n, piece in enumerate(pieces):
+                add_turned(acc, n, source, piece, step == 0 and n == 0, step == 1 and n == len(pieces) - 1)
+
+        def round_lone(acc, k, pieces):
+            half, first = divmod(pieces[0], PACK)
+            nc.scalar.copy(
+                halves1[half][:].rearrange("m (g p e) -> m g p e", g=PACK, e=2)[:, first : first + len(pieces), :, k % 2],
+                acc[:, 0 : len(pieces) * P].rearrange("m (g p) -> m g p", p=P),
+            )
+
+        backs = [bank(number) for number in BACK_BANKS[1]]
+        for q in range(QUARTERS):
+            turn_words(backs[q], 0, words2[q])
+        woven = [staging("woven%d" % q, PACK * QUARTER) for q in range(QUARTERS)]
+        lone = [bank(number) for number in LONE_BANKS]
+        for step in range(2):
+            for half in range(2):
+                sum_lone(lone[half], 6, range(PACK * half, PACK * half + PACK), step)
+        for half in range(2):
+            round_lone(lone[half], 6, range(PACK * half, PACK * half + PACK))
+        for q in range(QUARTERS):
+            turn_words(backs[q], 1, words1[q])
+            weave(backs[q], woven[q][:])
+
+        scores_in = {}
+
+        def score(b, q, half_n):
+            channels = (2 * half_n, 2 * half_n + 1)
             if b == 0:
-                codes, plane = (part[:, q * QUARTER : (q + 1) * QUARTER] for part in z_first)
+                scores_in.setdefault(q, {})[half_n] = bank(SCORE_BANKS[q][half_n])
+                half, n = divmod(ORDER.index(q), 2)
+                codes, plane = (part[:, n * QUARTER : (n + 1) * QUARTER] for part in z_first[half])
             else:
                 codes, plane = (part[:] for part in z_last[q])
-            for c in range(PACK):
+            for c in channels:
                 nc.tensor.matmul_mx(
                     out=scores_in[q][c // 2][:, (c % 2) * QUARTER : (c % 2 + 1) * QUARTER],
                     lhsT=wf_q[b][0][:, c * P : (c + 1) * P].bitcast(FP8X4),
@@ -420,29 +432,24 @@ def tile_list_fraud_residual_queue_kernel(
                     stop=(b == BLOCKS - 1 and c % 2 == 1),
                 )
 
-        scores_in = [[bank(number) for number in numbers] for numbers in SCORE_BANKS]
         for q in range(QUARTERS):
-            score(0, q)
-
+            for half in range(2):
+                score(0, q, half)
         for q in range(QUARTERS):
             cols = slice(q * QUARTER, (q + 1) * QUARTER)
-            nc.vector.tensor_tensor(rows[q][:, PACK - 1, :], last_page[:, cols], queue_sb[1, 1][:, 1, cols], ALU.add)
-            woven = ring.tile([P, PACK * QUARTER], BF16, name="woven", bufs=QUARTERS, align_bytes=64)
-            target = woven[:].rearrange("p (c e i) -> p c i e", e=4, i=PACK)
-            source = rows[q].rearrange("p i (c e) -> p c i e", e=4)
-            own = QUARTER // 8 if q == 1 else QUARTER // 4
-            nc.vector.tensor_copy(target[:, 0:own], source[:, 0:own])
-            if q == 1:
-                nc.scalar.copy(target[:, own:], source[:, own:])
-            quantise(z_last[q], 0, woven[:])
-            score(1, q)
+            nc.vector.tensor_tensor(
+                woven[q][:].rearrange("p (m i) -> p m i", i=PACK)[:, :, PACK - 1], page_of[7][:, cols], queue_sb[3][:, 1, cols], ALU.add
+            )
+            quantise(z_last[q], 0, woven[q][:])
+            for half in range(2):
+                score(1, q, half)
 
         out_rows = out.rearrange("(c p) m -> p c m", p=P)
-        for q in range(QUARTERS):
+        for q in ORDER:
             for half in range(2):
                 acc = scores_in[q][half]
                 channels = slice(2 * half, 2 * half + 2)
-                scores = ring.tile([P, 2, QUARTER], F32, name="scores", bufs=2 * QUARTERS, align_bytes=64)
+                scores = slot(2 + q // 2, "scores%d%d" % (q, half), [P, 2, QUARTER], F32, (q % 2 * 2 + half) * ROW)
                 if q >= 2 and half == 1:
                     nc.vector.tensor_tensor(
                         scores[:],

from contextlib import ExitStack

import concourse.mybir as mybir
from concourse.masks import make_identity

K, T, S, H, N, T2 = 1536, 2048, 512, 1024, 512, 1024
FLOPS = 2 * (2 * K * H * S + H * N * T2)

F32 = mybir.dt.float32
BF16 = mybir.dt.bfloat16
I32 = mybir.dt.int32
U32 = mybir.dt.uint32
U16 = mybir.dt.uint16
U8 = mybir.dt.uint8
FP8X4 = mybir.dt.float8_e4m3fn_x4
FP4X4 = mybir.dt.float4_e2m1fn_x4
ACT = mybir.ActivationFunctionType
ALU = mybir.AluOpType

P = 128
PACK = 4
KP = P * PACK
PASSES = K // KP
BLOCKS = H // KP
BANK = 512
QUADRANT = 32
QUADRANTS = P // QUADRANT
QUARTERS = 4
QUARTER = T2 // QUARTERS
ROWS_FROM = P - 16 * PASSES
SLOT = 4 * PACK * KP

ROW = 4 * S

ENCODE_BANK = (0, 1, 2, 3, 0, 1, 4, 5)
LINEAR_BANK = (4, 5, 6, 7, 4, 5, 6, 7)
PAIR_BANKS = ((4, 5, 6, 7), (0, 1, 2, 3), (0, 1, 2, 3))
BACK_BANKS = ((0, 1, 2, 3), (0, 1, 6, 7))
LONE_BANKS = (2, 3)
ORDER = (0, 1, 2, 3)
SCORE_BANKS = ((4, 5), (2, 0), (3, 1), (6, 7))
TANH_AT = ((4, 0), (4, ROW), (3, 0), (3, ROW), (9, 2 * ROW), (9, 3 * ROW), (8, 2 * ROW), (8, 3 * ROW))
H_AT = ((10, 2 * ROW), (10, 3 * ROW), (11, 0), (11, ROW), (11, 2 * ROW), (11, 3 * ROW), (10, 0), (10, ROW))


def tile_list_fraud_residual_queue_kernel(
    tc, tab_words, tab_scales, offs, w4_words, w4_scales, w1, dec, wgs, offs2, queue, wf, bf, out
):
    nc = tc.nc
    with ExitStack() as ctx:
        held = ctx.enter_context(tc.tile_pool(name="held", bufs=1))
        over = ctx.enter_context(tc.tile_pool(name="over", bufs=1))
        psum = ctx.enter_context(tc.psum_pool(name="psum", bufs=1))

        def keep(shape, dtype, name):
            return held.tile(shape, dtype, name=name, align_bytes=64)

        def slot(number, name, shape, dtype, at=0):
            return over.tile(shape, dtype, name=name, offset=number * SLOT + at, align_bytes=64)

        def bank(number):
            return psum.tile([P, BANK], F32, name="bank%d" % number)

        def load(tile, source):
            nc.sync.dma_start(out=tile[:], in_=source)
            return tile

        def load_table(number, a):
            return load(slot(number, "table%d" % a, [P, T], I32), tab_words[a].rearrange("p t i -> p (t i)").bitcast(I32))

        def load_weight(number, name, w, a, b):
            rows = w[a * KP : (a + 1) * KP, b * KP : (b + 1) * KP]
            return load(slot(number, name, [P, PACK, KP], F32), rows.rearrange("(p j) c -> p j c", j=PACK))

        def load_w4(b, parts):
            tile = keep([P, PASSES, 2 * KP], U8, "w4_raw%d" % b)
            words = w4_words[:, :, b * 2 * KP : (b + 1) * 2 * KP].rearrange("a p n -> p a n")
            for passes in parts:
                nc.sync.dma_start(out=tile[:, passes, :].bitcast(I32), in_=words[:, passes, :].bitcast(I32))
            return tile

        def load_queue(number, pair):
            b, u = divmod(pair, 2)
            rows = queue[b * KP : (b + 1) * KP, :].rearrange("(p i) m -> p i m", i=PACK)
            return load(slot(number, "queue%d" % pair, [P, 2, T2], F32), rows[:, 2 * u : 2 * u + 2, :])

        w4_planes_raw = keep([P, PASSES * H], U8, "w4_planes_raw")
        nc.gpsimd.memset(w4_planes_raw[:].bitcast(I32), 0)
        for q in range(QUADRANTS):
            nc.gpsimd.dma_start(
                out=w4_planes_raw[QUADRANT * q : QUADRANT * q + 4, :].bitcast(I32).rearrange("r (a c) -> r a c", a=PASSES),
                in_=w4_scales[:, 4 * q : 4 * q + 4, :].bitcast(I32).rearrange("a r c -> r a c"),
            )
        tab_planes = keep([P, T], U8, "tab_planes")
        nc.vector.memset(tab_planes[0:ROWS_FROM, :].bitcast(I32), 0)
        v_plane_tile = keep([P, PASSES * S], U8, "v_planes")
        nc.vector.memset(v_plane_tile[:].bitcast(I32), 0)
        v_planes = [v_plane_tile[:, a * S : (a + 1) * S] for a in range(PASSES)]
        pages = [keep([P, T2], F32, "page%d" % i) for i in range(PACK - 1)]
        for page in pages[:2]:
            nc.vector.memset(page[:], 0.0)
        identity = keep([P, P], F32, "identity")
        make_identity(nc, identity[:])
        nc.gpsimd.memset(pages[2][:], 0.0)

        picks = held.tile([P, S // 16], U16, name="picks")
        nc.sync.dma_start(picks[:], offs)
        for a in range(PASSES):
            nc.sync.dma_start(out=tab_planes[ROWS_FROM + a : P : PASSES, :].bitcast(I32), in_=tab_scales[a].bitcast(I32))
        table = [load_table(0, 0)]
        w4_raw = [load_w4(0, range(PASSES))]
        w1_raw = {(0, 0): load_weight(1, "w1_00", w1, 0, 0)}
        table.append(load_table(2, 1))
        table.append(load_table(5, 2))
        w1_raw[1, 0] = load_weight(4, "w1_10", w1, 1, 0)

        picked_planes = keep([P, S], U8, "picked_planes")
        nc.vector.tensor_copy(picked_planes[:], tab_planes[:].indirect(picks[:]))
        for q in range(QUADRANTS):
            first = ROWS_FROM + 4 * PASSES * q
            nc.scalar.dma_start(
                out=v_plane_tile[QUADRANT * q : QUADRANT * q + 4, :].bitcast(I32),
                in_=picked_planes[first : first + 4 * PASSES, :].bitcast(I32),
            )
        w1_raw[2, 0] = load_weight(3, "w1_20", w1, 2, 0)
        w4_raw.append(load_w4(1, [slice(0, PASSES)]))
        dec_sb = load(keep([P, BLOCKS, PACK], F32, "dec_sb"), dec.rearrange("(b p i) -> p b i", b=BLOCKS, i=PACK))
        places = held.tile([P, S // 16], U16, name="places")
        nc.sync.dma_start(places[:], offs2)
        wgs_sb = load(keep([P, S], F32, "wgs_sb"), wgs)
        w1_raw[0, 1] = load_weight(6, "w1_01", w1, 0, 1)
        w1_raw[1, 1] = load_weight(7, "w1_11", w1, 1, 1)
        queue_sb = [load_queue(14, 0)]
        w1_raw[2, 1] = load_weight(8, "w1_21", w1, 2, 1)

        v_words = {}

        def gather(a, tile):
            v_words[a] = tile
            nc.vector.tensor_copy(tile[:], table[a][:].bitcast(U32).indirect(picks[:]))

        def operand(name, width=KP):
            return keep([P, width], U32, name + "_codes"), keep([P, width], U8, name + "_plane")

        def cast(copy, raw, t0, t1, tile):
            src = raw[:].rearrange("p j (m t) -> p m j t", t=PACK)
            dst = tile[:].rearrange("p (t m j) -> p m j t", m=P, j=PACK)
            for t in range(t0, t1, 2):
                copy(dst[:, :, :, t - t0 : t - t0 + 2], src[:, :, :, t : t + 2])
            return tile

        def cast_straight(raw, tile):
            nc.scalar.copy(
                tile[:].rearrange("p (c e j) -> p c j e", e=4, j=PACK), raw[:].rearrange("p j (c e) -> p c j e", e=4)
            )
            return tile

        def quantise(target, c0, values):
            c1 = c0 + values.shape[1] // PACK
            nc.vector.quantize_mx(out=target[0][:, c0:c1].bitcast(FP8X4), scales=target[1][:, c0:c1], in_=values)

        def staging(name, width=PACK * KP):
            return keep([P, width], BF16, name)

        w1_q = {(a, 0): operand("w1_%d0" % a) for a in range(1, PASSES)}
        z_last = [operand("z_last%d" % q, QUARTER) for q in range(QUARTERS)]
        w4_codes = {}

        def order_words(b, tile):
            w4_codes[b] = tile
            nc.vector.tensor_copy(
                w4_codes[b][:].bitcast(U16).rearrange("p (a t m) -> p t a m", t=PACK, m=P),
                w4_raw[b][:].bitcast(U16).rearrange("p a (m t) -> p t a m", t=PACK),
            )

        gather(0, keep([P, S], U32, "tab_planes"))
        order_words(0, keep([P, PASSES * 2 * KP], U8, "w4_codes0"))
        w4_planes = keep([P, PASSES * H], U8, "w4_raw0")
        nc.vector.tensor_copy(
            w4_planes[:].rearrange("p (g t m) -> p g t m", t=PACK, m=P),
            w4_planes_raw[:].rearrange("p (g m t) -> p g t m", t=PACK, m=P),
        )
        gather(1, keep([P, S], U32, "w4_planes_raw"))
        w1_q[0, 0] = (slot(2, "w1_00_codes", [P, KP], U32), keep([P, KP], U8, "w1_00_plane"))
        quantise(w1_q[0, 0], 0, cast(nc.scalar.copy, w1_raw[0, 0], 0, PACK, staging("stage0"))[:])
        gather(2, keep([P, S], U32, "stage0"))

        def quantise_half(a, half, copy, tile):
            quantise(w1_q[a, 0], 2 * half * P, cast(copy, w1_raw[a, 0], 2 * half, 2 * half + 2, tile)[:])

        quantise_half(1, 0, nc.vector.tensor_copy, slot(5, "stage_10", [P, 2 * KP], BF16))
        quantise_half(1, 1, nc.scalar.copy, staging("stage1", 2 * KP))

        def encode_pass(k, a, acc):
            b, i = divmod(k, PACK)
            word0 = a * KP + i * P
            byte0 = a * H + b * KP + i * P
            nc.tensor.matmul_mx(
                out=acc[:],
                lhsT=w4_codes[b][:, 2 * word0 : 2 * (word0 + P)].bitcast(FP4X4),
                lhsT_scale=w4_planes[:, byte0 : byte0 + P],
                rhs=v_words[a][:].bitcast(FP8X4),
                rhs_scale=v_planes[a],
                start=(a == 0),
                stop=(a == PASSES - 1),
            )

        def linear_pass(k, a, acc):
            b, i = divmod(k, PACK)
            codes, plane = w1_q[a, b]
            nc.tensor.matmul_mx(
                out=acc[:],
                lhsT=codes[:, i * P : (i + 1) * P].bitcast(FP8X4),
                lhsT_scale=plane[:, i * P : (i + 1) * P],
                rhs=v_words[a][:].bitcast(FP8X4),
                rhs_scale=v_planes[a],
                start=(a == 0),
                stop=(a == PASSES - 1),
            )

        minus_enc = {}

        def saturate(k, acc):
            minus_enc[k] = slot(TANH_AT[k][0], "minus_enc%d" % k, [P, S], F32, TANH_AT[k][1])
            nc.scalar.activation(minus_enc[k][:], acc[:], ACT.Tanh, scale=-1.0)

        h = {}

        def residual(k):
            b, i = divmod(k, PACK)
            h[k] = slot(H_AT[k][0], "h%d" % k, [P, S], F32, H_AT[k][1])
            nc.vector.scalar_tensor_tensor(h[k][:], minus_enc[k][:], dec_sb[:, b, i : i + 1], lin[k][:], ALU.mult, ALU.add)

        page_of = {}

        def scatter(k, page):
            page_of[k] = page
            nc.vector.tensor_tensor(page[:].indirect(places[:]), h[k][:], wgs_sb[:], ALU.mult)

        def add_turned(acc, column, source, piece, start, stop):
            nc.tensor.matmul(
                acc[:, column * P : (column + 1) * P],
                lhsT=source[:, piece * P : (piece + 1) * P],
                rhs=identity[:],
                is_transpose=True,
                start=start,
                stop=stop,
            )

        def sum_pair(pair, accs, steps):
            for q, acc in accs.items():
                for step in steps:
                    e = step % 2
                    source = queue_sb[pair][:, e, :] if step < 2 else page_of[2 * pair + e][:]
                    for piece in range(2):
                        add_turned(acc, 2 * piece + e, source, 2 * q + piece, step == 0 and piece == 0, step == 3 and piece == 1)

        def round_pair(acc, target):
            nc.scalar.copy(
                target.rearrange("m (g p e) -> m g p e", g=2, e=2), acc[:].rearrange("m (g e p) -> m g p e", g=2, e=2)
            )

        def word_tiles(pair, number, at):
            halves = [slot(number, "words%d_%d" % (pair, half), [P, 2 * BANK], BF16, at + half * ROW) for half in range(2)]
            return halves, [halves[q // 2][:, q % 2 * BANK : (q % 2 + 1) * BANK] for q in range(QUARTERS)]

        def turn_words(acc, u, words):
            for piece in range(2):
                column = 2 * u + piece
                nc.tensor.transpose(
                    acc[:, column * P : (column + 1) * P], words.bitcast(F32)[:, piece * P : (piece + 1) * P], identity[:]
                )

        def weave(acc, target):
            nc.scalar.copy(target.bitcast(F32).rearrange("p (m u) -> p m u", u=2), acc[:].rearrange("p (u m) -> p m u", u=2))

        enc = {k: bank(ENCODE_BANK[k]) for k in range(PACK)}
        lin = {k: bank(LINEAR_BANK[k]) for k in range(PACK)}
        for a in range(PASSES - 1):
            for k in range(PACK):
                encode_pass(k, a, enc[k])
            for k in range(PACK):
                linear_pass(k, a, lin[k])
        for k in range(PACK):
            encode_pass(k, PASSES - 1, enc[k])
        saturate(0, enc[0])
        saturate(1, enc[1])
        quantise_half(2, 0, nc.vector.tensor_copy, staging("stage1", 2 * KP))
        for k in range(2):
            linear_pass(k, PASSES - 1, lin[k])
        order_words(1, keep([P, PASSES * 2 * KP], U8, "w4_codes1"))
        residual(0)
        quantise_half(2, 1, nc.scalar.copy, staging("stage2", 2 * KP))
        for k in range(2, PACK):
            linear_pass(k, PASSES - 1, lin[k])
        saturate(2, enc[2])
        saturate(3, enc[3])
        queue_sb.append(load_queue(2, 1))
        wf_raw = [load_weight(1, "wf_0", wf, 0, 0)]
        wf_raw.append(load_weight(15, "wf_1", wf, 1, 0))
        queue_sb.append(load_queue(16, 2))
        queue_sb.append(load_queue(0, 3))
        bias_sb = load(keep([P, PACK, 1], F32, "bias_sb"), bf.rearrange("(c p o) -> p c o", p=P, o=1))
        residual(1)
        scatter(0, pages[0])
        residual(2)
        residual(3)
        scatter(1, pages[1])
        scatter(2, pages[2])

        for a, number in enumerate((4, 6, 7)):
            plane = slot(H_AT[1][0], "w1_%d1_plane" % a, [P, KP], U8, H_AT[1][1] + a * KP)
            w1_q[a, 1] = (keep([P, KP], U32, "w1_%d1_codes" % a), plane)
            staged = slot(number, "stage_%d1" % a, [P, PACK * KP], BF16)
            quantise(w1_q[a, 1], 0, cast(nc.scalar.copy, w1_raw[a, 1], 0, PACK, staged)[:])
        late_page = slot(8, "page3", [P, T2], F32)
        nc.gpsimd.memset(late_page[:], 0.0)
        scatter(3, late_page)

        def encode(k):
            enc[k] = bank(ENCODE_BANK[k])
            for a in range(PASSES):
                encode_pass(k, a, enc[k])
            saturate(k, enc[k])

        encode(4)
        encode(5)

        def linear(*tiles):
            for k in tiles:
                lin[k] = bank(LINEAR_BANK[k])
            for a in range(PASSES):
                for k in tiles:
                    linear_pass(k, a, lin[k])

        def pair_banks(pair):
            return {q: bank(number) for q, number in enumerate(PAIR_BANKS[pair])}

        halves0, words0 = word_tiles(0, 8, 2 * ROW)
        accs = pair_banks(0)
        for steps in ((0, 1), (2,), (3,)):
            sum_pair(0, accs, steps)
        for q in range(QUARTERS):
            round_pair(accs[q], words0[q])
        linear(4, 5)
        accs = pair_banks(1)
        accs = {q: accs[q] for q in ORDER}
        sum_pair(1, accs, (0, 1))
        sum_pair(1, accs, (2,))
        linear(6, 7)
        residual(4)
        residual(5)
        wf_first = cast_straight(wf_raw[0], slot(14, "stage_wf0", [P, PACK * KP], BF16))
        wf_last = cast_straight(wf_raw[1], slot(1, "stage_wf1", [P, PACK * KP], BF16))
        sum_pair(1, accs, (3,))
        halves1, words1 = word_tiles(1, 13, 0)
        for q in ORDER:
            round_pair(accs[q], words1[q])
        scatter(4, pages[0])
        scatter(5, pages[1])
        wf_q = [(keep([P, KP], U32, "wf_0_codes"), slot(H_AT[4][0], "wf_0_plane", [P, KP], U8, H_AT[4][1]))]
        quantise(wf_q[0], 0, wf_first[:])
        z_halves = [slot(12, "z_half%d" % u, [P, PACK * KP], BF16, u * 2 * ROW) for u in range(2)]
        for n, q in enumerate(ORDER):
            acc = bank(BACK_BANKS[0][q])
            turn_words(acc, 0, words0[q])
            turn_words(acc, 1, words1[q])
            weave(acc, z_halves[n // 2][:, n % 2 * PACK * QUARTER : (n % 2 + 1) * PACK * QUARTER])
        encode(6)
        encode(7)
        z_first = [operand("z_first%d" % u, 2 * QUARTER) for u in range(2)]
        for u in range(2):
            quantise(z_first[u], 0, z_halves[u][:])
        residual(6)
        residual(7)
        scatter(6, pages[2])
        scatter(7, late_page)
        wf_q.append((keep([P, KP], U32, "wf_1_codes"), slot(H_AT[6][0], "wf_1_plane", [P, KP], U8, H_AT[6][1])))
        quantise(wf_q[1], 0, wf_last[:])

        halves2, words2 = word_tiles(2, 13, 2 * ROW)
        accs = pair_banks(2)
        for steps in ((0, 1), (2,), (3,)):
            sum_pair(2, accs, steps)
        for q in range(QUARTERS):
            round_pair(accs[q], words2[q])

        def sum_lone(acc, k, pieces, step):
            source = queue_sb[3][:, k % 2, :] if step == 0 else page_of[k][:]
            for n, piece in enumerate(pieces):
                add_turned(acc, n, source, piece, step == 0 and n == 0, step == 1 and n == len(pieces) - 1)

        def round_lone(acc, k, pieces):
            half, first = divmod(pieces[0], PACK)
            nc.scalar.copy(
                halves1[half][:].rearrange("m (g p e) -> m g p e", g=PACK, e=2)[:, first : first + len(pieces), :, k % 2],
                acc[:, 0 : len(pieces) * P].rearrange("m (g p) -> m g p", p=P),
            )

        backs = [bank(number) for number in BACK_BANKS[1]]
        for q in range(QUARTERS):
            turn_words(backs[q], 0, words2[q])
        woven = [staging("woven%d" % q, PACK * QUARTER) for q in range(QUARTERS)]
        lone = [bank(number) for number in LONE_BANKS]
        for step in range(2):
            for half in range(2):
                sum_lone(lone[half], 6, range(PACK * half, PACK * half + PACK), step)
        for half in range(2):
            round_lone(lone[half], 6, range(PACK * half, PACK * half + PACK))
        for q in range(QUARTERS):
            turn_words(backs[q], 1, words1[q])
            weave(backs[q], woven[q][:])

        scores_in = {}

        def score(b, q, half_n):
            channels = (2 * half_n, 2 * half_n + 1)
            if b == 0:
                scores_in.setdefault(q, {})[half_n] = bank(SCORE_BANKS[q][half_n])
                half, n = divmod(ORDER.index(q), 2)
                codes, plane = (part[:, n * QUARTER : (n + 1) * QUARTER] for part in z_first[half])
            else:
                codes, plane = (part[:] for part in z_last[q])
            for c in channels:
                nc.tensor.matmul_mx(
                    out=scores_in[q][c // 2][:, (c % 2) * QUARTER : (c % 2 + 1) * QUARTER],
                    lhsT=wf_q[b][0][:, c * P : (c + 1) * P].bitcast(FP8X4),
                    lhsT_scale=wf_q[b][1][:, c * P : (c + 1) * P],
                    rhs=codes.bitcast(FP8X4),
                    rhs_scale=plane,
                    start=(b == 0 and c % 2 == 0),
                    stop=(b == BLOCKS - 1 and c % 2 == 1),
                )

        for q in range(QUARTERS):
            for half in range(2):
                score(0, q, half)
        for q in range(QUARTERS):
            cols = slice(q * QUARTER, (q + 1) * QUARTER)
            nc.vector.tensor_tensor(
                woven[q][:].rearrange("p (m i) -> p m i", i=PACK)[:, :, PACK - 1], page_of[7][:, cols], queue_sb[3][:, 1, cols], ALU.add
            )
            quantise(z_last[q], 0, woven[q][:])
            for half in range(2):
                score(1, q, half)

        out_rows = out.rearrange("(c p) m -> p c m", p=P)
        for q in ORDER:
            for half in range(2):
                acc = scores_in[q][half]
                channels = slice(2 * half, 2 * half + 2)
                scores = slot(2 + q // 2, "scores%d%d" % (q, half), [P, 2, QUARTER], F32, (q % 2 * 2 + half) * ROW)
                if q >= 2 and half == 1:
                    nc.vector.tensor_tensor(
                        scores[:],
                        acc[:].rearrange("p (c m) -> p c m", c=2),
                        bias_sb[:, channels, :].to_broadcast([P, 2, QUARTER]),
                        ALU.add,
                    )
                else:
                    for e in range(2):
                        c = 2 * half + e
                        nc.scalar.activation(
                            scores[:, e, :], acc[:, e * QUARTER : (e + 1) * QUARTER], ACT.Identity, bias=bias_sb[:, c, :]
                        )
                nc.sync.dma_start(out=out_rows[:, channels, q * QUARTER : (q + 1) * QUARTER], in_=scores[:])
